import numpy as np
import ml_dtypes


def mxq(x, axis, fmt="e4m3"):
    dtype, down = {"e4m3": (ml_dtypes.float8_e4m3fn, 7), "e5m2": (ml_dtypes.float8_e5m2, 14)}[fmt]
    v = np.moveaxis(np.asarray(x, np.float32).astype(ml_dtypes.bfloat16).astype(np.float64), axis, -1)
    blocks = v.reshape(v.shape[:-1] + (-1, 32))
    amax = np.abs(blocks).max(-1, keepdims=True)
    byte = np.maximum(np.where(amax > 0, np.frexp(amax)[1] - 1 + 127, 0) - down, 1)
    scale = np.exp2(byte - 127.0)
    codes = (blocks / scale).astype(np.float32).astype(dtype).astype(np.float64)
    return np.moveaxis((codes * scale).reshape(v.shape), -1, axis)


WIDE = False


def mx_kscale(k):
    if not WIDE:
        return np.ones(k)
    levels = np.array([18, -18])
    if k % 512:
        return np.exp2(np.random.permutation(np.resize(levels, k // 32))).repeat(32)
    a = np.empty((k // 512, 16))
    for p in range(k // 512):
        a[p, :8] = np.random.permutation(np.resize(levels, 8))
        for g in range(8):
            far = levels[np.abs(levels - a[p, g]) >= 10]
            a[p, g + 8] = far[np.random.randint(len(far))]
    return np.exp2(a.ravel()).repeat(32)


def f64(x):
    return np.asarray(x).astype(np.float64)


def striped(idx):
    return np.tile(np.asarray(idx).reshape(-1, 16).T, (8, 1)).astype(np.uint16)


def unstriped(offs):
    return offs[:16].T.reshape(-1).astype(np.int64)


def setup_inputs():
    n = np.random.standard_normal
    uni = np.random.uniform
    hd = np.random.permutation(2048)[:512]
    rl = np.random.permutation(1024)[:512]
    idx = np.random.permutation(2048)[:512]
    f_i = np.ones(2048)
    f_i[idx] = mx_kscale(512)
    return {
        "hT": (np.round(n((512, 2048)) * 8) / 8).astype(np.float32),
        "rT": (np.round(n((512, 1024)) * 8) / 8).astype(np.float32),
        "G": (n((512, 512)) / np.sqrt(512) * f_i[idx][None, :]).astype(np.float32),
        "tT": (n((512, 2048)) / f_i[None, :]).astype(np.float32),
        "hoffs": striped(hd),
        "roffs": striped(rl),
        "offs": striped(idx),
    }


def reference(hT, rT, G, tT, hoffs, roffs, offs):
    hd = unstriped(hoffs)
    rl = unstriped(roffs)
    idx = unstriped(offs)
    h_ = f64(hT)[:, hd]
    r_ = f64(rT)[:, rl]
    tT_i = f64(tT)[:, idx]
    b = mxq(tT_i, 1, "e4m3") @ mxq(f64(G), 1, "e5m2").T
    dh = b * r_
    dr = b * h_
    out_0 = np.zeros((512, 2048))
    out_0[:, hd] = dh
    out_1 = np.zeros((512, 1024))
    out_1[:, rl] = dr
    return out_0, out_1

@@ -1,0 +1,155 @@
+from contextlib import ExitStack
+
+import concourse.mybir as mybir
+from concourse.masks import make_identity
+
+F32 = mybir.dt.float32
+BF16 = mybir.dt.bfloat16
+U32 = mybir.dt.uint32
+U16 = mybir.dt.uint16
+U8 = mybir.dt.uint8
+E4M3X4 = mybir.dt.float8_e4m3fn_x4
+E5M2X4 = mybir.dt.float8_e5m2_x4
+COPY = mybir.ActivationFunctionType.Copy
+MULT = mybir.AluOpType.mult
+
+P = 128
+FEATURES = 512
+QUERIES = 512
+SLOTS = 512
+ENTITIES = 2048
+RELATIONS = 1024
+BLOCKS = FEATURES // P
+QBLOCKS = QUERIES // P
+DH_TILES = 3
+DR_TILES = 2
+
+FLOPS = 2 * FEATURES * QUERIES * SLOTS
+
+
+def tile_attend_gdistm_hr_kernel(tc, hT, rT, G, tT, hoffs, roffs, offs, out_0, out_1):
+    nc = tc.nc
+    with ExitStack() as ctx:
+        lists = ctx.enter_context(tc.tile_pool(name="lists", bufs=1))
+        held = ctx.enter_context(tc.tile_pool(name="held", bufs=1))
+        psum = ctx.enter_context(tc.psum_pool(name="psum", bufs=1))
+        psum2 = ctx.enter_context(tc.psum_pool(name="psum2", bufs=2))
+
+        tail_list = lists.tile([P, SLOTS // 16], U16, name="tail_list")
+        head_list = lists.tile([P, QUERIES // 16], U16, name="head_list")
+        rel_list = lists.tile([P, QUERIES // 16], U16, name="rel_list")
+
+        tails = [held.tile([P, ENTITIES], F32, name="tails%d" % k) for k in range(BLOCKS)]
+        heads = [held.tile([P, ENTITIES], F32, name="heads%d" % k) for k in range(BLOCKS)]
+        rels = [held.tile([P, RELATIONS], F32, name="rels%d" % k) for k in range(BLOCKS)]
+        grads = [held.tile([P, 2, SLOTS], F32, name="grads%d" % h) for h in range(2)]
+        dh = [held.tile([P, ENTITIES], F32, name="dh%d" % k) for k in range(DH_TILES)]
+        dr = [held.tile([P, RELATIONS], F32, name="dr%d" % k) for k in range(DR_TILES)]
+        ident = held.tile([P, P], F32, name="ident")
+
+        def rows(k):
+            return slice(k * P, (k + 1) * P)
+
+        nc.sync.dma_start(tails[0][:], tT[rows(0), :])
+        nc.sync.dma_start(tail_list[:], offs)
+        for h in range(2):
+            nc.sync.dma_start(grads[h][:], G[h * 2 * P:(h + 1) * 2 * P, :].rearrange("(a p) i -> p a i", p=P))
+        nc.sync.dma_start(rel_list[:], roffs)
+        nc.sync.dma_start(rels[0][:], rT[rows(0), :])
+        nc.sync.dma_start(head_list[:], hoffs)
+        half = ENTITIES // 2
+        for k in range(1, BLOCKS):
+            if k == 1:
+                nc.sync.dma_start(tails[k][:, :half], tT[rows(k), :half])
+                nc.sync.dma_start(tails[k][:, half:], tT[rows(k), half:])
+            else:
+                nc.sync.dma_start(tails[k][:], tT[rows(k), :])
+            nc.sync.dma_start(rels[k][:], rT[rows(k), :])
+            nc.sync.dma_start(heads[k - 1][:], hT[rows(k - 1), :])
+        nc.sync.dma_start(heads[BLOCKS - 1][:], hT[rows(BLOCKS - 1), :])
+
+        make_identity(nc, ident[:])
+        for window in dh + dr:
+            nc.vector.memset(window[:], 0.0)
+
+        def turn(src, dst, bank):
+            words = src.bitcast(F32)
+            for u in range(2):
+                nc.tensor.transpose(bank[:, u, :], words[:, u::2], ident[:])
+            nc.scalar.copy(dst.bitcast(F32).rearrange("p (x u) -> p x u", u=2), bank[:].rearrange("p u x -> p x u"))
+
+        def tails_operand(k):
+            picked = held.tile([P, SLOTS], BF16, name="picked%d" % k, align_bytes=64)
+            if k == 0:
+                nc.vector.tensor_copy(picked[:], tails[k][:].indirect(tail_list[:]))
+            else:
+                rounded = held.tile([P, ENTITIES], BF16, name="rounded%d" % k, align_bytes=64)
+                if k == 1:
+                    nc.scalar.activation(rounded[:, :half], tails[k][:, :half], COPY)
+                    nc.scalar.activation(rounded[:, half:], tails[k][:, half:], COPY)
+                else:
+                    nc.scalar.activation(rounded[:], tails[k][:], COPY)
+                nc.scalar.activation(picked[:], rounded[:].indirect(tail_list[:]), COPY)
+            grouped = held.tile([P, 4 * P], BF16, name="tgrouped%d" % k, tag="tgrouped%d" % k, align_bytes=64)
+            bank = psum2.tile([P, 2, P], F32, name="tbank")
+            turn(picked[:], grouped[:], bank)
+            return grouped
+
+        def quantise_tails(k, grouped):
+            codes = held.tile([P, P], U32, name="tcodes%d" % k, align_bytes=64)
+            scales = held.tile([P, P], U8, name="tscales%d" % k, align_bytes=64)
+            nc.vector.quantize_mx(out=codes[:].bitcast(E4M3X4), scales=scales[:], in_=grouped[:])
+            return codes, scales
+
+        grouped0 = tails_operand(0)
+
+        g_codes = held.tile([P, QUERIES], U32, name="g_codes", align_bytes=64)
+        g_scales = held.tile([P, QUERIES], U8, name="g_scales", align_bytes=64)
+        g_grouped = []
+        for a in range(QBLOCKS):
+            g_bf = held.tile([P, SLOTS], BF16, name="g_bf%d" % a, align_bytes=64)
+            if a == 0:
+                nc.scalar.activation(g_bf[:], grads[a // 2][:, a % 2, :], COPY)
+            else:
+                nc.vector.tensor_copy(g_bf[:], grads[a // 2][:, a % 2, :])
+            gg = held.tile([P, 4 * P], BF16, name="g_grouped%d" % a, tag="g_grouped%d" % a, align_bytes=64)
+            bank = psum.tile([P, 2, P], F32, name="gbank%d" % a)
+            turn(g_bf[:], gg[:], bank)
+            g_grouped.append(gg)
+        operand = quantise_tails(0, grouped0)
+        for a in range(QBLOCKS):
+            nc.vector.quantize_mx(out=g_codes[:, rows(a)].bitcast(E5M2X4), scales=g_scales[:, rows(a)], in_=g_grouped[a][:])
+
+        def product(k, operand):
+            codes, scales = operand
+            acc = psum2.tile([P, QUERIES], F32, name="acc")
+            nc.tensor.matmul_mx(out=acc[:], lhsT=codes[:].bitcast(E4M3X4), lhsT_scale=scales[:],
+                                rhs=g_codes[:].bitcast(E5M2X4), rhs_scale=g_scales[:], start=True, stop=True)
+            b = held.tile([P, QUERIES], F32, name="b%d" % k)
+            nc.scalar.copy(b[:], acc[:])
+            return b
+
+        def pick_rels(k):
+            if k == 0:
+                picked = held.tile([P, QUERIES], F32, name="r_picked0", tag="g_grouped%d" % (QBLOCKS - 1), align_bytes=64)
+            else:
+                picked = held.tile([P, QUERIES], F32, name="r_picked%d" % k)
+            nc.vector.tensor_copy(picked[:], rels[k][:].indirect(rel_list[:]))
+            return picked
+
+        b = product(0, operand)
+        r_picked = pick_rels(0)
+        for k in range(BLOCKS):
+            last = k + 1 == BLOCKS
+            nc.vector.tensor_tensor(dh[k % DH_TILES][:].indirect(head_list[:]), b[:], r_picked[:], MULT)
+            nc.sync.dma_start(out_0[rows(k), :], dh[k % DH_TILES][:])
+            b_now = b
+            if last:
+                h_picked = held.tile([P, QUERIES], F32, name="h_picked%d" % k)
+            else:
+                r_picked = pick_rels(k + 1)
+                b = product(k + 1, quantise_tails(k + 1, tails_operand(k + 1)))
+                h_picked = held.tile([P, QUERIES], F32, name="h_picked%d" % k, tag="tgrouped%d" % (k + 1), align_bytes=64)
+            nc.vector.tensor_copy(h_picked[:], heads[k][:].indirect(head_list[:]))
+            nc.vector.tensor_tensor(dr[k % DR_TILES][:].indirect(rel_list[:]), b_now[:], h_picked[:], MULT)
+            nc.sync.dma_start(out_1[rows(k), :], dr[k % DR_TILES][:])

@@ -5,6 +5,7 @@ from concourse.masks import make_identity
 
 F32 = mybir.dt.float32
 BF16 = mybir.dt.bfloat16
+I32 = mybir.dt.int32
 U32 = mybir.dt.uint32
 U16 = mybir.dt.uint16
 U8 = mybir.dt.uint8
@@ -21,8 +22,10 @@ ENTITIES = 2048
 RELATIONS = 1024
 BLOCKS = FEATURES // P
 QBLOCKS = QUERIES // P
-DH_TILES = 3
-DR_TILES = 2
+OUT_TILES = 2
+PICK = 4 * QUERIES
+GROUPED = 2 * SLOTS
+TABLE = 4 * ENTITIES
 
 FLOPS = 2 * FEATURES * QUERIES * SLOTS
 
@@ -32,32 +35,46 @@ def tile_attend_gdistm_hr_kernel(tc, hT, rT, G, tT, hoffs, roffs, offs, out_0, o
     with ExitStack() as ctx:
         lists = ctx.enter_context(tc.tile_pool(name="lists", bufs=1))
         held = ctx.enter_context(tc.tile_pool(name="held", bufs=1))
+        shared = ctx.enter_context(tc.tile_pool(name="shared", bufs=1))
         psum = ctx.enter_context(tc.psum_pool(name="psum", bufs=1))
         psum2 = ctx.enter_context(tc.psum_pool(name="psum2", bufs=2))
+
+        def pair_at(k):
+            return TABLE - PICK + 2 * PICK * k
+
+        def grouped_at(k):
+            return pair_at(k) + PICK - GROUPED // 2
+
+        first_codes_at = pair_at(BLOCKS)
+        second_dh_at = first_codes_at + TABLE // 2
+        first_heads_at = second_dh_at + TABLE // 2
+        second_dr_at = second_dh_at + TABLE
 
         tail_list = lists.tile([P, SLOTS // 16], U16, name="tail_list")
         head_list = lists.tile([P, QUERIES // 16], U16, name="head_list")
         rel_list = lists.tile([P, QUERIES // 16], U16, name="rel_list")
 
         tails = [held.tile([P, ENTITIES], F32, name="tails%d" % k) for k in range(BLOCKS)]
-        heads = [held.tile([P, ENTITIES], F32, name="heads%d" % k) for k in range(BLOCKS)]
+        heads = [shared.tile([P, ENTITIES], F32, name="heads0", align_bytes=64, offset=first_heads_at)]
+        heads.extend([held.tile([P, ENTITIES], F32, name="heads%d" % k) for k in range(1, BLOCKS - 1)])
         rels = [held.tile([P, RELATIONS], F32, name="rels%d" % k) for k in range(BLOCKS)]
-        grads = [held.tile([P, 2, SLOTS], F32, name="grads%d" % h) for h in range(2)]
-        dh = [held.tile([P, ENTITIES], F32, name="dh%d" % k) for k in range(DH_TILES)]
-        dr = [held.tile([P, RELATIONS], F32, name="dr%d" % k) for k in range(DR_TILES)]
+        grads = [held.tile([P, SLOTS], F32, name="grads%d" % a) for a in range(QBLOCKS)]
+        dh = [held.tile([P, ENTITIES], F32, name="dh0")]
+        dr = [held.tile([P, RELATIONS], F32, name="dr0")]
         ident = held.tile([P, P], F32, name="ident")
 
         def rows(k):
             return slice(k * P, (k + 1) * P)
 
+        half = ENTITIES // 2
         nc.sync.dma_start(tails[0][:], tT[rows(0), :])
         nc.sync.dma_start(tail_list[:], offs)
-        for h in range(2):
-            nc.sync.dma_start(grads[h][:], G[h * 2 * P:(h + 1) * 2 * P, :].rearrange("(a p) i -> p a i", p=P))
+        for a in range(QBLOCKS):
+            nc.sync.dma_start(grads[a][:], G[rows(a), :])
         nc.sync.dma_start(rel_list[:], roffs)
         nc.sync.dma_start(rels[0][:], rT[rows(0), :])
         nc.sync.dma_start(head_list[:], hoffs)
-        half = ENTITIES // 2
+        nc.sync.dma_start(heads[0][:], hT[rows(0), :])
         for k in range(1, BLOCKS):
             if k == 1:
                 nc.sync.dma_start(tails[k][:, :half], tT[rows(k), :half])
@@ -65,12 +82,12 @@ def tile_attend_gdistm_hr_kernel(tc, hT, rT, G, tT, hoffs, roffs, offs, out_0, o
             else:
                 nc.sync.dma_start(tails[k][:], tT[rows(k), :])
             nc.sync.dma_start(rels[k][:], rT[rows(k), :])
-            nc.sync.dma_start(heads[k - 1][:], hT[rows(k - 1), :])
-        nc.sync.dma_start(heads[BLOCKS - 1][:], hT[rows(BLOCKS - 1), :])
+            if k + 1 < BLOCKS:
+                nc.sync.dma_start(heads[k][:], hT[rows(k), :])
 
         make_identity(nc, ident[:])
         for window in dh + dr:
-            nc.vector.memset(window[:], 0.0)
+            nc.vector.memset(window[:].bitcast(I32), 0)
 
         def turn(src, dst, bank):
             words = src.bitcast(F32)
@@ -82,21 +99,26 @@ def tile_attend_gdistm_hr_kernel(tc, hT, rT, G, tT, hoffs, roffs, offs, out_0, o
             picked = held.tile([P, SLOTS], BF16, name="picked%d" % k, align_bytes=64)
             if k == 0:
                 nc.vector.tensor_copy(picked[:], tails[k][:].indirect(tail_list[:]))
+                grouped = held.tile([P, 4 * P], BF16, name="tgrouped0", align_bytes=64)
             else:
-                rounded = held.tile([P, ENTITIES], BF16, name="rounded%d" % k, align_bytes=64)
                 if k == 1:
+                    rounded = shared.tile([P, ENTITIES], BF16, name="rounded1", align_bytes=64, offset=first_codes_at)
                     nc.scalar.activation(rounded[:, :half], tails[k][:, :half], COPY)
                     nc.scalar.activation(rounded[:, half:], tails[k][:, half:], COPY)
                 else:
+                    rounded = held.tile([P, ENTITIES], BF16, name="rounded%d" % k, align_bytes=64)
                     nc.scalar.activation(rounded[:], tails[k][:], COPY)
                 nc.scalar.activation(picked[:], rounded[:].indirect(tail_list[:]), COPY)
-            grouped = held.tile([P, 4 * P], BF16, name="tgrouped%d" % k, tag="tgrouped%d" % k, align_bytes=64)
+                grouped = shared.tile([P, 4 * P], BF16, name="tgrouped%d" % k, align_bytes=64, offset=grouped_at(k))
             bank = psum2.tile([P, 2, P], F32, name="tbank")
             turn(picked[:], grouped[:], bank)
             return grouped
 
         def quantise_tails(k, grouped):
-            codes = held.tile([P, P], U32, name="tcodes%d" % k, align_bytes=64)
+            if k == 0:
+                codes = shared.tile([P, P], U32, name="tcodes0", align_bytes=64, offset=first_codes_at)
+            else:
+                codes = held.tile([P, P], U32, name="tcodes%d" % k, align_bytes=64)
             scales = held.tile([P, P], U8, name="tscales%d" % k, align_bytes=64)
             nc.vector.quantize_mx(out=codes[:].bitcast(E4M3X4), scales=scales[:], in_=grouped[:])
             return codes, scales
@@ -109,10 +131,13 @@ def tile_attend_gdistm_hr_kernel(tc, hT, rT, G, tT, hoffs, roffs, offs, out_0, o
         for a in range(QBLOCKS):
             g_bf = held.tile([P, SLOTS], BF16, name="g_bf%d" % a, align_bytes=64)
             if a == 0:
-                nc.scalar.activation(g_bf[:], grads[a // 2][:, a % 2, :], COPY)
+                nc.scalar.activation(g_bf[:], grads[a][:], COPY)
             else:
-                nc.vector.tensor_copy(g_bf[:], grads[a // 2][:, a % 2, :])
-            gg = held.tile([P, 4 * P], BF16, name="g_grouped%d" % a, tag="g_grouped%d" % a, align_bytes=64)
+                nc.vector.tensor_copy(g_bf[:], grads[a][:])
+            if a + 1 == QBLOCKS:
+                gg = shared.tile([P, 4 * P], BF16, name="g_grouped%d" % a, align_bytes=64, offset=grouped_at(0))
+            else:
+                gg = held.tile([P, 4 * P], BF16, name="g_grouped%d" % a, align_bytes=64)
             bank = psum.tile([P, 2, P], F32, name="gbank%d" % a)
             turn(g_bf[:], gg[:], bank)
             g_grouped.append(gg)
@@ -129,27 +154,26 @@ def tile_attend_gdistm_hr_kernel(tc, hT, rT, G, tT, hoffs, roffs, offs, out_0, o
             nc.scalar.copy(b[:], acc[:])
             return b
 
-        def pick_rels(k):
-            if k == 0:
-                picked = held.tile([P, QUERIES], F32, name="r_picked0", tag="g_grouped%d" % (QBLOCKS - 1), align_bytes=64)
-            else:
-                picked = held.tile([P, QUERIES], F32, name="r_picked%d" % k)
-            nc.vector.tensor_copy(picked[:], rels[k][:].indirect(rel_list[:]))
+        def pick(name, table, offsets, at):
+            picked = shared.tile([P, QUERIES], F32, name=name, align_bytes=64, offset=at)
+            nc.vector.tensor_copy(picked[:], table[:].indirect(offsets[:]))
             return picked
 
-        b = product(0, operand)
-        r_picked = pick_rels(0)
         for k in range(BLOCKS):
-            last = k + 1 == BLOCKS
-            nc.vector.tensor_tensor(dh[k % DH_TILES][:].indirect(head_list[:]), b[:], r_picked[:], MULT)
-            nc.sync.dma_start(out_0[rows(k), :], dh[k % DH_TILES][:])
-            b_now = b
-            if last:
-                h_picked = held.tile([P, QUERIES], F32, name="h_picked%d" % k)
-            else:
-                r_picked = pick_rels(k + 1)
-                b = product(k + 1, quantise_tails(k + 1, tails_operand(k + 1)))
-                h_picked = held.tile([P, QUERIES], F32, name="h_picked%d" % k, tag="tgrouped%d" % (k + 1), align_bytes=64)
-            nc.vector.tensor_copy(h_picked[:], heads[k][:].indirect(head_list[:]))
-            nc.vector.tensor_tensor(dr[k % DR_TILES][:].indirect(rel_list[:]), b_now[:], h_picked[:], MULT)
-            nc.sync.dma_start(out_1[rows(k), :], dr[k % DR_TILES][:])
+            if k > 0:
+                operand = quantise_tails(k, tails_operand(k))
+            b = product(k, operand)
+            r_picked = pick("r_picked%d" % k, rels[k], rel_list, pair_at(k))
+            h_picked = pick("h_picked%d" % k, heads[k], head_list, pair_at(k) + PICK)
+            if k == 0:
+                dh.append(shared.tile([P, ENTITIES], F32, name="dh1", align_bytes=64, offset=second_dh_at))
+                dr.append(shared.tile([P, RELATIONS], F32, name="dr1", align_bytes=64, offset=second_dr_at))
+                nc.gpsimd.memset(dh[1][:].bitcast(I32), 0)
+                nc.gpsimd.memset(dr[1][:].bitcast(I32), 0)
+            nc.vector.tensor_tensor(dh[k % OUT_TILES][:].indirect(head_list[:]), b[:], r_picked[:], MULT)
+            nc.sync.dma_start(out_0[rows(k), :], dh[k % OUT_TILES][:])
+            nc.vector.tensor_tensor(dr[k % OUT_TILES][:].indirect(rel_list[:]), b[:], h_picked[:], MULT)
+            nc.sync.dma_start(out_1[rows(k), :], dr[k % OUT_TILES][:])
+            if k == 0:
+                heads.append(shared.tile([P, ENTITIES], F32, name="last_heads", align_bytes=64, offset=0))
+                nc.sync.dma_start(heads[BLOCKS - 1][:], hT[rows(BLOCKS - 1), :])

@@ -40,13 +40,14 @@ def tile_attend_gdistm_hr_kernel(tc, hT, rT, G, tT, hoffs, roffs, offs, out_0, o
         psum2 = ctx.enter_context(tc.psum_pool(name="psum2", bufs=2))
 
         def pair_at(k):
-            return TABLE - PICK + 2 * PICK * k
+            return 2 * PICK * k
 
         def grouped_at(k):
             return pair_at(k) + PICK - GROUPED // 2
 
-        first_codes_at = pair_at(BLOCKS)
-        second_dh_at = first_codes_at + TABLE // 2
+        first_codes_at = pair_at(3)
+        second_rounded_at = first_codes_at + TABLE // 2
+        second_dh_at = second_rounded_at + TABLE // 2
         first_heads_at = second_dh_at + TABLE // 2
         second_dr_at = second_dh_at + TABLE
 
@@ -56,7 +57,7 @@ def tile_attend_gdistm_hr_kernel(tc, hT, rT, G, tT, hoffs, roffs, offs, out_0, o
 
         tails = [held.tile([P, ENTITIES], F32, name="tails%d" % k) for k in range(BLOCKS)]
         heads = [shared.tile([P, ENTITIES], F32, name="heads0", align_bytes=64, offset=first_heads_at)]
-        heads.extend([held.tile([P, ENTITIES], F32, name="heads%d" % k) for k in range(1, BLOCKS - 1)])
+        heads.extend([held.tile([P, ENTITIES], F32, name="heads%d" % k) for k in range(1, BLOCKS)])
         rels = [held.tile([P, RELATIONS], F32, name="rels%d" % k) for k in range(BLOCKS)]
         grads = [held.tile([P, SLOTS], F32, name="grads%d" % a) for a in range(QBLOCKS)]
         dh = [held.tile([P, ENTITIES], F32, name="dh0")]
@@ -72,18 +73,18 @@ def tile_attend_gdistm_hr_kernel(tc, hT, rT, G, tT, hoffs, roffs, offs, out_0, o
         for a in range(QBLOCKS):
             nc.sync.dma_start(grads[a][:], G[rows(a), :])
         nc.sync.dma_start(rel_list[:], roffs)
-        nc.sync.dma_start(rels[0][:], rT[rows(0), :])
-        nc.sync.dma_start(head_list[:], hoffs)
-        nc.sync.dma_start(heads[0][:], hT[rows(0), :])
-        for k in range(1, BLOCKS):
-            if k == 1:
-                nc.sync.dma_start(tails[k][:, :half], tT[rows(k), :half])
-                nc.sync.dma_start(tails[k][:, half:], tT[rows(k), half:])
-            else:
-                nc.sync.dma_start(tails[k][:], tT[rows(k), :])
+        for k in range(3):
             nc.sync.dma_start(rels[k][:], rT[rows(k), :])
-            if k + 1 < BLOCKS:
-                nc.sync.dma_start(heads[k][:], hT[rows(k), :])
+        nc.sync.dma_start(head_list[:], hoffs)
+        nc.sync.dma_start(tails[1][:, :half], tT[rows(1), :half])
+        nc.sync.dma_start(tails[1][:, half:], tT[rows(1), half:])
+        nc.sync.dma_start(heads[0][:], hT[rows(0), :])
+        nc.sync.dma_start(tails[2][:], tT[rows(2), :])
+        nc.sync.dma_start(heads[1][:], hT[rows(1), :])
+        nc.sync.dma_start(rels[3][:], rT[rows(3), :])
+        nc.sync.dma_start(tails[3][:], tT[rows(3), :])
+        nc.sync.dma_start(heads[2][:], hT[rows(2), :])
+        nc.sync.dma_start(heads[3][:], hT[rows(3), :])
 
         make_identity(nc, ident[:])
         for window in dh + dr:
@@ -95,35 +96,44 @@ def tile_attend_gdistm_hr_kernel(tc, hT, rT, G, tT, hoffs, roffs, offs, out_0, o
                 nc.tensor.transpose(bank[:, u, :], words[:, u::2], ident[:])
             nc.scalar.copy(dst.bitcast(F32).rearrange("p (x u) -> p x u", u=2), bank[:].rearrange("p u x -> p x u"))
 
-        def tails_operand(k):
-            picked = held.tile([P, SLOTS], BF16, name="picked%d" % k, align_bytes=64)
-            if k == 0:
-                nc.vector.tensor_copy(picked[:], tails[k][:].indirect(tail_list[:]))
-                grouped = held.tile([P, 4 * P], BF16, name="tgrouped0", align_bytes=64)
-            else:
-                if k == 1:
-                    rounded = shared.tile([P, ENTITIES], BF16, name="rounded1", align_bytes=64, offset=first_codes_at)
-                    nc.scalar.activation(rounded[:, :half], tails[k][:, :half], COPY)
-                    nc.scalar.activation(rounded[:, half:], tails[k][:, half:], COPY)
-                else:
-                    rounded = held.tile([P, ENTITIES], BF16, name="rounded%d" % k, align_bytes=64)
-                    nc.scalar.activation(rounded[:], tails[k][:], COPY)
-                nc.scalar.activation(picked[:], rounded[:].indirect(tail_list[:]), COPY)
-                grouped = shared.tile([P, 4 * P], BF16, name="tgrouped%d" % k, align_bytes=64, offset=grouped_at(k))
+        def turn_tails(k, picked, grouped):
             bank = psum2.tile([P, 2, P], F32, name="tbank")
-            turn(picked[:], grouped[:], bank)
-            return grouped
+            turn(picked[:], grouped, bank)
 
-        def quantise_tails(k, grouped):
-            if k == 0:
-                codes = shared.tile([P, P], U32, name="tcodes0", align_bytes=64, offset=first_codes_at)
-            else:
-                codes = held.tile([P, P], U32, name="tcodes%d" % k, align_bytes=64)
-            scales = held.tile([P, P], U8, name="tscales%d" % k, align_bytes=64)
-            nc.vector.quantize_mx(out=codes[:].bitcast(E4M3X4), scales=scales[:], in_=grouped[:])
-            return codes, scales
+        def pick_tails_on_scalar(k, rounded, pieces):
+            width = ENTITIES // pieces
+            for c in range(0, ENTITIES, width):
+                nc.scalar.activation(rounded[:, c:c + width], tails[k][:, c:c + width], COPY)
+            picked = held.tile([P, SLOTS], BF16, name="picked%d" % k, tag="picked%d" % k, align_bytes=64)
+            nc.scalar.activation(picked[:], rounded[:].indirect(tail_list[:]), COPY)
+            return picked
 
-        grouped0 = tails_operand(0)
+        def pick(picked, table, offsets):
+            nc.vector.tensor_copy(picked[:], table[:].indirect(offsets[:]))
+            return picked
+
+        def pick_at(name, table, offsets, at):
+            return pick(shared.tile([P, QUERIES], F32, name=name, align_bytes=64, offset=at), table, offsets)
+
+        def product(codes, scales, b):
+            acc = psum2.tile([P, QUERIES], F32, name="acc")
+            nc.tensor.matmul_mx(out=acc[:], lhsT=codes.bitcast(E4M3X4), lhsT_scale=scales,
+                                rhs=g_codes[:].bitcast(E5M2X4), rhs_scale=g_scales[:], start=True, stop=True)
+            nc.scalar.copy(b[:], acc[:])
+            return b
+
+        def put_heads(k, b, r_picked):
+            nc.vector.tensor_tensor(dh[k % OUT_TILES][:].indirect(head_list[:]), b[:], r_picked[:], MULT)
+            nc.sync.dma_start(out_0[rows(k), :], dh[k % OUT_TILES][:])
+
+        def put_rels(k, b, h_picked):
+            nc.vector.tensor_tensor(dr[k % OUT_TILES][:].indirect(rel_list[:]), b[:], h_picked[:], MULT)
+            nc.sync.dma_start(out_1[rows(k), :], dr[k % OUT_TILES][:])
+
+        picked0 = held.tile([P, SLOTS], BF16, name="picked0", align_bytes=64)
+        pick(picked0, tails[0], tail_list)
+        grouped0 = held.tile([P, 4 * P], BF16, name="tgrouped0", align_bytes=64)
+        turn_tails(0, picked0, grouped0[:])
 
         g_codes = held.tile([P, QUERIES], U32, name="g_codes", align_bytes=64)
         g_scales = held.tile([P, QUERIES], U8, name="g_scales", align_bytes=64)
@@ -141,39 +151,52 @@ def tile_attend_gdistm_hr_kernel(tc, hT, rT, G, tT, hoffs, roffs, offs, out_0, o
             bank = psum.tile([P, 2, P], F32, name="gbank%d" % a)
             turn(g_bf[:], gg[:], bank)
             g_grouped.append(gg)
-        operand = quantise_tails(0, grouped0)
+
+        codes0 = shared.tile([P, P], U32, name="tcodes0", align_bytes=64, offset=first_codes_at)
+        scales0 = held.tile([P, P], U8, name="tscales0", align_bytes=64)
+        nc.vector.quantize_mx(out=codes0[:].bitcast(E4M3X4), scales=scales0[:], in_=grouped0[:])
+        r0 = held.tile([P, QUERIES], F32, name="r_picked0")
         for a in range(QBLOCKS):
+            if a + 1 == QBLOCKS:
+                pick(r0, rels[0], rel_list)
             nc.vector.quantize_mx(out=g_codes[:, rows(a)].bitcast(E5M2X4), scales=g_scales[:, rows(a)], in_=g_grouped[a][:])
+        b0 = product(codes0[:], scales0[:], held.tile([P, QUERIES], F32, name="b0"))
+        r1 = pick_at("r_picked1", rels[1], rel_list, pair_at(0))
+        r2 = pick_at("r_picked2", rels[2], rel_list, pair_at(0) + PICK)
+        put_heads(0, b0, r0)
+        h0 = pick(held.tile([P, QUERIES], F32, name="h_picked0"), heads[0], head_list)
+        dh.append(shared.tile([P, ENTITIES], F32, name="dh1", align_bytes=64, offset=second_dh_at))
+        dr.append(shared.tile([P, RELATIONS], F32, name="dr1", align_bytes=64, offset=second_dr_at))
+        nc.gpsimd.memset(dh[1][:].bitcast(I32), 0)
+        nc.gpsimd.memset(dr[1][:].bitcast(I32), 0)
+        put_rels(0, b0, h0)
 
-        def product(k, operand):
-            codes, scales = operand
-            acc = psum2.tile([P, QUERIES], F32, name="acc")
-            nc.tensor.matmul_mx(out=acc[:], lhsT=codes[:].bitcast(E4M3X4), lhsT_scale=scales[:],
-                                rhs=g_codes[:].bitcast(E5M2X4), rhs_scale=g_scales[:], start=True, stop=True)
-            b = held.tile([P, QUERIES], F32, name="b%d" % k)
-            nc.scalar.copy(b[:], acc[:])
-            return b
+        rounded1 = shared.tile([P, ENTITIES], BF16, name="rounded1", align_bytes=64, offset=first_codes_at)
+        grouped1 = shared.tile([P, 4 * P], BF16, name="tgrouped1", align_bytes=64, offset=grouped_at(1))
+        turn_tails(1, pick_tails_on_scalar(1, rounded1, 2), grouped1[:])
+        rounded2 = shared.tile([P, ENTITIES], BF16, name="rounded2", align_bytes=64, offset=second_rounded_at)
+        picked2 = pick_tails_on_scalar(2, rounded2, 1)
+        grouped23 = shared.tile([P, 8 * P], BF16, name="tgrouped23", align_bytes=64, offset=pair_at(2) + PICK - GROUPED)
+        turn_tails(2, picked2, grouped23[:, :4 * P])
+        codes1 = held.tile([P, P], U32, name="tcodes1", align_bytes=64)
+        scales1 = held.tile([P, P], U8, name="tscales1", align_bytes=64)
+        nc.vector.quantize_mx(out=codes1[:].bitcast(E4M3X4), scales=scales1[:], in_=grouped1[:])
+        b1 = product(codes1[:], scales1[:], held.tile([P, QUERIES], F32, name="b1", tag="picked2", align_bytes=64))
+        h1 = pick(held.tile([P, QUERIES], F32, name="h_picked1"), heads[1], head_list)
+        r3 = pick(held.tile([P, QUERIES], F32, name="r_picked3"), rels[3], rel_list)
+        put_heads(1, b1, r1)
+        put_rels(1, b1, h1)
 
-        def pick(name, table, offsets, at):
-            picked = shared.tile([P, QUERIES], F32, name=name, align_bytes=64, offset=at)
-            nc.vector.tensor_copy(picked[:], table[:].indirect(offsets[:]))
-            return picked
-
-        for k in range(BLOCKS):
-            if k > 0:
-                operand = quantise_tails(k, tails_operand(k))
-            b = product(k, operand)
-            r_picked = pick("r_picked%d" % k, rels[k], rel_list, pair_at(k))
-            h_picked = pick("h_picked%d" % k, heads[k], head_list, pair_at(k) + PICK)
-            if k == 0:
-                dh.append(shared.tile([P, ENTITIES], F32, name="dh1", align_bytes=64, offset=second_dh_at))
-                dr.append(shared.tile([P, RELATIONS], F32, name="dr1", align_bytes=64, offset=second_dr_at))
-                nc.gpsimd.memset(dh[1][:].bitcast(I32), 0)
-                nc.gpsimd.memset(dr[1][:].bitcast(I32), 0)
-            nc.vector.tensor_tensor(dh[k % OUT_TILES][:].indirect(head_list[:]), b[:], r_picked[:], MULT)
-            nc.sync.dma_start(out_0[rows(k), :], dh[k % OUT_TILES][:])
-            nc.vector.tensor_tensor(dr[k % OUT_TILES][:].indirect(rel_list[:]), b[:], h_picked[:], MULT)
-            nc.sync.dma_start(out_1[rows(k), :], dr[k % OUT_TILES][:])
-            if k == 0:
-                heads.append(shared.tile([P, ENTITIES], F32, name="last_heads", align_bytes=64, offset=0))
-                nc.sync.dma_start(heads[BLOCKS - 1][:], hT[rows(BLOCKS - 1), :])
+        rounded3 = held.tile([P, ENTITIES], BF16, name="rounded3", align_bytes=64)
+        turn_tails(3, pick_tails_on_scalar(3, rounded3, 1), grouped23[:, 4 * P:])
+        codes23 = held.tile([P, 2 * P], U32, name="tcodes23", align_bytes=64)
+        scales23 = held.tile([P, 2 * P], U8, name="tscales23", align_bytes=64)
+        nc.vector.quantize_mx(out=codes23[:].bitcast(E4M3X4), scales=scales23[:], in_=grouped23[:])
+        b2 = product(codes23[:, :P], scales23[:, :P], held.tile([P, QUERIES], F32, name="b2"))
+        b3 = product(codes23[:, P:], scales23[:, P:], held.tile([P, QUERIES], F32, name="b3"))
+        h2 = pick_at("h_picked2", heads[2], head_list, pair_at(2))
+        h3 = pick_at("h_picked3", heads[3], head_list, pair_at(2) + PICK)
+        put_heads(2, b2, r2)
+        put_rels(2, b2, h2)
+        put_heads(3, b3, r3)
+        put_rels(3, b3, h3)

@@ -56,12 +56,11 @@ def tile_attend_gdistm_hr_kernel(tc, hT, rT, G, tT, hoffs, roffs, offs, out_0, o
         rel_list = lists.tile([P, QUERIES // 16], U16, name="rel_list")
 
         tails = [held.tile([P, ENTITIES], F32, name="tails%d" % k) for k in range(BLOCKS)]
-        heads = [shared.tile([P, ENTITIES], F32, name="heads0", align_bytes=64, offset=first_heads_at)]
-        heads.extend([held.tile([P, ENTITIES], F32, name="heads%d" % k) for k in range(1, BLOCKS)])
+        heads = [held.tile([P, ENTITIES], F32, name="heads%d" % k) for k in range(BLOCKS)]
         rels = [held.tile([P, RELATIONS], F32, name="rels%d" % k) for k in range(BLOCKS)]
         grads = [held.tile([P, SLOTS], F32, name="grads%d" % a) for a in range(QBLOCKS)]
         dh = [held.tile([P, ENTITIES], F32, name="dh0")]
-        dr = [held.tile([P, RELATIONS], F32, name="dr0")]
+        dr = [held.tile([P, RELATIONS], F32, name="dr%d" % k) for k in range(OUT_TILES)]
         ident = held.tile([P, P], F32, name="ident")
 
         def rows(k):
@@ -165,37 +164,39 @@ def tile_attend_gdistm_hr_kernel(tc, hT, rT, G, tT, hoffs, roffs, offs, out_0, o
         r2 = pick_at("r_picked2", rels[2], rel_list, pair_at(0) + PICK)
         put_heads(0, b0, r0)
         h0 = pick(held.tile([P, QUERIES], F32, name="h_picked0"), heads[0], head_list)
-        dh.append(shared.tile([P, ENTITIES], F32, name="dh1", align_bytes=64, offset=second_dh_at))
-        dr.append(shared.tile([P, RELATIONS], F32, name="dr1", align_bytes=64, offset=second_dr_at))
-        nc.gpsimd.memset(dh[1][:].bitcast(I32), 0)
-        nc.gpsimd.memset(dr[1][:].bitcast(I32), 0)
         put_rels(0, b0, h0)
 
         rounded1 = shared.tile([P, ENTITIES], BF16, name="rounded1", align_bytes=64, offset=first_codes_at)
-        grouped1 = shared.tile([P, 4 * P], BF16, name="tgrouped1", align_bytes=64, offset=grouped_at(1))
+        grouped1 = shared.tile([P, 4 * P], BF16, name="tgrouped1", align_bytes=64, offset=second_dh_at)
         turn_tails(1, pick_tails_on_scalar(1, rounded1, 2), grouped1[:])
         rounded2 = shared.tile([P, ENTITIES], BF16, name="rounded2", align_bytes=64, offset=second_rounded_at)
         picked2 = pick_tails_on_scalar(2, rounded2, 1)
-        grouped23 = shared.tile([P, 8 * P], BF16, name="tgrouped23", align_bytes=64, offset=pair_at(2) + PICK - GROUPED)
-        turn_tails(2, picked2, grouped23[:, :4 * P])
+        grouped2 = held.tile([P, 4 * P], BF16, name="tgrouped2", align_bytes=64)
+        turn_tails(2, picked2, grouped2[:])
         codes1 = held.tile([P, P], U32, name="tcodes1", align_bytes=64)
         scales1 = held.tile([P, P], U8, name="tscales1", align_bytes=64)
         nc.vector.quantize_mx(out=codes1[:].bitcast(E4M3X4), scales=scales1[:], in_=grouped1[:])
+        dh.append(shared.tile([P, ENTITIES], F32, name="dh1", align_bytes=64, offset=second_dh_at))
+        nc.gpsimd.memset(dh[1][:].bitcast(I32), 0)
         b1 = product(codes1[:], scales1[:], held.tile([P, QUERIES], F32, name="b1", tag="picked2", align_bytes=64))
         h1 = pick(held.tile([P, QUERIES], F32, name="h_picked1"), heads[1], head_list)
         r3 = pick(held.tile([P, QUERIES], F32, name="r_picked3"), rels[3], rel_list)
         put_heads(1, b1, r1)
         put_rels(1, b1, h1)
 
+        codes2 = held.tile([P, P], U32, name="tcodes2", align_bytes=64)
+        scales2 = held.tile([P, P], U8, name="tscales2", align_bytes=64)
+        nc.vector.quantize_mx(out=codes2[:].bitcast(E4M3X4), scales=scales2[:], in_=grouped2[:])
+        b2 = product(codes2[:], scales2[:], held.tile([P, QUERIES], F32, name="b2"))
+        h2 = pick(held.tile([P, QUERIES], F32, name="h_picked2"), heads[2], head_list)
         rounded3 = held.tile([P, ENTITIES], BF16, name="rounded3", align_bytes=64)
-        turn_tails(3, pick_tails_on_scalar(3, rounded3, 1), grouped23[:, 4 * P:])
-        codes23 = held.tile([P, 2 * P], U32, name="tcodes23", align_bytes=64)
-        scales23 = held.tile([P, 2 * P], U8, name="tscales23", align_bytes=64)
-        nc.vector.quantize_mx(out=codes23[:].bitcast(E4M3X4), scales=scales23[:], in_=grouped23[:])
-        b2 = product(codes23[:, :P], scales23[:, :P], held.tile([P, QUERIES], F32, name="b2"))
-        b3 = product(codes23[:, P:], scales23[:, P:], held.tile([P, QUERIES], F32, name="b3"))
-        h2 = pick_at("h_picked2", heads[2], head_list, pair_at(2))
-        h3 = pick_at("h_picked3", heads[3], head_list, pair_at(2) + PICK)
+        grouped3 = held.tile([P, 4 * P], BF16, name="tgrouped3", align_bytes=64)
+        turn_tails(3, pick_tails_on_scalar(3, rounded3, 1), grouped3[:])
+        codes3 = held.tile([P, P], U32, name="tcodes3", align_bytes=64)
+        scales3 = held.tile([P, P], U8, name="tscales3", align_bytes=64)
+        nc.vector.quantize_mx(out=codes3[:].bitcast(E4M3X4), scales=scales3[:], in_=grouped3[:])
+        b3 = product(codes3[:], scales3[:], held.tile([P, QUERIES], F32, name="b3"))
+        h3 = pick(held.tile([P, QUERIES], F32, name="h_picked3"), heads[3], head_list)
         put_heads(2, b2, r2)
         put_rels(2, b2, h2)
         put_heads(3, b3, r3)

@@ -1,7 +1,6 @@
 from contextlib import ExitStack
 
 import concourse.mybir as mybir
-from concourse.masks import make_identity
 
 F32 = mybir.dt.float32
 BF16 = mybir.dt.bfloat16
@@ -21,11 +20,10 @@ SLOTS = 512
 ENTITIES = 2048
 RELATIONS = 1024
 BLOCKS = FEATURES // P
-QBLOCKS = QUERIES // P
+QUERY_BLOCKS = QUERIES // P
 OUT_TILES = 2
-PICK = 4 * QUERIES
-GROUPED = 2 * SLOTS
-TABLE = 4 * ENTITIES
+PICKED_BYTES = 4 * QUERIES
+TURNED_BYTES = 2 * SLOTS
 
 FLOPS = 2 * FEATURES * QUERIES * SLOTS
 
@@ -36,20 +34,23 @@ def tile_attend_gdistm_hr_kernel(tc, hT, rT, G, tT, hoffs, roffs, offs, out_0, o
         lists = ctx.enter_context(tc.tile_pool(name="lists", bufs=1))
         held = ctx.enter_context(tc.tile_pool(name="held", bufs=1))
         shared = ctx.enter_context(tc.tile_pool(name="shared", bufs=1))
-        psum = ctx.enter_context(tc.psum_pool(name="psum", bufs=1))
-        psum2 = ctx.enter_context(tc.psum_pool(name="psum2", bufs=2))
+        g_banks = ctx.enter_context(tc.psum_pool(name="g_banks", bufs=1))
+        block_banks = ctx.enter_context(tc.psum_pool(name="block_banks", bufs=2))
 
-        def pair_at(k):
-            return 2 * PICK * k
+        def placed(name, shape, dtype, offset):
+            return shared.tile(shape, dtype, name=name, align_bytes=64, offset=offset)
 
-        def grouped_at(k):
-            return pair_at(k) + PICK - GROUPED // 2
+        def first_of(region):
+            return 2 * PICKED_BYTES * region
 
-        first_codes_at = pair_at(3)
-        second_rounded_at = first_codes_at + TABLE // 2
-        second_dh_at = second_rounded_at + TABLE // 2
-        first_heads_at = second_dh_at + TABLE // 2
-        second_dr_at = second_dh_at + TABLE
+        def second_of(region):
+            return first_of(region) + PICKED_BYTES
+
+        def across(region):
+            return second_of(region) - TURNED_BYTES // 2
+
+        def rows(k):
+            return slice(k * P, (k + 1) * P)
 
         tail_list = lists.tile([P, SLOTS // 16], U16, name="tail_list")
         head_list = lists.tile([P, QUERIES // 16], U16, name="head_list")
@@ -58,21 +59,18 @@ def tile_attend_gdistm_hr_kernel(tc, hT, rT, G, tT, hoffs, roffs, offs, out_0, o
         tails = [held.tile([P, ENTITIES], F32, name="tails%d" % k) for k in range(BLOCKS)]
         heads = [held.tile([P, ENTITIES], F32, name="heads%d" % k) for k in range(BLOCKS)]
         rels = [held.tile([P, RELATIONS], F32, name="rels%d" % k) for k in range(BLOCKS)]
-        grads = [held.tile([P, SLOTS], F32, name="grads%d" % a) for a in range(QBLOCKS)]
+        grads = [held.tile([P, SLOTS], F32, name="grads%d" % a) for a in range(QUERY_BLOCKS)]
         dh = [held.tile([P, ENTITIES], F32, name="dh0")]
         dr = [held.tile([P, RELATIONS], F32, name="dr%d" % k) for k in range(OUT_TILES)]
         ident = held.tile([P, P], F32, name="ident")
 
-        def rows(k):
-            return slice(k * P, (k + 1) * P)
-
         half = ENTITIES // 2
-        nc.sync.dma_start(tails[0][:], tT[rows(0), :])
-        nc.sync.dma_start(tail_list[:], offs)
-        for a in range(QBLOCKS):
+        for a in range(QUERY_BLOCKS):
             nc.sync.dma_start(grads[a][:], G[rows(a), :])
+        nc.sync.dma_start(tail_list[:], offs)
+        nc.sync.dma_start(tails[0][:], tT[rows(0), :])
         nc.sync.dma_start(rel_list[:], roffs)
-        for k in range(3):
+        for k in range(BLOCKS - 1):
             nc.sync.dma_start(rels[k][:], rT[rows(k), :])
         nc.sync.dma_start(head_list[:], hoffs)
         nc.sync.dma_start(tails[1][:, :half], tT[rows(1), :half])
@@ -85,25 +83,31 @@ def tile_attend_gdistm_hr_kernel(tc, hT, rT, G, tT, hoffs, roffs, offs, out_0, o
         nc.sync.dma_start(heads[2][:], hT[rows(2), :])
         nc.sync.dma_start(heads[3][:], hT[rows(3), :])
 
-        make_identity(nc, ident[:])
-        for window in dh + dr:
+        zeros = held.tile([P, P], F32, name="zeros", tag="dh1")
+        nc.gpsimd.memset(zeros[:], 0.0)
+        nc.gpsimd.affine_select(out=ident[:], in_=zeros[:], compare_op=mybir.AluOpType.not_equal, fill=1.0, base=0,
+                                pattern=[[-1, P]], channel_multiplier=1)
+        dh.append(held.tile([P, ENTITIES], F32, name="dh1", tag="dh1"))
+        nc.gpsimd.memset(dh[1][:].bitcast(I32), 0)
+        for window in dh[:1] + dr:
             nc.vector.memset(window[:].bitcast(I32), 0)
 
         def turn(src, dst, bank):
-            words = src.bitcast(F32)
+            words = src[:].bitcast(F32)
             for u in range(2):
                 nc.tensor.transpose(bank[:, u, :], words[:, u::2], ident[:])
-            nc.scalar.copy(dst.bitcast(F32).rearrange("p (x u) -> p x u", u=2), bank[:].rearrange("p u x -> p x u"))
+            nc.scalar.copy(dst[:].bitcast(F32).rearrange("p (x u) -> p x u", u=2), bank[:].rearrange("p u x -> p x u"))
+            return dst
 
-        def turn_tails(k, picked, grouped):
-            bank = psum2.tile([P, 2, P], F32, name="tbank")
-            turn(picked[:], grouped, bank)
+        def turn_tails(picked, turned):
+            bank = block_banks.tile([P, 2, P], F32, name="tails_bank")
+            return turn(picked, turned, bank)
 
         def pick_tails_on_scalar(k, rounded, pieces):
             width = ENTITIES // pieces
             for c in range(0, ENTITIES, width):
                 nc.scalar.activation(rounded[:, c:c + width], tails[k][:, c:c + width], COPY)
-            picked = held.tile([P, SLOTS], BF16, name="picked%d" % k, tag="picked%d" % k, align_bytes=64)
+            picked = held.tile([P, SLOTS], BF16, name="t_picked%d" % k, tag="t_picked%d" % k, align_bytes=64)
             nc.scalar.activation(picked[:], rounded[:].indirect(tail_list[:]), COPY)
             return picked
 
@@ -111,12 +115,24 @@ def tile_attend_gdistm_hr_kernel(tc, hT, rT, G, tT, hoffs, roffs, offs, out_0, o
             nc.vector.tensor_copy(picked[:], table[:].indirect(offsets[:]))
             return picked
 
-        def pick_at(name, table, offsets, at):
-            return pick(shared.tile([P, QUERIES], F32, name=name, align_bytes=64, offset=at), table, offsets)
+        def floats(name):
+            return held.tile([P, QUERIES], F32, name=name)
 
-        def product(codes, scales, b):
-            acc = psum2.tile([P, QUERIES], F32, name="acc")
-            nc.tensor.matmul_mx(out=acc[:], lhsT=codes.bitcast(E4M3X4), lhsT_scale=scales,
+        def turned_tile(name):
+            return held.tile([P, 4 * P], BF16, name=name, align_bytes=64)
+
+        def codes_tile(k):
+            return held.tile([P, P], U32, name="t_codes%d" % k, align_bytes=64)
+
+        def quantise_tails(k, turned, codes):
+            scales = held.tile([P, P], U8, name="t_scales%d" % k, align_bytes=64)
+            nc.vector.quantize_mx(out=codes[:].bitcast(E4M3X4), scales=scales[:], in_=turned[:])
+            return codes, scales
+
+        def product(operand, b):
+            codes, scales = operand
+            acc = block_banks.tile([P, QUERIES], F32, name="acc")
+            nc.tensor.matmul_mx(out=acc[:], lhsT=codes[:].bitcast(E4M3X4), lhsT_scale=scales[:],
                                 rhs=g_codes[:].bitcast(E5M2X4), rhs_scale=g_scales[:], start=True, stop=True)
             nc.scalar.copy(b[:], acc[:])
             return b
@@ -129,74 +145,48 @@ def tile_attend_gdistm_hr_kernel(tc, hT, rT, G, tT, hoffs, roffs, offs, out_0, o
             nc.vector.tensor_tensor(dr[k % OUT_TILES][:].indirect(rel_list[:]), b[:], h_picked[:], MULT)
             nc.sync.dma_start(out_1[rows(k), :], dr[k % OUT_TILES][:])
 
-        picked0 = held.tile([P, SLOTS], BF16, name="picked0", align_bytes=64)
-        pick(picked0, tails[0], tail_list)
-        grouped0 = held.tile([P, 4 * P], BF16, name="tgrouped0", align_bytes=64)
-        turn_tails(0, picked0, grouped0[:])
-
         g_codes = held.tile([P, QUERIES], U32, name="g_codes", align_bytes=64)
         g_scales = held.tile([P, QUERIES], U8, name="g_scales", align_bytes=64)
-        g_grouped = []
-        for a in range(QBLOCKS):
-            g_bf = held.tile([P, SLOTS], BF16, name="g_bf%d" % a, align_bytes=64)
-            if a == 0:
-                nc.scalar.activation(g_bf[:], grads[a][:], COPY)
+        for a in range(QUERY_BLOCKS):
+            g_rounded = held.tile([P, SLOTS], BF16, name="g_rounded%d" % a, align_bytes=64)
+            nc.scalar.activation(g_rounded[:], grads[a][:], COPY)
+            if a + 1 == QUERY_BLOCKS:
+                g_turned = placed("g_turned%d" % a, [P, 4 * P], BF16, across(1))
             else:
-                nc.vector.tensor_copy(g_bf[:], grads[a][:])
-            if a + 1 == QBLOCKS:
-                gg = shared.tile([P, 4 * P], BF16, name="g_grouped%d" % a, align_bytes=64, offset=grouped_at(0))
-            else:
-                gg = held.tile([P, 4 * P], BF16, name="g_grouped%d" % a, align_bytes=64)
-            bank = psum.tile([P, 2, P], F32, name="gbank%d" % a)
-            turn(g_bf[:], gg[:], bank)
-            g_grouped.append(gg)
+                g_turned = turned_tile("g_turned%d" % a)
+            bank = g_banks.tile([P, 2, P], F32, name="g_bank%d" % a)
+            turn(g_rounded, g_turned, bank)
+            nc.vector.quantize_mx(out=g_codes[:, rows(a)].bitcast(E5M2X4), scales=g_scales[:, rows(a)], in_=g_turned[:])
 
-        codes0 = shared.tile([P, P], U32, name="tcodes0", align_bytes=64, offset=first_codes_at)
-        scales0 = held.tile([P, P], U8, name="tscales0", align_bytes=64)
-        nc.vector.quantize_mx(out=codes0[:].bitcast(E4M3X4), scales=scales0[:], in_=grouped0[:])
-        r0 = held.tile([P, QUERIES], F32, name="r_picked0")
-        for a in range(QBLOCKS):
-            if a + 1 == QBLOCKS:
-                pick(r0, rels[0], rel_list)
-            nc.vector.quantize_mx(out=g_codes[:, rows(a)].bitcast(E5M2X4), scales=g_scales[:, rows(a)], in_=g_grouped[a][:])
-        b0 = product(codes0[:], scales0[:], held.tile([P, QUERIES], F32, name="b0"))
-        r1 = pick_at("r_picked1", rels[1], rel_list, pair_at(0))
-        r2 = pick_at("r_picked2", rels[2], rel_list, pair_at(0) + PICK)
+        t_picked0 = pick(placed("t_picked0", [P, SLOTS], BF16, second_of(1)), tails[0], tail_list)
+        t_turned0 = turn_tails(t_picked0, placed("t_turned0", [P, 4 * P], BF16, across(0)))
+        r0 = pick(placed("r_picked0", [P, QUERIES], F32, first_of(1)), rels[0], rel_list)
+        b0 = product(quantise_tails(0, t_turned0, placed("t_codes0", [P, P], U32, first_of(2))), floats("b0"))
+        r1 = pick(placed("r_picked1", [P, QUERIES], F32, first_of(0)), rels[1], rel_list)
+        r2 = pick(placed("r_picked2", [P, QUERIES], F32, second_of(0)), rels[2], rel_list)
         put_heads(0, b0, r0)
-        h0 = pick(held.tile([P, QUERIES], F32, name="h_picked0"), heads[0], head_list)
+        h0 = pick(floats("h_picked0"), heads[0], head_list)
+
+        t_rounded1 = placed("t_rounded1", [P, ENTITIES], BF16, first_of(2))
+        t_turned1 = turn_tails(pick_tails_on_scalar(1, t_rounded1, 2), turned_tile("t_turned1"))
+        t_rounded2 = held.tile([P, ENTITIES], BF16, name="t_rounded2", align_bytes=64)
+        t_picked2 = pick_tails_on_scalar(2, t_rounded2, 1)
+        t_turned2 = turn_tails(t_picked2, turned_tile("t_turned2"))
+        operand1 = quantise_tails(1, t_turned1, codes_tile(1))
         put_rels(0, b0, h0)
 
-        rounded1 = shared.tile([P, ENTITIES], BF16, name="rounded1", align_bytes=64, offset=first_codes_at)
-        grouped1 = shared.tile([P, 4 * P], BF16, name="tgrouped1", align_bytes=64, offset=second_dh_at)
-        turn_tails(1, pick_tails_on_scalar(1, rounded1, 2), grouped1[:])
-        rounded2 = shared.tile([P, ENTITIES], BF16, name="rounded2", align_bytes=64, offset=second_rounded_at)
-        picked2 = pick_tails_on_scalar(2, rounded2, 1)
-        grouped2 = held.tile([P, 4 * P], BF16, name="tgrouped2", align_bytes=64)
-        turn_tails(2, picked2, grouped2[:])
-        codes1 = held.tile([P, P], U32, name="tcodes1", align_bytes=64)
-        scales1 = held.tile([P, P], U8, name="tscales1", align_bytes=64)
-        nc.vector.quantize_mx(out=codes1[:].bitcast(E4M3X4), scales=scales1[:], in_=grouped1[:])
-        dh.append(shared.tile([P, ENTITIES], F32, name="dh1", align_bytes=64, offset=second_dh_at))
-        nc.gpsimd.memset(dh[1][:].bitcast(I32), 0)
-        b1 = product(codes1[:], scales1[:], held.tile([P, QUERIES], F32, name="b1", tag="picked2", align_bytes=64))
-        h1 = pick(held.tile([P, QUERIES], F32, name="h_picked1"), heads[1], head_list)
-        r3 = pick(held.tile([P, QUERIES], F32, name="r_picked3"), rels[3], rel_list)
+        b1 = product(operand1, held.tile([P, QUERIES], F32, name="b1", tag="t_picked2", align_bytes=64))
+        h1 = pick(floats("h_picked1"), heads[1], head_list)
+        r3 = pick(floats("r_picked3"), rels[3], rel_list)
         put_heads(1, b1, r1)
         put_rels(1, b1, h1)
 
-        codes2 = held.tile([P, P], U32, name="tcodes2", align_bytes=64)
-        scales2 = held.tile([P, P], U8, name="tscales2", align_bytes=64)
-        nc.vector.quantize_mx(out=codes2[:].bitcast(E4M3X4), scales=scales2[:], in_=grouped2[:])
-        b2 = product(codes2[:], scales2[:], held.tile([P, QUERIES], F32, name="b2"))
-        h2 = pick(held.tile([P, QUERIES], F32, name="h_picked2"), heads[2], head_list)
-        rounded3 = held.tile([P, ENTITIES], BF16, name="rounded3", align_bytes=64)
-        grouped3 = held.tile([P, 4 * P], BF16, name="tgrouped3", align_bytes=64)
-        turn_tails(3, pick_tails_on_scalar(3, rounded3, 1), grouped3[:])
-        codes3 = held.tile([P, P], U32, name="tcodes3", align_bytes=64)
-        scales3 = held.tile([P, P], U8, name="tscales3", align_bytes=64)
-        nc.vector.quantize_mx(out=codes3[:].bitcast(E4M3X4), scales=scales3[:], in_=grouped3[:])
-        b3 = product(codes3[:], scales3[:], held.tile([P, QUERIES], F32, name="b3"))
-        h3 = pick(held.tile([P, QUERIES], F32, name="h_picked3"), heads[3], head_list)
+        b2 = product(quantise_tails(2, t_turned2, codes_tile(2)), floats("b2"))
+        h2 = pick(floats("h_picked2"), heads[2], head_list)
+        t_rounded3 = held.tile([P, ENTITIES], BF16, name="t_rounded3", align_bytes=64)
+        t_turned3 = turn_tails(pick_tails_on_scalar(3, t_rounded3, 1), turned_tile("t_turned3"))
+        b3 = product(quantise_tails(3, t_turned3, codes_tile(3)), floats("b3"))
+        h3 = pick(floats("h_picked3"), heads[3], head_list)
         put_heads(2, b2, r2)
         put_rels(2, b2, h2)
         put_heads(3, b3, r3)

@@ -24,6 +24,8 @@ QUERY_BLOCKS = QUERIES // P
 OUT_TILES = 2
 PICKED_BYTES = 4 * QUERIES
 TURNED_BYTES = 2 * SLOTS
+TABLE_BYTES = 4 * ENTITIES
+EARLY = QUERIES // 2
 
 FLOPS = 2 * FEATURES * QUERIES * SLOTS
 
@@ -34,20 +36,13 @@ def tile_attend_gdistm_hr_kernel(tc, hT, rT, G, tT, hoffs, roffs, offs, out_0, o
         lists = ctx.enter_context(tc.tile_pool(name="lists", bufs=1))
         held = ctx.enter_context(tc.tile_pool(name="held", bufs=1))
         shared = ctx.enter_context(tc.tile_pool(name="shared", bufs=1))
-        g_banks = ctx.enter_context(tc.psum_pool(name="g_banks", bufs=1))
-        block_banks = ctx.enter_context(tc.psum_pool(name="block_banks", bufs=2))
+        banks = ctx.enter_context(tc.psum_pool(name="banks", bufs=1))
 
         def placed(name, shape, dtype, offset):
             return shared.tile(shape, dtype, name=name, align_bytes=64, offset=offset)
 
-        def first_of(region):
-            return 2 * PICKED_BYTES * region
-
-        def second_of(region):
-            return first_of(region) + PICKED_BYTES
-
-        def across(region):
-            return second_of(region) - TURNED_BYTES // 2
+        def kept(name, shape, dtype, tag=None):
+            return held.tile(shape, dtype, name=name, tag=tag or name, align_bytes=64)
 
         def rows(k):
             return slice(k * P, (k + 1) * P)
@@ -56,138 +51,215 @@ def tile_attend_gdistm_hr_kernel(tc, hT, rT, G, tT, hoffs, roffs, offs, out_0, o
         head_list = lists.tile([P, QUERIES // 16], U16, name="head_list")
         rel_list = lists.tile([P, QUERIES // 16], U16, name="rel_list")
 
-        tails = [held.tile([P, ENTITIES], F32, name="tails%d" % k) for k in range(BLOCKS)]
-        heads = [held.tile([P, ENTITIES], F32, name="heads%d" % k) for k in range(BLOCKS)]
-        rels = [held.tile([P, RELATIONS], F32, name="rels%d" % k) for k in range(BLOCKS)]
-        grads = [held.tile([P, SLOTS], F32, name="grads%d" % a) for a in range(QUERY_BLOCKS)]
-        dh = [held.tile([P, ENTITIES], F32, name="dh0")]
-        dr = [held.tile([P, RELATIONS], F32, name="dr%d" % k) for k in range(OUT_TILES)]
-        ident = held.tile([P, P], F32, name="ident")
+        pieces = {1: (768, 768, 512), 2: (256, 256, 768, 768), 3: (1024, 1024)}
+        kib = 1024
+        tails0 = kept("tails0", [P, ENTITIES], F32)
+        tails = {(k, c): kept("tails%d_%d" % (k, c), [P, pieces[k][c]], F32)[:]
+                 for k, c in ((1, 0), (1, 1), (2, 0), (2, 1), (2, 2), (2, 3), (3, 0), (3, 1))}
+        tails[1, 2] = placed("tails1_2", [P, pieces[1][2]], F32, 27 * kib)[:]
 
-        half = ENTITIES // 2
-        for a in range(QUERY_BLOCKS):
+        def columns(k, c):
+            return slice(sum(pieces[k][:c]), sum(pieces[k][:c + 1]))
+
+        heads = [kept("heads%d" % k, [P, ENTITIES], F32) for k in range(BLOCKS)]
+        rels = [kept("rels%d" % k, [P, RELATIONS], F32) for k in range(BLOCKS)]
+        grads = [kept("grads%d" % a, [P, SLOTS], F32) for a in range(QUERY_BLOCKS)]
+        dh = [kept("dh0", [P, ENTITIES], F32)]
+        dr = [kept("dr%d" % k, [P, RELATIONS], F32) for k in range(OUT_TILES)]
+        ident = kept("ident", [P, P], F32)
+
+        def load_tails(k, which):
+            for c in which:
+                nc.sync.dma_start(tails[k, c], tT[rows(k), columns(k, c)])
+
+        for a in range(2):
             nc.sync.dma_start(grads[a][:], G[rows(a), :])
         nc.sync.dma_start(tail_list[:], offs)
-        nc.sync.dma_start(tails[0][:], tT[rows(0), :])
+        nc.sync.dma_start(tails0[:], tT[rows(0), :])
         nc.sync.dma_start(rel_list[:], roffs)
-        for k in range(BLOCKS - 1):
-            nc.sync.dma_start(rels[k][:], rT[rows(k), :])
+        nc.sync.dma_start(rels[0][:], rT[rows(0), :])
+        nc.sync.dma_start(rels[1][:], rT[rows(1), :])
+        nc.sync.dma_start(rels[2][:], rT[rows(2), :])
         nc.sync.dma_start(head_list[:], hoffs)
-        nc.sync.dma_start(tails[1][:, :half], tT[rows(1), :half])
-        nc.sync.dma_start(tails[1][:, half:], tT[rows(1), half:])
+        for a in range(2, 4):
+            nc.sync.dma_start(grads[a][:], G[rows(a), :])
         nc.sync.dma_start(heads[0][:], hT[rows(0), :])
-        nc.sync.dma_start(tails[2][:], tT[rows(2), :])
-        nc.sync.dma_start(heads[1][:], hT[rows(1), :])
+        load_tails(1, range(3))
         nc.sync.dma_start(rels[3][:], rT[rows(3), :])
-        nc.sync.dma_start(tails[3][:], tT[rows(3), :])
+        nc.sync.dma_start(heads[1][:], hT[rows(1), :])
+        load_tails(2, range(1))
         nc.sync.dma_start(heads[2][:], hT[rows(2), :])
+        load_tails(2, range(1, 4))
+        load_tails(3, range(2))
         nc.sync.dma_start(heads[3][:], hT[rows(3), :])
 
-        zeros = held.tile([P, P], F32, name="zeros", tag="dh1")
+        early_codes = placed("early_codes", [P, QUERIES], U32, 8 * kib)
+        early_scales = kept("early_scales", [P, QUERIES], U8)
+        g_codes = kept("g_codes", [P, QUERIES], U32)
+        g_scales = kept("g_scales", [P, QUERIES], U8)
+        zeros = kept("zeros", [P, P], F32, "dh1")
         nc.gpsimd.memset(zeros[:], 0.0)
         nc.gpsimd.affine_select(out=ident[:], in_=zeros[:], compare_op=mybir.AluOpType.not_equal, fill=1.0, base=0,
                                 pattern=[[-1, P]], channel_multiplier=1)
-        dh.append(held.tile([P, ENTITIES], F32, name="dh1", tag="dh1"))
+        dh.append(kept("dh1", [P, ENTITIES], F32))
         nc.gpsimd.memset(dh[1][:].bitcast(I32), 0)
+        nc.vector.memset(early_codes[:, EARLY:], 0)
+        nc.vector.memset(early_scales[:, EARLY:].bitcast(U32), 0)
         for window in dh[:1] + dr:
             nc.vector.memset(window[:].bitcast(I32), 0)
 
-        def turn(src, dst, bank):
+        def transpose_words(src, bank):
             words = src[:].bitcast(F32)
             for u in range(2):
                 nc.tensor.transpose(bank[:, u, :], words[:, u::2], ident[:])
-            nc.scalar.copy(dst[:].bitcast(F32).rearrange("p (x u) -> p x u", u=2), bank[:].rearrange("p u x -> p x u"))
+
+        def turn(src, dst, bank_tag):
+            return turn_in(src, dst, banks.tile([P, 2, P], F32, name="turn_bank", tag=bank_tag)[:])
+
+        def turn_in(src, dst, bank):
+            transpose_words(src, bank)
+            nc.scalar.copy(dst.bitcast(F32).rearrange("p (x u) -> p x u", u=2), bank.rearrange("p u x -> p x u"))
             return dst
 
-        def turn_tails(picked, turned):
-            bank = block_banks.tile([P, 2, P], F32, name="tails_bank")
-            return turn(picked, turned, bank)
+        def round_tails(k, rounded, which, calls=1):
+            for c in which:
+                width = pieces[k][c] // calls
+                for at in range(0, pieces[k][c], width):
+                    first = columns(k, c).start + at
+                    nc.scalar.activation(rounded[:, first:first + width], tails[k, c][:, at:at + width], COPY)
 
-        def pick_tails_on_scalar(k, rounded, pieces):
-            width = ENTITIES // pieces
-            for c in range(0, ENTITIES, width):
-                nc.scalar.activation(rounded[:, c:c + width], tails[k][:, c:c + width], COPY)
-            picked = held.tile([P, SLOTS], BF16, name="t_picked%d" % k, tag="t_picked%d" % k, align_bytes=64)
+        def pick_tails_on_scalar(rounded, picked):
             nc.scalar.activation(picked[:], rounded[:].indirect(tail_list[:]), COPY)
             return picked
 
+        def part(offsets, queries):
+            return offsets[:, queries.start // 16:queries.stop // 16]
+
         def pick(picked, table, offsets):
-            nc.vector.tensor_copy(picked[:], table[:].indirect(offsets[:]))
+            nc.vector.tensor_copy(picked, table[:].indirect(offsets))
             return picked
 
-        def floats(name):
-            return held.tile([P, QUERIES], F32, name=name)
-
-        def turned_tile(name):
-            return held.tile([P, 4 * P], BF16, name=name, align_bytes=64)
-
-        def codes_tile(k):
-            return held.tile([P, P], U32, name="t_codes%d" % k, align_bytes=64)
-
-        def quantise_tails(k, turned, codes):
-            scales = held.tile([P, P], U8, name="t_scales%d" % k, align_bytes=64)
-            nc.vector.quantize_mx(out=codes[:].bitcast(E4M3X4), scales=scales[:], in_=turned[:])
+        def quantise_tails(k, turned, calls=1):
+            codes = kept("t_codes%d" % k, [P, P], U32)
+            scales = kept("t_scales%d" % k, [P, P], U8)
+            width = P // calls
+            for c in range(0, P, width):
+                nc.vector.quantize_mx(out=codes[:, c:c + width].bitcast(E4M3X4), scales=scales[:, c:c + width],
+                                      in_=turned[:, 4 * c:4 * (c + width)])
             return codes, scales
 
-        def product(operand, b):
-            codes, scales = operand
-            acc = block_banks.tile([P, QUERIES], F32, name="acc")
-            nc.tensor.matmul_mx(out=acc[:], lhsT=codes[:].bitcast(E4M3X4), lhsT_scale=scales[:],
-                                rhs=g_codes[:].bitcast(E5M2X4), rhs_scale=g_scales[:], start=True, stop=True)
-            nc.scalar.copy(b[:], acc[:])
+        def quantise_grads(codes, scales, queries, turned):
+            nc.vector.quantize_mx(out=codes[:, queries].bitcast(E5M2X4), scales=scales[:, queries], in_=turned)
+
+        def product(operand, moving, bank_tag):
+            acc = banks.tile([P, QUERIES], F32, name="acc", tag=bank_tag)
+            nc.tensor.matmul_mx(out=acc[:], lhsT=operand[0][:].bitcast(E4M3X4), lhsT_scale=operand[1][:],
+                                rhs=moving[0][:].bitcast(E5M2X4), rhs_scale=moving[1][:], start=True, stop=True)
+            return acc
+
+        def leave(b, acc, queries):
+            nc.scalar.copy(b[:, queries], acc[:, queries])
             return b
 
-        def put_heads(k, b, r_picked):
-            nc.vector.tensor_tensor(dh[k % OUT_TILES][:].indirect(head_list[:]), b[:], r_picked[:], MULT)
-            nc.sync.dma_start(out_0[rows(k), :], dh[k % OUT_TILES][:])
+        def scatter_heads(k, b, r_picked, queries):
+            nc.vector.tensor_tensor(dh[k][:].indirect(part(head_list, queries)), b, r_picked, MULT)
 
-        def put_rels(k, b, h_picked):
-            nc.vector.tensor_tensor(dr[k % OUT_TILES][:].indirect(rel_list[:]), b[:], h_picked[:], MULT)
-            nc.sync.dma_start(out_1[rows(k), :], dr[k % OUT_TILES][:])
+        def scatter_rels(k, b, h_picked, queries):
+            nc.vector.tensor_tensor(dr[k][:].indirect(part(rel_list, queries)), b, h_picked, MULT)
 
-        g_codes = held.tile([P, QUERIES], U32, name="g_codes", align_bytes=64)
-        g_scales = held.tile([P, QUERIES], U8, name="g_scales", align_bytes=64)
-        for a in range(QUERY_BLOCKS):
-            g_rounded = held.tile([P, SLOTS], BF16, name="g_rounded%d" % a, align_bytes=64)
-            nc.scalar.activation(g_rounded[:], grads[a][:], COPY)
-            if a + 1 == QUERY_BLOCKS:
-                g_turned = placed("g_turned%d" % a, [P, 4 * P], BF16, across(1))
-            else:
-                g_turned = turned_tile("g_turned%d" % a)
-            bank = g_banks.tile([P, 2, P], F32, name="g_bank%d" % a)
-            turn(g_rounded, g_turned, bank)
-            nc.vector.quantize_mx(out=g_codes[:, rows(a)].bitcast(E5M2X4), scales=g_scales[:, rows(a)], in_=g_turned[:])
+        def put_heads(k, b, r_picked, queries):
+            scatter_heads(k, b, r_picked, queries)
+            nc.sync.dma_start(out_0[rows(k), :], dh[k][:])
 
-        t_picked0 = pick(placed("t_picked0", [P, SLOTS], BF16, second_of(1)), tails[0], tail_list)
-        t_turned0 = turn_tails(t_picked0, placed("t_turned0", [P, 4 * P], BF16, across(0)))
-        r0 = pick(placed("r_picked0", [P, QUERIES], F32, first_of(1)), rels[0], rel_list)
-        b0 = product(quantise_tails(0, t_turned0, placed("t_codes0", [P, P], U32, first_of(2))), floats("b0"))
-        r1 = pick(placed("r_picked1", [P, QUERIES], F32, first_of(0)), rels[1], rel_list)
-        r2 = pick(placed("r_picked2", [P, QUERIES], F32, second_of(0)), rels[2], rel_list)
-        put_heads(0, b0, r0)
-        h0 = pick(floats("h_picked0"), heads[0], head_list)
+        def put_rels(k, b, h_picked, queries):
+            scatter_rels(k, b, h_picked, queries)
+            nc.sync.dma_start(out_1[rows(k), :], dr[k][:])
 
-        t_rounded1 = placed("t_rounded1", [P, ENTITIES], BF16, first_of(2))
-        t_turned1 = turn_tails(pick_tails_on_scalar(1, t_rounded1, 2), turned_tile("t_turned1"))
-        t_rounded2 = held.tile([P, ENTITIES], BF16, name="t_rounded2", align_bytes=64)
-        t_picked2 = pick_tails_on_scalar(2, t_rounded2, 1)
-        t_turned2 = turn_tails(t_picked2, turned_tile("t_turned2"))
-        operand1 = quantise_tails(1, t_turned1, codes_tile(1))
-        put_rels(0, b0, h0)
+        def round_grads(a, rounded):
+            nc.scalar.activation(rounded[:], grads[a][:], COPY)
+            return rounded
 
-        b1 = product(operand1, held.tile([P, QUERIES], F32, name="b1", tag="t_picked2", align_bytes=64))
-        h1 = pick(floats("h_picked1"), heads[1], head_list)
-        r3 = pick(floats("r_picked3"), rels[3], rel_list)
-        put_heads(1, b1, r1)
-        put_rels(1, b1, h1)
+        early, late, every = slice(0, EARLY), slice(EARLY, QUERIES), slice(0, QUERIES)
+        first_moving, moving = (early_codes, early_scales), (g_codes, g_scales)
+        g_turned0 = turn(round_grads(0, kept("g_rounded0", [P, SLOTS], BF16)), kept("g_turned0", [P, 4 * P], BF16)[:], "g0")
+        for target in (first_moving, moving):
+            quantise_grads(target[0], target[1], rows(0), g_turned0)
+        g_turned1 = placed("g_turned1", [P, 4 * P], BF16, kib // 2)
+        turn(round_grads(1, kept("g_rounded1", [P, SLOTS], BF16)), g_turned1[:], "g1")
+        for target in (first_moving, moving):
+            quantise_grads(target[0], target[1], rows(1), g_turned1[:])
 
-        b2 = product(quantise_tails(2, t_turned2, codes_tile(2)), floats("b2"))
-        h2 = pick(floats("h_picked2"), heads[2], head_list)
-        t_rounded3 = held.tile([P, ENTITIES], BF16, name="t_rounded3", align_bytes=64)
-        t_turned3 = turn_tails(pick_tails_on_scalar(3, t_rounded3, 1), turned_tile("t_turned3"))
-        b3 = product(quantise_tails(3, t_turned3, codes_tile(3)), floats("b3"))
-        h3 = pick(floats("h_picked3"), heads[3], head_list)
-        put_heads(2, b2, r2)
-        put_rels(2, b2, h2)
-        put_heads(3, b3, r3)
-        put_rels(3, b3, h3)
+        t_picked0 = placed("t_picked0", [P, SLOTS], BF16, 0)
+        pick(t_picked0[:], tails0, tail_list[:])
+        trio = placed("trio", [P, 3 * QUERIES], F32, kib)
+        r0, r1, r2 = trio[:, :QUERIES], trio[:, QUERIES:2 * QUERIES], trio[:, 2 * QUERIES:]
+        t_turned0 = turn(t_picked0, trio[:, 2 * QUERIES - P:2 * QUERIES + P].bitcast(BF16), "t0")
+        pick(r0, rels[0], rel_list[:])
+        pick(r1[:, early], rels[1], part(rel_list, early))
+        operand0 = quantise_tails(0, t_turned0, 2)
+        acc_early = product(operand0, first_moving, "early")
+        b0 = leave(kept("b0", [P, QUERIES], F32), acc_early, early)
+        pick(r1[:, late], rels[1], part(rel_list, late))
+        pick(r2, rels[2], rel_list[:])
+        scatter_heads(0, b0[:, early], r0[:, early], early)
+
+        g_rounded2 = round_grads(2, placed("g_rounded2", [P, SLOTS], BF16, 8 * kib))
+        g_rounded3 = round_grads(3, placed("g_rounded3", [P, SLOTS], BF16, 9 * kib))
+        h0 = pick(kept("h_picked0", [P, QUERIES], F32, "grads3")[:], heads[0], head_list[:])
+        late_bank = banks.tile([P, 2, 2, P], F32, name="late_bank", tag="g0")
+        transpose_words(g_rounded2, late_bank[:, 0])
+        transpose_words(g_rounded3, late_bank[:, 1])
+        g_turned_late = kept("g_turned_late", [P, 8 * P], BF16)
+        nc.scalar.copy(g_turned_late[:].bitcast(F32).rearrange("p (a x u) -> p a x u", a=2, u=2),
+                       late_bank[:].rearrange("p a u x -> p a x u"))
+        quantise_grads(g_codes, g_scales, late, g_turned_late[:])
+        b0_early = placed("b0_early", [P, EARLY], F32, 8 * kib + kib // 2)
+        nc.scalar.copy(b0_early[:], acc_early[:, early])
+        acc_late = product(operand0, moving, "late")
+        leave(b0, acc_late, late)
+        scatter_rels(0, b0_early[:], h0[:, early], early)
+        put_heads(0, b0[:, late], r0[:, late], late)
+
+        t_rounded1 = placed("t_rounded1", [P, ENTITIES], BF16, 9 * kib + kib // 2)
+        round_tails(1, t_rounded1, range(3))
+        t_picked1 = pick_tails_on_scalar(t_rounded1, kept("t_picked1", [P, SLOTS], BF16))
+        r3 = pick(placed("r_picked3", [P, QUERIES], F32, 26 * kib)[:], rels[3], rel_list[:])
+        h1 = pick(placed("h_picked1", [P, QUERIES], F32, 28 * kib)[:], heads[1], head_list[:])
+        t_rounded2 = placed("t_rounded2", [P, ENTITIES], BF16, 16 * kib)
+        round_tails(2, t_rounded2, range(1))
+        t_turned1 = turn_in(t_picked1, kept("t_turned1", [P, 4 * P], BF16, "tails2_0")[:],
+                            acc_late[:, early].rearrange("p (u x) -> p u x", u=2))
+        operand1 = quantise_tails(1, t_turned1)
+        b0_late = kept("b0_late", [P, QUERIES - EARLY], F32)
+        nc.scalar.copy(b0_late[:], acc_late[:, late])
+        put_rels(0, b0_late[:], h0[:, late], late)
+        acc1 = product(operand1, moving, "b1")
+        round_tails(2, t_rounded2, range(1, 2))
+        b1 = leave(kept("b1", [P, QUERIES], F32, "tails2_1"), acc1, every)
+        h2 = pick(kept("h_picked2", [P, QUERIES], F32, "tails2_0")[:], heads[2], head_list[:])
+        round_tails(2, t_rounded2, range(2, 4))
+        put_heads(1, b1[:], r1, every)
+        dh.append(kept("dh2", [P, ENTITIES], F32, "heads2"))
+        nc.gpsimd.memset(dh[2][:].bitcast(I32), 0)
+        dh.append(dh[1])
+        dr.extend(dr[:2])
+        scatter_rels(1, b1[:, early], h1[:, early], early)
+
+        t_picked2 = pick_tails_on_scalar(t_rounded2, kept("t_picked2", [P, SLOTS], BF16))
+        t_turned2 = turn_in(t_picked2, kept("t_turned2", [P, 4 * P], BF16)[:],
+                            acc1[:, early].rearrange("p (u x) -> p u x", u=2))
+        operand2 = quantise_tails(2, t_turned2)
+        b1_late = kept("b1_late", [P, QUERIES - EARLY], F32)
+        nc.scalar.copy(b1_late[:], acc1[:, late])
+        put_rels(1, b1_late[:], h1[:, late], late)
+        b2 = leave(kept("b2", [P, QUERIES], F32), product(operand2, moving, "b2"), every)
+        t_rounded3 = placed("t_rounded3", [P, ENTITIES], BF16, 16 * kib)
+        round_tails(3, t_rounded3, range(2))
+        h3 = pick(kept("h_picked3", [P, QUERIES], F32, "tails3_0")[:], heads[3], head_list[:])
+        t_picked3 = pick_tails_on_scalar(t_rounded3, kept("t_picked3", [P, SLOTS], BF16))
+        put_heads(2, b2[:], r2, every)
+        operand3 = quantise_tails(3, turn(t_picked3, kept("t_turned3", [P, 4 * P], BF16)[:], "t0"))
+        b3 = leave(kept("b3", [P, QUERIES], F32), product(operand3, moving, "early"), every)
+        put_rels(2, b2[:], h2, every)
+        put_heads(3, b3[:], r3, every)
+        put_rels(3, b3[:], h3, every)

@@ -51,7 +51,7 @@ def tile_attend_gdistm_hr_kernel(tc, hT, rT, G, tT, hoffs, roffs, offs, out_0, o
         head_list = lists.tile([P, QUERIES // 16], U16, name="head_list")
         rel_list = lists.tile([P, QUERIES // 16], U16, name="rel_list")
 
-        pieces = {1: (768, 768, 512), 2: (256, 256, 768, 768), 3: (1024, 1024)}
+        pieces = {1: (768, 768, 512), 2: (256, 512, 256, 1024), 3: (1024, 1024)}
         kib = 1024
         tails0 = kept("tails0", [P, ENTITIES], F32)
         tails = {(k, c): kept("tails%d_%d" % (k, c), [P, pieces[k][c]], F32)[:]
@@ -85,11 +85,11 @@ def tile_attend_gdistm_hr_kernel(tc, hT, rT, G, tT, hoffs, roffs, offs, out_0, o
             nc.sync.dma_start(grads[a][:], G[rows(a), :])
         nc.sync.dma_start(heads[0][:], hT[rows(0), :])
         load_tails(1, range(3))
-        nc.sync.dma_start(rels[3][:], rT[rows(3), :])
         nc.sync.dma_start(heads[1][:], hT[rows(1), :])
-        load_tails(2, range(1))
+        load_tails(2, range(2))
+        nc.sync.dma_start(rels[3][:], rT[rows(3), :])
         nc.sync.dma_start(heads[2][:], hT[rows(2), :])
-        load_tails(2, range(1, 4))
+        load_tails(2, range(2, 4))
         load_tails(3, range(2))
         nc.sync.dma_start(heads[3][:], hT[rows(3), :])
 
@@ -219,25 +219,21 @@ def tile_attend_gdistm_hr_kernel(tc, hT, rT, G, tT, hoffs, roffs, offs, out_0, o
         leave(b0, acc_late, late)
         scatter_rels(0, b0_early[:], h0[:, early], early)
         put_heads(0, b0[:, late], r0[:, late], late)
+        put_rels(0, b0[:, late], h0[:, late], late)
 
         t_rounded1 = placed("t_rounded1", [P, ENTITIES], BF16, 9 * kib + kib // 2)
         round_tails(1, t_rounded1, range(3))
         t_picked1 = pick_tails_on_scalar(t_rounded1, kept("t_picked1", [P, SLOTS], BF16))
-        r3 = pick(placed("r_picked3", [P, QUERIES], F32, 26 * kib)[:], rels[3], rel_list[:])
         h1 = pick(placed("h_picked1", [P, QUERIES], F32, 28 * kib)[:], heads[1], head_list[:])
         t_rounded2 = placed("t_rounded2", [P, ENTITIES], BF16, 16 * kib)
         round_tails(2, t_rounded2, range(1))
-        t_turned1 = turn_in(t_picked1, kept("t_turned1", [P, 4 * P], BF16, "tails2_0")[:],
-                            acc_late[:, early].rearrange("p (u x) -> p u x", u=2))
-        operand1 = quantise_tails(1, t_turned1)
-        b0_late = kept("b0_late", [P, QUERIES - EARLY], F32)
-        nc.scalar.copy(b0_late[:], acc_late[:, late])
-        put_rels(0, b0_late[:], h0[:, late], late)
+        operand1 = quantise_tails(1, turn(t_picked1, kept("t_turned1", [P, 4 * P], BF16, "tails2_0")[:], "t1"))
         acc1 = product(operand1, moving, "b1")
-        round_tails(2, t_rounded2, range(1, 2))
-        b1 = leave(kept("b1", [P, QUERIES], F32, "tails2_1"), acc1, every)
-        h2 = pick(kept("h_picked2", [P, QUERIES], F32, "tails2_0")[:], heads[2], head_list[:])
-        round_tails(2, t_rounded2, range(2, 4))
+        round_tails(2, t_rounded2, range(1, 3))
+        b1 = leave(kept("b1", [P, QUERIES], F32, "tails2_2"), acc1, every)
+        r3 = pick(kept("r_picked3", [P, QUERIES], F32)[:], rels[3], rel_list[:])
+        h2 = pick(kept("h_picked2", [P, QUERIES], F32)[:], heads[2], head_list[:])
+        round_tails(2, t_rounded2, range(3, 4))
         put_heads(1, b1[:], r1, every)
         dh.append(kept("dh2", [P, ENTITIES], F32, "heads2"))
         nc.gpsimd.memset(dh[2][:].bitcast(I32), 0)

@@ -51,19 +51,20 @@ def tile_attend_gdistm_hr_kernel(tc, hT, rT, G, tT, hoffs, roffs, offs, out_0, o
         head_list = lists.tile([P, QUERIES // 16], U16, name="head_list")
         rel_list = lists.tile([P, QUERIES // 16], U16, name="rel_list")
 
-        pieces = {1: (768, 768, 512), 2: (256, 512, 256, 1024), 3: (1024, 1024)}
+        pieces = {1: (896, 1152), 2: (256, 256, 768, 768), 3: (1024, 1024)}
         kib = 1024
         tails0 = kept("tails0", [P, ENTITIES], F32)
         tails = {(k, c): kept("tails%d_%d" % (k, c), [P, pieces[k][c]], F32)[:]
-                 for k, c in ((1, 0), (1, 1), (2, 0), (2, 1), (2, 2), (2, 3), (3, 0), (3, 1))}
-        tails[1, 2] = placed("tails1_2", [P, pieces[1][2]], F32, 27 * kib)[:]
+                 for k, c in ((1, 0), (2, 0), (2, 1), (2, 2), (2, 3), (3, 0), (3, 1))}
+        tails[1, 1] = placed("tails1_1", [P, pieces[1][1]], F32, 26 * kib)[:]
 
         def columns(k, c):
             return slice(sum(pieces[k][:c]), sum(pieces[k][:c + 1]))
 
         heads = [kept("heads%d" % k, [P, ENTITIES], F32) for k in range(BLOCKS)]
         rels = [kept("rels%d" % k, [P, RELATIONS], F32) for k in range(BLOCKS)]
-        grads = [kept("grads%d" % a, [P, SLOTS], F32) for a in range(QUERY_BLOCKS)]
+        grads = [kept("grads%d" % a, [P, SLOTS], F32) for a in range(2)]
+        late_grads = kept("late_grads", [P, 2, SLOTS], F32)
         dh = [kept("dh0", [P, ENTITIES], F32)]
         dr = [kept("dr%d" % k, [P, RELATIONS], F32) for k in range(OUT_TILES)]
         ident = kept("ident", [P, P], F32)
@@ -81,15 +82,14 @@ def tile_attend_gdistm_hr_kernel(tc, hT, rT, G, tT, hoffs, roffs, offs, out_0, o
         nc.sync.dma_start(rels[1][:], rT[rows(1), :])
         nc.sync.dma_start(rels[2][:], rT[rows(2), :])
         nc.sync.dma_start(head_list[:], hoffs)
-        for a in range(2, 4):
-            nc.sync.dma_start(grads[a][:], G[rows(a), :])
+        nc.sync.dma_start(late_grads[:], G[EARLY:, :].rearrange("(p e) i -> p e i", e=2))
         nc.sync.dma_start(heads[0][:], hT[rows(0), :])
-        load_tails(1, range(3))
+        load_tails(1, range(2))
         nc.sync.dma_start(heads[1][:], hT[rows(1), :])
-        load_tails(2, range(2))
-        nc.sync.dma_start(rels[3][:], rT[rows(3), :])
+        load_tails(2, range(1))
         nc.sync.dma_start(heads[2][:], hT[rows(2), :])
-        load_tails(2, range(2, 4))
+        nc.sync.dma_start(rels[3][:], rT[rows(3), :])
+        load_tails(2, range(1, 4))
         load_tails(3, range(2))
         nc.sync.dma_start(heads[3][:], hT[rows(3), :])
 
@@ -198,44 +198,48 @@ def tile_attend_gdistm_hr_kernel(tc, hT, rT, G, tT, hoffs, roffs, offs, out_0, o
         pick(r1[:, early], rels[1], part(rel_list, early))
         operand0 = quantise_tails(0, t_turned0, 2)
         acc_early = product(operand0, first_moving, "early")
-        b0 = leave(kept("b0", [P, QUERIES], F32), acc_early, early)
+        b0 = leave(kept("b0", [P, EARLY], F32), acc_early, early)
         pick(r1[:, late], rels[1], part(rel_list, late))
         pick(r2, rels[2], rel_list[:])
         scatter_heads(0, b0[:, early], r0[:, early], early)
 
-        g_rounded2 = round_grads(2, placed("g_rounded2", [P, SLOTS], BF16, 8 * kib))
-        g_rounded3 = round_grads(3, placed("g_rounded3", [P, SLOTS], BF16, 9 * kib))
-        h0 = pick(kept("h_picked0", [P, QUERIES], F32, "grads3")[:], heads[0], head_list[:])
+        g_rounded2 = placed("g_rounded2", [P, SLOTS], BF16, 8 * kib)
+        g_rounded3 = placed("g_rounded3", [P, SLOTS], BF16, 9 * kib)
+        nc.scalar.activation(g_rounded2[:], late_grads[:, 0, :], COPY)
+        nc.scalar.activation(g_rounded3[:], late_grads[:, 1, :], COPY)
+        h0 = pick(kept("h_picked0", [P, QUERIES], F32, "late_grads")[:], heads[0], head_list[:])
         late_bank = banks.tile([P, 2, 2, P], F32, name="late_bank", tag="g0")
         transpose_words(g_rounded2, late_bank[:, 0])
         transpose_words(g_rounded3, late_bank[:, 1])
         g_turned_late = kept("g_turned_late", [P, 8 * P], BF16)
-        nc.scalar.copy(g_turned_late[:].bitcast(F32).rearrange("p (a x u) -> p a x u", a=2, u=2),
-                       late_bank[:].rearrange("p a u x -> p a x u"))
+        nc.scalar.copy(g_turned_late[:].bitcast(F32).rearrange("p (x e u) -> p x e u", e=2, u=2),
+                       late_bank[:].rearrange("p e u x -> p x e u"))
         quantise_grads(g_codes, g_scales, late, g_turned_late[:])
         b0_early = placed("b0_early", [P, EARLY], F32, 8 * kib + kib // 2)
         nc.scalar.copy(b0_early[:], acc_early[:, early])
         acc_late = product(operand0, moving, "late")
-        leave(b0, acc_late, late)
-        scatter_rels(0, b0_early[:], h0[:, early], early)
-        put_heads(0, b0[:, late], r0[:, late], late)
-        put_rels(0, b0[:, late], h0[:, late], late)
-
         t_rounded1 = placed("t_rounded1", [P, ENTITIES], BF16, 9 * kib + kib // 2)
-        round_tails(1, t_rounded1, range(3))
+        round_tails(1, t_rounded1, range(1))
+        b0_late = kept("b0_late", [P, QUERIES - EARLY], F32, "tails1_0")
+        nc.scalar.copy(b0_late[:], acc_late[:, late])
+        scatter_rels(0, b0_early[:], h0[:, early], early)
+        put_heads(0, b0_late[:], r0[:, late], late)
+        put_rels(0, b0_late[:], h0[:, late], late)
+
+        round_tails(1, t_rounded1, range(1, 2))
         t_picked1 = pick_tails_on_scalar(t_rounded1, kept("t_picked1", [P, SLOTS], BF16))
         h1 = pick(placed("h_picked1", [P, QUERIES], F32, 28 * kib)[:], heads[1], head_list[:])
         t_rounded2 = placed("t_rounded2", [P, ENTITIES], BF16, 16 * kib)
         round_tails(2, t_rounded2, range(1))
         operand1 = quantise_tails(1, turn(t_picked1, kept("t_turned1", [P, 4 * P], BF16, "tails2_0")[:], "t1"))
         acc1 = product(operand1, moving, "b1")
-        round_tails(2, t_rounded2, range(1, 3))
-        b1 = leave(kept("b1", [P, QUERIES], F32, "tails2_2"), acc1, every)
-        r3 = pick(kept("r_picked3", [P, QUERIES], F32)[:], rels[3], rel_list[:])
+        round_tails(2, t_rounded2, range(1, 2))
+        b1 = leave(kept("b1", [P, QUERIES], F32, "tails2_1"), acc1, every)
         h2 = pick(kept("h_picked2", [P, QUERIES], F32)[:], heads[2], head_list[:])
-        round_tails(2, t_rounded2, range(3, 4))
+        r3 = pick(kept("r_picked3", [P, QUERIES], F32)[:], rels[3], rel_list[:])
+        round_tails(2, t_rounded2, range(2, 4))
         put_heads(1, b1[:], r1, every)
-        dh.append(kept("dh2", [P, ENTITIES], F32, "heads2"))
+        dh.append(kept("dh2", [P, ENTITIES], F32, "rels3"))
         nc.gpsimd.memset(dh[2][:].bitcast(I32), 0)
         dh.append(dh[1])
         dr.extend(dr[:2])

@@ -88,8 +88,9 @@ def tile_attend_gdistm_hr_kernel(tc, hT, rT, G, tT, hoffs, roffs, offs, out_0, o
         nc.sync.dma_start(heads[1][:], hT[rows(1), :])
         load_tails(2, range(1))
         nc.sync.dma_start(heads[2][:], hT[rows(2), :])
+        load_tails(2, range(1, 2))
         nc.sync.dma_start(rels[3][:], rT[rows(3), :])
-        load_tails(2, range(1, 4))
+        load_tails(2, range(2, 4))
         load_tails(3, range(2))
         nc.sync.dma_start(heads[3][:], hT[rows(3), :])
 
@@ -243,15 +244,16 @@ def tile_attend_gdistm_hr_kernel(tc, hT, rT, G, tT, hoffs, roffs, offs, out_0, o
         nc.gpsimd.memset(dh[2][:].bitcast(I32), 0)
         dh.append(dh[1])
         dr.extend(dr[:2])
-        scatter_rels(1, b1[:, early], h1[:, early], early)
+        before, behind = slice(0, 320), slice(320, QUERIES)
+        scatter_rels(1, b1[:, before], h1[:, before], before)
 
         t_picked2 = pick_tails_on_scalar(t_rounded2, kept("t_picked2", [P, SLOTS], BF16))
         t_turned2 = turn_in(t_picked2, kept("t_turned2", [P, 4 * P], BF16)[:],
                             acc1[:, early].rearrange("p (u x) -> p u x", u=2))
         operand2 = quantise_tails(2, t_turned2)
-        b1_late = kept("b1_late", [P, QUERIES - EARLY], F32)
-        nc.scalar.copy(b1_late[:], acc1[:, late])
-        put_rels(1, b1_late[:], h1[:, late], late)
+        b1_late = kept("b1_late", [P, QUERIES - 320], F32)
+        nc.scalar.copy(b1_late[:], acc1[:, behind])
+        put_rels(1, b1_late[:], h1[:, behind], behind)
         b2 = leave(kept("b2", [P, QUERIES], F32), product(operand2, moving, "b2"), every)
         t_rounded3 = placed("t_rounded3", [P, ENTITIES], BF16, 16 * kib)
         round_tails(3, t_rounded3, range(2))

@@ -63,7 +63,7 @@ def tile_attend_gdistm_hr_kernel(tc, hT, rT, G, tT, hoffs, roffs, offs, out_0, o
 
         heads = [kept("heads%d" % k, [P, ENTITIES], F32) for k in range(BLOCKS)]
         rels = [kept("rels%d" % k, [P, RELATIONS], F32) for k in range(BLOCKS)]
-        grads = [kept("grads%d" % a, [P, SLOTS], F32) for a in range(2)]
+        early_grads = kept("early_grads", [P, 2, SLOTS], F32)
         late_grads = kept("late_grads", [P, 2, SLOTS], F32)
         dh = [kept("dh0", [P, ENTITIES], F32)]
         dr = [kept("dr%d" % k, [P, RELATIONS], F32) for k in range(OUT_TILES)]
@@ -73,10 +73,9 @@ def tile_attend_gdistm_hr_kernel(tc, hT, rT, G, tT, hoffs, roffs, offs, out_0, o
             for c in which:
                 nc.sync.dma_start(tails[k, c], tT[rows(k), columns(k, c)])
 
-        for a in range(2):
-            nc.sync.dma_start(grads[a][:], G[rows(a), :])
         nc.sync.dma_start(tail_list[:], offs)
         nc.sync.dma_start(tails0[:], tT[rows(0), :])
+        nc.sync.dma_start(early_grads[:], G[:EARLY, :].rearrange("(p e) i -> p e i", e=2))
         nc.sync.dma_start(rel_list[:], roffs)
         nc.sync.dma_start(rels[0][:], rT[rows(0), :])
         nc.sync.dma_start(rels[1][:], rT[rows(1), :])
@@ -94,8 +93,6 @@ def tile_attend_gdistm_hr_kernel(tc, hT, rT, G, tT, hoffs, roffs, offs, out_0, o
         load_tails(3, range(2))
         nc.sync.dma_start(heads[3][:], hT[rows(3), :])
 
-        early_codes = placed("early_codes", [P, QUERIES], U32, 8 * kib)
-        early_scales = kept("early_scales", [P, QUERIES], U8)
         g_codes = kept("g_codes", [P, QUERIES], U32)
         g_scales = kept("g_scales", [P, QUERIES], U8)
         zeros = kept("zeros", [P, P], F32, "dh1")
@@ -104,8 +101,8 @@ def tile_attend_gdistm_hr_kernel(tc, hT, rT, G, tT, hoffs, roffs, offs, out_0, o
                                 pattern=[[-1, P]], channel_multiplier=1)
         dh.append(kept("dh1", [P, ENTITIES], F32))
         nc.gpsimd.memset(dh[1][:].bitcast(I32), 0)
-        nc.vector.memset(early_codes[:, EARLY:], 0)
-        nc.vector.memset(early_scales[:, EARLY:].bitcast(U32), 0)
+        nc.vector.memset(g_codes[:, EARLY:], 0)
+        nc.vector.memset(g_scales[:, EARLY:].bitcast(U32), 0)
         for window in dh[:1] + dr:
             nc.vector.memset(window[:].bitcast(I32), 0)
 
@@ -176,29 +173,32 @@ def tile_attend_gdistm_hr_kernel(tc, hT, rT, G, tT, hoffs, roffs, offs, out_0, o
             scatter_rels(k, b, h_picked, queries)
             nc.sync.dma_start(out_1[rows(k), :], dr[k][:])
 
-        def round_grads(a, rounded):
-            nc.scalar.activation(rounded[:], grads[a][:], COPY)
-            return rounded
-
         early, late, every = slice(0, EARLY), slice(EARLY, QUERIES), slice(0, QUERIES)
-        first_moving, moving = (early_codes, early_scales), (g_codes, g_scales)
-        g_turned0 = turn(round_grads(0, kept("g_rounded0", [P, SLOTS], BF16)), kept("g_turned0", [P, 4 * P], BF16)[:], "g0")
-        for target in (first_moving, moving):
-            quantise_grads(target[0], target[1], rows(0), g_turned0)
-        g_turned1 = placed("g_turned1", [P, 4 * P], BF16, kib // 2)
-        turn(round_grads(1, kept("g_rounded1", [P, SLOTS], BF16)), g_turned1[:], "g1")
-        for target in (first_moving, moving):
-            quantise_grads(target[0], target[1], rows(1), g_turned1[:])
+        moving = (g_codes, g_scales)
 
-        t_picked0 = placed("t_picked0", [P, SLOTS], BF16, 0)
+        def turn_pair(rounded, dst, bank_tag):
+            bank = banks.tile([P, 2, 2, P], F32, name="pair_bank", tag=bank_tag)
+            for e in range(2):
+                transpose_words(rounded[e], bank[:, e])
+            nc.scalar.copy(dst.bitcast(F32).rearrange("p (x e u) -> p x e u", e=2, u=2),
+                           bank[:].rearrange("p e u x -> p x e u"))
+
+        t_picked0 = kept("t_picked0", [P, SLOTS], BF16)
         pick(t_picked0[:], tails0, tail_list[:])
-        trio = placed("trio", [P, 3 * QUERIES], F32, kib)
+        t_turned0 = turn(t_picked0, kept("t_turned0", [P, 4 * P], BF16)[:], "t0")
+        early_rounded = [kept("g_rounded%d" % e, [P, SLOTS], BF16) for e in range(2)]
+        for e in range(2):
+            nc.vector.tensor_copy(early_rounded[e][:], early_grads[:, e, :])
+        trio = kept("trio", [P, 3 * QUERIES], F32)
         r0, r1, r2 = trio[:, :QUERIES], trio[:, QUERIES:2 * QUERIES], trio[:, 2 * QUERIES:]
-        t_turned0 = turn(t_picked0, trio[:, 2 * QUERIES - P:2 * QUERIES + P].bitcast(BF16), "t0")
+        g_turned_early = trio[:, 2 * QUERIES - EARLY:2 * QUERIES + EARLY].bitcast(BF16)
+        turn_pair(early_rounded, g_turned_early, "g1")
         pick(r0, rels[0], rel_list[:])
+        operand0 = quantise_tails(0, t_turned0)
         pick(r1[:, early], rels[1], part(rel_list, early))
-        operand0 = quantise_tails(0, t_turned0, 2)
-        acc_early = product(operand0, first_moving, "early")
+        for a in range(2):
+            quantise_grads(g_codes, g_scales, rows(a), g_turned_early[:, a * SLOTS:(a + 1) * SLOTS])
+        acc_early = product(operand0, moving, "early")
         b0 = leave(kept("b0", [P, EARLY], F32), acc_early, early)
         pick(r1[:, late], rels[1], part(rel_list, late))
         pick(r2, rels[2], rel_list[:])
@@ -209,12 +209,8 @@ def tile_attend_gdistm_hr_kernel(tc, hT, rT, G, tT, hoffs, roffs, offs, out_0, o
         nc.scalar.activation(g_rounded2[:], late_grads[:, 0, :], COPY)
         nc.scalar.activation(g_rounded3[:], late_grads[:, 1, :], COPY)
         h0 = pick(kept("h_picked0", [P, QUERIES], F32, "late_grads")[:], heads[0], head_list[:])
-        late_bank = banks.tile([P, 2, 2, P], F32, name="late_bank", tag="g0")
-        transpose_words(g_rounded2, late_bank[:, 0])
-        transpose_words(g_rounded3, late_bank[:, 1])
         g_turned_late = kept("g_turned_late", [P, 8 * P], BF16)
-        nc.scalar.copy(g_turned_late[:].bitcast(F32).rearrange("p (x e u) -> p x e u", e=2, u=2),
-                       late_bank[:].rearrange("p e u x -> p x e u"))
+        turn_pair([g_rounded2, g_rounded3], g_turned_late[:], "g0")
         quantise_grads(g_codes, g_scales, late, g_turned_late[:])
         b0_early = placed("b0_early", [P, EARLY], F32, 8 * kib + kib // 2)
         nc.scalar.copy(b0_early[:], acc_early[:, early])

@@ -73,8 +73,8 @@ def tile_attend_gdistm_hr_kernel(tc, hT, rT, G, tT, hoffs, roffs, offs, out_0, o
             for c in which:
                 nc.sync.dma_start(tails[k, c], tT[rows(k), columns(k, c)])
 
-        nc.sync.dma_start(tail_list[:], offs)
         nc.sync.dma_start(tails0[:], tT[rows(0), :])
+        nc.sync.dma_start(tail_list[:], offs)
         nc.sync.dma_start(early_grads[:], G[:EARLY, :].rearrange("(p e) i -> p e i", e=2))
         nc.sync.dma_start(rel_list[:], roffs)
         nc.sync.dma_start(rels[0][:], rT[rows(0), :])

@@ -20,12 +20,7 @@ SLOTS = 512
 ENTITIES = 2048
 RELATIONS = 1024
 BLOCKS = FEATURES // P
-QUERY_BLOCKS = QUERIES // P
-OUT_TILES = 2
-PICKED_BYTES = 4 * QUERIES
-TURNED_BYTES = 2 * SLOTS
-TABLE_BYTES = 4 * ENTITIES
-EARLY = QUERIES // 2
+HALF = QUERIES // 2
 
 FLOPS = 2 * FEATURES * QUERIES * SLOTS
 
@@ -38,226 +33,135 @@ def tile_attend_gdistm_hr_kernel(tc, hT, rT, G, tT, hoffs, roffs, offs, out_0, o
         shared = ctx.enter_context(tc.tile_pool(name="shared", bufs=1))
         banks = ctx.enter_context(tc.psum_pool(name="banks", bufs=1))
 
-        def placed(name, shape, dtype, offset):
-            return shared.tile(shape, dtype, name=name, align_bytes=64, offset=offset)
+        def kept(name, shape, dtype):
+            return held.tile(shape, dtype, name=name, align_bytes=64)
 
-        def kept(name, shape, dtype, tag=None):
-            return held.tile(shape, dtype, name=name, tag=tag or name, align_bytes=64)
+        def placed(name, shape, dtype, kib):
+            return shared.tile(shape, dtype, name=name, align_bytes=64, offset=int(1024 * kib))
 
-        def rows(k):
-            return slice(k * P, (k + 1) * P)
+        def dealt(table):
+            return table.rearrange("(p k) c -> p k c", k=BLOCKS)
 
         tail_list = lists.tile([P, SLOTS // 16], U16, name="tail_list")
         head_list = lists.tile([P, QUERIES // 16], U16, name="head_list")
         rel_list = lists.tile([P, QUERIES // 16], U16, name="rel_list")
 
-        pieces = {1: (896, 1152), 2: (256, 256, 768, 768), 3: (1024, 1024)}
-        kib = 1024
-        tails0 = kept("tails0", [P, ENTITIES], F32)
-        tails = {(k, c): kept("tails%d_%d" % (k, c), [P, pieces[k][c]], F32)[:]
-                 for k, c in ((1, 0), (2, 0), (2, 1), (2, 2), (2, 3), (3, 0), (3, 1))}
-        tails[1, 1] = placed("tails1_1", [P, pieces[1][1]], F32, 26 * kib)[:]
-
-        def columns(k, c):
-            return slice(sum(pieces[k][:c]), sum(pieces[k][:c + 1]))
-
-        heads = [kept("heads%d" % k, [P, ENTITIES], F32) for k in range(BLOCKS)]
-        rels = [kept("rels%d" % k, [P, RELATIONS], F32) for k in range(BLOCKS)]
-        early_grads = kept("early_grads", [P, 2, SLOTS], F32)
-        late_grads = kept("late_grads", [P, 2, SLOTS], F32)
-        dh = [kept("dh0", [P, ENTITIES], F32)]
-        dr = [kept("dr%d" % k, [P, RELATIONS], F32) for k in range(OUT_TILES)]
+        tails = [kept("tails%d" % k, [P, ENTITIES], F32) for k in range(BLOCKS)]
+        head_pairs = [kept("heads%d" % j, [P, 2, ENTITIES], F32) for j in range(BLOCKS // 2)]
+        rel_pairs = [kept("rels%d" % j, [P, 2, RELATIONS], F32) for j in range(BLOCKS // 2)]
+        grads = kept("grads", [P, 4, SLOTS], F32)
         ident = kept("ident", [P, P], F32)
+        zeros = kept("zeros", [P, P], F32)
 
-        def load_tails(k, which):
-            for c in which:
-                nc.sync.dma_start(tails[k, c], tT[rows(k), columns(k, c)])
-
-        nc.sync.dma_start(tails0[:], tT[rows(0), :])
+        nc.sync.dma_start(tails[0][:], dealt(tT)[:, 0, :])
         nc.sync.dma_start(tail_list[:], offs)
-        nc.sync.dma_start(early_grads[:], G[:EARLY, :].rearrange("(p e) i -> p e i", e=2))
+        nc.sync.dma_start(grads[:], G.rearrange("(p e) i -> p e i", e=4))
+        nc.sync.dma_start(tails[1][:], dealt(tT)[:, 1, :])
         nc.sync.dma_start(rel_list[:], roffs)
-        nc.sync.dma_start(rels[0][:], rT[rows(0), :])
-        nc.sync.dma_start(rels[1][:], rT[rows(1), :])
-        nc.sync.dma_start(rels[2][:], rT[rows(2), :])
         nc.sync.dma_start(head_list[:], hoffs)
-        nc.sync.dma_start(late_grads[:], G[EARLY:, :].rearrange("(p e) i -> p e i", e=2))
-        nc.sync.dma_start(heads[0][:], hT[rows(0), :])
-        load_tails(1, range(2))
-        nc.sync.dma_start(heads[1][:], hT[rows(1), :])
-        load_tails(2, range(1))
-        nc.sync.dma_start(heads[2][:], hT[rows(2), :])
-        load_tails(2, range(1, 2))
-        nc.sync.dma_start(rels[3][:], rT[rows(3), :])
-        load_tails(2, range(2, 4))
-        load_tails(3, range(2))
-        nc.sync.dma_start(heads[3][:], hT[rows(3), :])
+        nc.sync.dma_start(rel_pairs[0][:], dealt(rT)[:, 0:2, :])
+        nc.sync.dma_start(tails[2][:], dealt(tT)[:, 2, :])
+        nc.sync.dma_start(tails[3][:], dealt(tT)[:, 3, :])
+        nc.sync.dma_start(rel_pairs[1][:], dealt(rT)[:, 2:4, :])
+        nc.sync.dma_start(head_pairs[0][:], dealt(hT)[:, 0:2, :])
+        nc.sync.dma_start(head_pairs[1][:], dealt(hT)[:, 2:4, :])
 
-        g_codes = kept("g_codes", [P, QUERIES], U32)
-        g_scales = kept("g_scales", [P, QUERIES], U8)
-        zeros = kept("zeros", [P, P], F32, "dh1")
         nc.gpsimd.memset(zeros[:], 0.0)
         nc.gpsimd.affine_select(out=ident[:], in_=zeros[:], compare_op=mybir.AluOpType.not_equal, fill=1.0, base=0,
                                 pattern=[[-1, P]], channel_multiplier=1)
-        dh.append(kept("dh1", [P, ENTITIES], F32))
-        nc.gpsimd.memset(dh[1][:].bitcast(I32), 0)
-        nc.vector.memset(g_codes[:, EARLY:], 0)
-        nc.vector.memset(g_scales[:, EARLY:].bitcast(U32), 0)
-        for window in dh[:1] + dr:
-            nc.vector.memset(window[:].bitcast(I32), 0)
 
         def transpose_words(src, bank):
-            words = src[:].bitcast(F32)
+            words = src.bitcast(F32)
             for u in range(2):
                 nc.tensor.transpose(bank[:, u, :], words[:, u::2], ident[:])
 
-        def turn(src, dst, bank_tag):
-            return turn_in(src, dst, banks.tile([P, 2, P], F32, name="turn_bank", tag=bank_tag)[:])
-
-        def turn_in(src, dst, bank):
-            transpose_words(src, bank)
-            nc.scalar.copy(dst.bitcast(F32).rearrange("p (x u) -> p x u", u=2), bank.rearrange("p u x -> p x u"))
-            return dst
-
-        def round_tails(k, rounded, which, calls=1):
-            for c in which:
-                width = pieces[k][c] // calls
-                for at in range(0, pieces[k][c], width):
-                    first = columns(k, c).start + at
-                    nc.scalar.activation(rounded[:, first:first + width], tails[k, c][:, at:at + width], COPY)
-
-        def pick_tails_on_scalar(rounded, picked):
-            nc.scalar.activation(picked[:], rounded[:].indirect(tail_list[:]), COPY)
+        def pick_on_scalar(name, window, offsets, dtype):
+            picked = kept(name, [P, QUERIES], dtype)
+            nc.scalar.activation(picked[:], window.indirect(offsets[:]), COPY)
             return picked
 
-        def part(offsets, queries):
-            return offsets[:, queries.start // 16:queries.stop // 16]
-
-        def pick(picked, table, offsets):
-            nc.vector.tensor_copy(picked, table[:].indirect(offsets))
+        def pick_on_vector(name, window, offsets, dtype):
+            picked = kept(name, [P, QUERIES], dtype)
+            nc.vector.tensor_copy(picked[:], window.indirect(offsets[:]))
             return picked
 
-        def quantise_tails(k, turned, calls=1):
+        def tail_operand(k, picked, turned):
+            bank = banks.tile([P, 2, P], F32, name="t_bank", tag="turn%d" % (k % 2))
+            transpose_words(picked[:], bank[:])
+            nc.scalar.copy(turned[:].bitcast(F32).rearrange("p (x u) -> p x u", u=2), bank[:].rearrange("p u x -> p x u"))
             codes = kept("t_codes%d" % k, [P, P], U32)
             scales = kept("t_scales%d" % k, [P, P], U8)
-            width = P // calls
-            for c in range(0, P, width):
-                nc.vector.quantize_mx(out=codes[:, c:c + width].bitcast(E4M3X4), scales=scales[:, c:c + width],
-                                      in_=turned[:, 4 * c:4 * (c + width)])
+            nc.vector.quantize_mx(out=codes[:].bitcast(E4M3X4), scales=scales[:], in_=turned[:])
             return codes, scales
 
-        def quantise_grads(codes, scales, queries, turned):
-            nc.vector.quantize_mx(out=codes[:, queries].bitcast(E5M2X4), scales=scales[:, queries], in_=turned)
-
-        def product(operand, moving, bank_tag):
-            acc = banks.tile([P, QUERIES], F32, name="acc", tag=bank_tag)
+        def product(k, operand):
+            acc = banks.tile([P, QUERIES], F32, name="acc", tag="acc%d" % k)
             nc.tensor.matmul_mx(out=acc[:], lhsT=operand[0][:].bitcast(E4M3X4), lhsT_scale=operand[1][:],
-                                rhs=moving[0][:].bitcast(E5M2X4), rhs_scale=moving[1][:], start=True, stop=True)
+                                rhs=g_codes[:].bitcast(E5M2X4), rhs_scale=g_scales[:], start=True, stop=True)
             return acc
 
-        def leave(b, acc, queries):
-            nc.scalar.copy(b[:, queries], acc[:, queries])
+        def leave(k, acc):
+            b = kept("b%d" % k, [P, QUERIES], F32)
+            nc.scalar.copy(b[:], acc[:])
             return b
 
-        def scatter_heads(k, b, r_picked, queries):
-            nc.vector.tensor_tensor(dh[k][:].indirect(part(head_list, queries)), b, r_picked, MULT)
+        def put_pair(name, pair, pick_list, put_list, windows, b_even, acc_odd):
+            odd = pick_on_vector(name + "_odd", pair[:, 1, :], pick_list, F32)
+            even = pick_on_scalar(name + "_even", pair[:, 0, :], pick_list, F32)
+            values = kept(name + "_values", [P, QUERIES], F32)
+            nc.vector.tensor_tensor(values[:], acc_odd[:], odd[:], MULT)
+            nc.vector.tensor_tensor(windows[0][:].indirect(put_list[:]), b_even[:], even[:], MULT)
+            for at in range(0, QUERIES, HALF):
+                nc.scalar.activation(windows[1][:].indirect(put_list[:, at // 16:(at + HALF) // 16]),
+                                     values[:, at:at + HALF], COPY)
 
-        def scatter_rels(k, b, h_picked, queries):
-            nc.vector.tensor_tensor(dr[k][:].indirect(part(rel_list, queries)), b, h_picked, MULT)
+        dh = [kept("dh%d" % k, [P, ENTITIES], F32) for k in range(2)]
+        for window in dh:
+            nc.vector.memset(window[:].bitcast(I32), 0)
 
-        def put_heads(k, b, r_picked, queries):
-            scatter_heads(k, b, r_picked, queries)
-            nc.sync.dma_start(out_0[rows(k), :], dh[k][:])
-
-        def put_rels(k, b, h_picked, queries):
-            scatter_rels(k, b, h_picked, queries)
-            nc.sync.dma_start(out_1[rows(k), :], dr[k][:])
-
-        early, late, every = slice(0, EARLY), slice(EARLY, QUERIES), slice(0, QUERIES)
-        moving = (g_codes, g_scales)
-
-        def turn_pair(rounded, dst, bank_tag):
-            bank = banks.tile([P, 2, 2, P], F32, name="pair_bank", tag=bank_tag)
+        operand0 = tail_operand(0, pick_on_scalar("t_picked0", tails[0][:], tail_list, BF16),
+                                kept("t_turned0", [P, 4 * P], BF16))
+        g_rounded = kept("g_rounded", [P, 4, SLOTS], BF16)
+        g_turned = placed("g_turned", [P, 4 * QUERIES], BF16, 6)
+        g_codes = kept("g_codes", [P, QUERIES], U32)
+        g_scales = kept("g_scales", [P, QUERIES], U8)
+        for j in range(2):
+            nc.vector.tensor_copy(g_rounded[:, 2 * j:2 * j + 2, :], grads[:, 2 * j:2 * j + 2, :])
+        g_words = g_turned[:].bitcast(F32).rearrange("p (x j e u) -> p j x e u", j=2, e=2, u=2)
+        for j in range(2):
+            bank = banks.tile([P, 2, 2, P], F32, name="g_bank", tag="g%d" % j)
             for e in range(2):
-                transpose_words(rounded[e], bank[:, e])
-            nc.scalar.copy(dst.bitcast(F32).rearrange("p (x e u) -> p x e u", e=2, u=2),
-                           bank[:].rearrange("p e u x -> p x e u"))
+                transpose_words(g_rounded[:, 2 * j + e, :], bank[:, e])
+            nc.scalar.copy(g_words[:, j], bank[:].rearrange("p e u x -> p x e u"))
+        nc.vector.quantize_mx(out=g_codes[:].bitcast(E5M2X4), scales=g_scales[:], in_=g_turned[:])
+        operand1 = tail_operand(1, pick_on_scalar("t_picked1", tails[1][:], tail_list, BF16),
+                                placed("t_turned1", [P, 4 * P], BF16, 19.5))
+        b0 = leave(0, product(0, operand0))
+        acc1 = product(1, operand1)
 
-        t_picked0 = kept("t_picked0", [P, SLOTS], BF16)
-        pick(t_picked0[:], tails0, tail_list[:])
-        t_turned0 = turn(t_picked0, kept("t_turned0", [P, 4 * P], BF16)[:], "t0")
-        early_rounded = [kept("g_rounded%d" % e, [P, SLOTS], BF16) for e in range(2)]
-        for e in range(2):
-            nc.vector.tensor_copy(early_rounded[e][:], early_grads[:, e, :])
-        trio = kept("trio", [P, 3 * QUERIES], F32)
-        r0, r1, r2 = trio[:, :QUERIES], trio[:, QUERIES:2 * QUERIES], trio[:, 2 * QUERIES:]
-        g_turned_early = trio[:, 2 * QUERIES - EARLY:2 * QUERIES + EARLY].bitcast(BF16)
-        turn_pair(early_rounded, g_turned_early, "g1")
-        pick(r0, rels[0], rel_list[:])
-        operand0 = quantise_tails(0, t_turned0)
-        pick(r1[:, early], rels[1], part(rel_list, early))
-        for a in range(2):
-            quantise_grads(g_codes, g_scales, rows(a), g_turned_early[:, a * SLOTS:(a + 1) * SLOTS])
-        acc_early = product(operand0, moving, "early")
-        b0 = leave(kept("b0", [P, EARLY], F32), acc_early, early)
-        pick(r1[:, late], rels[1], part(rel_list, late))
-        pick(r2, rels[2], rel_list[:])
-        scatter_heads(0, b0[:, early], r0[:, early], early)
+        dh.append(placed("dh2", [P, ENTITIES], F32, 0))
+        dh.append(placed("dh3", [P, ENTITIES], F32, 8))
+        dr = [placed("dr%d" % k, [P, RELATIONS], F32, 16 + 4 * k) for k in range(2)]
+        for window in dh[2:] + dr:
+            nc.gpsimd.memset(window[:].bitcast(I32), 0)
 
-        g_rounded2 = placed("g_rounded2", [P, SLOTS], BF16, 8 * kib)
-        g_rounded3 = placed("g_rounded3", [P, SLOTS], BF16, 9 * kib)
-        nc.scalar.activation(g_rounded2[:], late_grads[:, 0, :], COPY)
-        nc.scalar.activation(g_rounded3[:], late_grads[:, 1, :], COPY)
-        h0 = pick(kept("h_picked0", [P, QUERIES], F32, "late_grads")[:], heads[0], head_list[:])
-        g_turned_late = kept("g_turned_late", [P, 8 * P], BF16)
-        turn_pair([g_rounded2, g_rounded3], g_turned_late[:], "g0")
-        quantise_grads(g_codes, g_scales, late, g_turned_late[:])
-        b0_early = placed("b0_early", [P, EARLY], F32, 8 * kib + kib // 2)
-        nc.scalar.copy(b0_early[:], acc_early[:, early])
-        acc_late = product(operand0, moving, "late")
-        t_rounded1 = placed("t_rounded1", [P, ENTITIES], BF16, 9 * kib + kib // 2)
-        round_tails(1, t_rounded1, range(1))
-        b0_late = kept("b0_late", [P, QUERIES - EARLY], F32, "tails1_0")
-        nc.scalar.copy(b0_late[:], acc_late[:, late])
-        scatter_rels(0, b0_early[:], h0[:, early], early)
-        put_heads(0, b0_late[:], r0[:, late], late)
-        put_rels(0, b0_late[:], h0[:, late], late)
+        put_pair("r0", rel_pairs[0], rel_list, head_list, dh[:2], b0, acc1)
 
-        round_tails(1, t_rounded1, range(1, 2))
-        t_picked1 = pick_tails_on_scalar(t_rounded1, kept("t_picked1", [P, SLOTS], BF16))
-        h1 = pick(placed("h_picked1", [P, QUERIES], F32, 28 * kib)[:], heads[1], head_list[:])
-        t_rounded2 = placed("t_rounded2", [P, ENTITIES], BF16, 16 * kib)
-        round_tails(2, t_rounded2, range(1))
-        operand1 = quantise_tails(1, turn(t_picked1, kept("t_turned1", [P, 4 * P], BF16, "tails2_0")[:], "t1"))
-        acc1 = product(operand1, moving, "b1")
-        round_tails(2, t_rounded2, range(1, 2))
-        b1 = leave(kept("b1", [P, QUERIES], F32, "tails2_1"), acc1, every)
-        h2 = pick(kept("h_picked2", [P, QUERIES], F32)[:], heads[2], head_list[:])
-        r3 = pick(kept("r_picked3", [P, QUERIES], F32)[:], rels[3], rel_list[:])
-        round_tails(2, t_rounded2, range(2, 4))
-        put_heads(1, b1[:], r1, every)
-        dh.append(kept("dh2", [P, ENTITIES], F32, "rels3"))
-        nc.gpsimd.memset(dh[2][:].bitcast(I32), 0)
-        dh.append(dh[1])
-        dr.extend(dr[:2])
-        before, behind = slice(0, 320), slice(320, QUERIES)
-        scatter_rels(1, b1[:, before], h1[:, before], before)
+        picked2 = pick_on_vector("t_picked2", tails[2][:], tail_list, BF16)
+        picked3 = pick_on_scalar("t_picked3", tails[3][:], tail_list, BF16)
+        operand2 = tail_operand(2, picked2, held.tile([P, 4 * P], BF16, name="t_turned2", tag="tails3", align_bytes=64))
+        operand3 = tail_operand(3, picked3, placed("t_turned3", [P, 4 * P], BF16, 27.5))
+        b2 = leave(2, product(2, operand2))
+        acc3 = product(3, operand3)
+        dr.extend([placed("dr%d" % k, [P, RELATIONS], F32, 16 + 4 * k) for k in range(2, 4)])
+        for window in dr[2:]:
+            nc.gpsimd.memset(window[:].bitcast(I32), 0)
 
-        t_picked2 = pick_tails_on_scalar(t_rounded2, kept("t_picked2", [P, SLOTS], BF16))
-        t_turned2 = turn_in(t_picked2, kept("t_turned2", [P, 4 * P], BF16)[:],
-                            acc1[:, early].rearrange("p (u x) -> p u x", u=2))
-        operand2 = quantise_tails(2, t_turned2)
-        b1_late = kept("b1_late", [P, QUERIES - 320], F32)
-        nc.scalar.copy(b1_late[:], acc1[:, behind])
-        put_rels(1, b1_late[:], h1[:, behind], behind)
-        b2 = leave(kept("b2", [P, QUERIES], F32), product(operand2, moving, "b2"), every)
-        t_rounded3 = placed("t_rounded3", [P, ENTITIES], BF16, 16 * kib)
-        round_tails(3, t_rounded3, range(2))
-        h3 = pick(kept("h_picked3", [P, QUERIES], F32, "tails3_0")[:], heads[3], head_list[:])
-        t_picked3 = pick_tails_on_scalar(t_rounded3, kept("t_picked3", [P, SLOTS], BF16))
-        put_heads(2, b2[:], r2, every)
-        operand3 = quantise_tails(3, turn(t_picked3, kept("t_turned3", [P, 4 * P], BF16)[:], "t0"))
-        b3 = leave(kept("b3", [P, QUERIES], F32), product(operand3, moving, "early"), every)
-        put_rels(2, b2[:], h2, every)
-        put_heads(3, b3[:], r3, every)
-        put_rels(3, b3[:], h3, every)
+        put_pair("r1", rel_pairs[1], rel_list, head_list, dh[2:], b2, acc3)
+        put_pair("h0", head_pairs[0], head_list, rel_list, dr[:2], b0, acc1)
+        put_pair("h1", head_pairs[1], head_list, rel_list, dr[2:], b2, acc3)
+
+        for k in range(BLOCKS):
+            nc.sync.dma_start(dealt(out_0)[:, k, :], dh[k][:])
+        for k in range(BLOCKS):
+            nc.sync.dma_start(dealt(out_1)[:, k, :], dr[k][:])

@@ -53,15 +53,15 @@ def tile_attend_gdistm_hr_kernel(tc, hT, rT, G, tT, hoffs, roffs, offs, out_0, o
         ident = kept("ident", [P, P], F32)
         zeros = kept("zeros", [P, P], F32)
 
+        nc.sync.dma_start(grads[:], G.rearrange("(p e) i -> p e i", e=4))
         nc.sync.dma_start(tails[0][:], dealt(tT)[:, 0, :])
         nc.sync.dma_start(tail_list[:], offs)
-        nc.sync.dma_start(grads[:], G.rearrange("(p e) i -> p e i", e=4))
         nc.sync.dma_start(tails[1][:], dealt(tT)[:, 1, :])
+        nc.sync.dma_start(tails[2][:], dealt(tT)[:, 2, :])
+        nc.sync.dma_start(tails[3][:], dealt(tT)[:, 3, :])
         nc.sync.dma_start(rel_list[:], roffs)
         nc.sync.dma_start(head_list[:], hoffs)
         nc.sync.dma_start(rel_pairs[0][:], dealt(rT)[:, 0:2, :])
-        nc.sync.dma_start(tails[2][:], dealt(tT)[:, 2, :])
-        nc.sync.dma_start(tails[3][:], dealt(tT)[:, 3, :])
         nc.sync.dma_start(rel_pairs[1][:], dealt(rT)[:, 2:4, :])
         nc.sync.dma_start(head_pairs[0][:], dealt(hT)[:, 0:2, :])
         nc.sync.dma_start(head_pairs[1][:], dealt(hT)[:, 2:4, :])
@@ -75,24 +75,31 @@ def tile_attend_gdistm_hr_kernel(tc, hT, rT, G, tT, hoffs, roffs, offs, out_0, o
             for u in range(2):
                 nc.tensor.transpose(bank[:, u, :], words[:, u::2], ident[:])
 
-        def pick_on_scalar(name, window, offsets, dtype):
-            picked = kept(name, [P, QUERIES], dtype)
+        def over(name, shape, dtype, tag):
+            return held.tile(shape, dtype, name=name, tag=tag, align_bytes=64)
+
+        def pick_on_scalar(name, window, offsets, dtype, tag=None):
+            picked = over(name, [P, QUERIES], dtype, tag or name)
             nc.scalar.activation(picked[:], window.indirect(offsets[:]), COPY)
             return picked
 
-        def pick_on_vector(name, window, offsets, dtype):
-            picked = kept(name, [P, QUERIES], dtype)
-            nc.vector.tensor_copy(picked[:], window.indirect(offsets[:]))
-            return picked
-
-        def tail_operand(k, picked, turned):
+        def turn(k, picked):
             bank = banks.tile([P, 2, P], F32, name="t_bank", tag="turn%d" % (k % 2))
             transpose_words(picked[:], bank[:])
-            nc.scalar.copy(turned[:].bitcast(F32).rearrange("p (x u) -> p x u", u=2), bank[:].rearrange("p u x -> p x u"))
-            codes = kept("t_codes%d" % k, [P, P], U32)
+            return bank
+
+        def leave_turned(turned, bank, copy):
+            copy(turned[:].bitcast(F32).rearrange("p (x u) -> p x u", u=2), bank[:].rearrange("p u x -> p x u"))
+            return turned
+
+        def quantise_tails(k, turned, tag):
+            codes = over("t_codes%d" % k, [P, P], U32, tag)
             scales = kept("t_scales%d" % k, [P, P], U8)
             nc.vector.quantize_mx(out=codes[:].bitcast(E4M3X4), scales=scales[:], in_=turned[:])
             return codes, scales
+
+        def tail_operand(k, picked, turned, copy):
+            return quantise_tails(k, leave_turned(turned, turn(k, picked), copy), "t_codes%d" % k)
 
         def product(k, operand):
             acc = banks.tile([P, QUERIES], F32, name="acc", tag="acc%d" % k)
@@ -100,68 +107,77 @@ def tile_attend_gdistm_hr_kernel(tc, hT, rT, G, tT, hoffs, roffs, offs, out_0, o
                                 rhs=g_codes[:].bitcast(E5M2X4), rhs_scale=g_scales[:], start=True, stop=True)
             return acc
 
-        def leave(k, acc):
-            b = kept("b%d" % k, [P, QUERIES], F32)
-            nc.scalar.copy(b[:], acc[:])
+        def leave(b, acc, copy):
+            copy(b[:], acc[:])
             return b
 
-        def put_pair(name, pair, pick_list, put_list, windows, b_even, acc_odd):
-            odd = pick_on_vector(name + "_odd", pair[:, 1, :], pick_list, F32)
-            even = pick_on_scalar(name + "_even", pair[:, 0, :], pick_list, F32)
+        def part(offsets, first, last):
+            return offsets[:, first // 16:last // 16]
+
+        def pick_pair(name, pair, pick_list, b_even):
             values = kept(name + "_values", [P, QUERIES], F32)
-            nc.vector.tensor_tensor(values[:], acc_odd[:], odd[:], MULT)
-            nc.vector.tensor_tensor(windows[0][:].indirect(put_list[:]), b_even[:], even[:], MULT)
-            for at in range(0, QUERIES, HALF):
-                nc.scalar.activation(windows[1][:].indirect(put_list[:, at // 16:(at + HALF) // 16]),
-                                     values[:, at:at + HALF], COPY)
+            whole = pair[:].rearrange("p e c -> p (e c)")
+            nc.vector.tensor_tensor(values[:], whole.indirect(pick_list[:]), b_even[:], MULT)
+            return values, pick_on_scalar(name + "_odd", pair[:, 1, :], pick_list, F32)
+
+        def put_pair(picked, put_list, windows, b_odd, on_vector=0):
+            values, odd = picked
+            if on_vector:
+                nc.vector.tensor_copy(windows[0][:].indirect(part(put_list, 0, on_vector)), values[:, :on_vector])
+                pieces = [(on_vector, QUERIES)]
+            else:
+                pieces = [(0, HALF), (HALF, QUERIES)]
+            nc.vector.tensor_tensor(windows[1][:].indirect(put_list[:]), b_odd[:], odd[:], MULT)
+            for first, last in pieces:
+                nc.scalar.activation(windows[0][:].indirect(part(put_list, first, last)), values[:, first:last], COPY)
 
         dh = [kept("dh%d" % k, [P, ENTITIES], F32) for k in range(2)]
         for window in dh:
             nc.vector.memset(window[:].bitcast(I32), 0)
 
-        operand0 = tail_operand(0, pick_on_scalar("t_picked0", tails[0][:], tail_list, BF16),
-                                kept("t_turned0", [P, 4 * P], BF16))
-        g_rounded = kept("g_rounded", [P, 4, SLOTS], BF16)
-        g_turned = placed("g_turned", [P, 4 * QUERIES], BF16, 6)
+        g_rounded = [kept("g_rounded%d" % j, [P, 2, SLOTS], BF16) for j in range(2)]
+        g_turned = placed("g_turned", [P, 4 * QUERIES], BF16, 22)
         g_codes = kept("g_codes", [P, QUERIES], U32)
         g_scales = kept("g_scales", [P, QUERIES], U8)
         for j in range(2):
-            nc.vector.tensor_copy(g_rounded[:, 2 * j:2 * j + 2, :], grads[:, 2 * j:2 * j + 2, :])
+            nc.vector.tensor_copy(g_rounded[j][:], grads[:, 2 * j:2 * j + 2, :])
         g_words = g_turned[:].bitcast(F32).rearrange("p (x j e u) -> p j x e u", j=2, e=2, u=2)
-        for j in range(2):
+        for j, copy in enumerate((nc.scalar.copy, nc.vector.tensor_copy)):
             bank = banks.tile([P, 2, 2, P], F32, name="g_bank", tag="g%d" % j)
             for e in range(2):
-                transpose_words(g_rounded[:, 2 * j + e, :], bank[:, e])
-            nc.scalar.copy(g_words[:, j], bank[:].rearrange("p e u x -> p x e u"))
+                transpose_words(g_rounded[j][:, e, :], bank[:, e])
+            copy(g_words[:, j], bank[:].rearrange("p e u x -> p x e u"))
         nc.vector.quantize_mx(out=g_codes[:].bitcast(E5M2X4), scales=g_scales[:], in_=g_turned[:])
-        operand1 = tail_operand(1, pick_on_scalar("t_picked1", tails[1][:], tail_list, BF16),
-                                placed("t_turned1", [P, 4 * P], BF16, 19.5))
-        b0 = leave(0, product(0, operand0))
-        acc1 = product(1, operand1)
-
-        dh.append(placed("dh2", [P, ENTITIES], F32, 0))
-        dh.append(placed("dh3", [P, ENTITIES], F32, 8))
-        dr = [placed("dr%d" % k, [P, RELATIONS], F32, 16 + 4 * k) for k in range(2)]
-        for window in dh[2:] + dr:
+        dh.extend([placed("dh%d" % k, [P, ENTITIES], F32, 8 * k) for k in range(2, BLOCKS)])
+        for window in dh[2:]:
             nc.gpsimd.memset(window[:].bitcast(I32), 0)
 
-        put_pair("r0", rel_pairs[0], rel_list, head_list, dh[:2], b0, acc1)
+        picked = [pick_on_scalar("t_picked%d" % k, tails[k][:], tail_list, BF16, "g_rounded0" if k == 0 else None)
+                  for k in range(BLOCKS)]
 
-        picked2 = pick_on_vector("t_picked2", tails[2][:], tail_list, BF16)
-        picked3 = pick_on_scalar("t_picked3", tails[3][:], tail_list, BF16)
-        operand2 = tail_operand(2, picked2, held.tile([P, 4 * P], BF16, name="t_turned2", tag="tails3", align_bytes=64))
-        operand3 = tail_operand(3, picked3, placed("t_turned3", [P, 4 * P], BF16, 27.5))
-        b2 = leave(2, product(2, operand2))
-        acc3 = product(3, operand3)
-        dr.extend([placed("dr%d" % k, [P, RELATIONS], F32, 16 + 4 * k) for k in range(2, 4)])
-        for window in dr[2:]:
+        def block_product(k, turned):
+            return product(k, tail_operand(k, picked[k], turned, nc.vector.tensor_copy))
+
+        b = []
+        for k in range(2):
+            acc = block_product(k, kept("t_turned%d" % k, [P, 4 * P], BF16))
+            b.append(leave(over("b%d" % k, [P, QUERIES], F32, "tails%d" % (k + 2)), acc, nc.scalar.copy))
+        acc = block_product(2, placed("t_turned2", [P, 4 * P], BF16, 3.5))
+        b.append(leave(kept("b2", [P, QUERIES], F32), acc, nc.vector.tensor_copy))
+        operand_bank = turn(3, picked[3])
+        turned = leave_turned(placed("t_turned3", [P, 4 * P], BF16, 11.5), operand_bank, nc.scalar.copy)
+        rels_picked = pick_pair("r0", rel_pairs[0], rel_list, b[0])
+        acc = product(3, quantise_tails(3, turned, "rels0"))
+        put_pair(rels_picked, head_list, dh, b[1])
+        b.append(leave(over("b3", [P, QUERIES], F32, "r0_odd"), acc, nc.vector.tensor_copy))
+        dr = [placed("dr%d" % k, [P, RELATIONS], F32, 4 * k) for k in range(BLOCKS)]
+        for window in dr:
             nc.gpsimd.memset(window[:].bitcast(I32), 0)
+        put_pair(pick_pair("r1", rel_pairs[1], rel_list, b[2]), head_list, dh[2:], b[3])
+        put_pair(pick_pair("h0", head_pairs[0], head_list, b[0]), rel_list, dr, b[1], 128)
+        put_pair(pick_pair("h1", head_pairs[1], head_list, b[2]), rel_list, dr[2:], b[3])
 
-        put_pair("r1", rel_pairs[1], rel_list, head_list, dh[2:], b2, acc3)
-        put_pair("h0", head_pairs[0], head_list, rel_list, dr[:2], b0, acc1)
-        put_pair("h1", head_pairs[1], head_list, rel_list, dr[2:], b2, acc3)
-
-        for k in range(BLOCKS):
+        for k in (1, 0, 3, 2):
             nc.sync.dma_start(dealt(out_0)[:, k, :], dh[k][:])
-        for k in range(BLOCKS):
+        for k in (1, 0, 3, 2):
             nc.sync.dma_start(dealt(out_1)[:, k, :], dr[k][:])

@@ -120,15 +120,10 @@ def tile_attend_gdistm_hr_kernel(tc, hT, rT, G, tT, hoffs, roffs, offs, out_0, o
             nc.vector.tensor_tensor(values[:], whole.indirect(pick_list[:]), b_even[:], MULT)
             return values, pick_on_scalar(name + "_odd", pair[:, 1, :], pick_list, F32)
 
-        def put_pair(picked, put_list, windows, b_odd, on_vector=0):
+        def put_pair(picked, put_list, windows, b_odd):
             values, odd = picked
-            if on_vector:
-                nc.vector.tensor_copy(windows[0][:].indirect(part(put_list, 0, on_vector)), values[:, :on_vector])
-                pieces = [(on_vector, QUERIES)]
-            else:
-                pieces = [(0, HALF), (HALF, QUERIES)]
             nc.vector.tensor_tensor(windows[1][:].indirect(put_list[:]), b_odd[:], odd[:], MULT)
-            for first, last in pieces:
+            for first, last in ((0, HALF), (HALF, QUERIES)):
                 nc.scalar.activation(windows[0][:].indirect(part(put_list, first, last)), values[:, first:last], COPY)
 
         dh = [kept("dh%d" % k, [P, ENTITIES], F32) for k in range(2)]
@@ -169,12 +164,12 @@ def tile_attend_gdistm_hr_kernel(tc, hT, rT, G, tT, hoffs, roffs, offs, out_0, o
         rels_picked = pick_pair("r0", rel_pairs[0], rel_list, b[0])
         acc = product(3, quantise_tails(3, turned, "rels0"))
         put_pair(rels_picked, head_list, dh, b[1])
-        b.append(leave(over("b3", [P, QUERIES], F32, "r0_odd"), acc, nc.vector.tensor_copy))
+        b.append(leave(kept("b3", [P, QUERIES], F32), acc, nc.scalar.copy))
         dr = [placed("dr%d" % k, [P, RELATIONS], F32, 4 * k) for k in range(BLOCKS)]
         for window in dr:
             nc.gpsimd.memset(window[:].bitcast(I32), 0)
         put_pair(pick_pair("r1", rel_pairs[1], rel_list, b[2]), head_list, dh[2:], b[3])
-        put_pair(pick_pair("h0", head_pairs[0], head_list, b[0]), rel_list, dr, b[1], 128)
+        put_pair(pick_pair("h0", head_pairs[0], head_list, b[0]), rel_list, dr, b[1])
         put_pair(pick_pair("h1", head_pairs[1], head_list, b[2]), rel_list, dr[2:], b[3])
 
         for k in (1, 0, 3, 2):

@@ -47,8 +47,10 @@ def tile_attend_gdistm_hr_kernel(tc, hT, rT, G, tT, hoffs, roffs, offs, out_0, o
         rel_list = lists.tile([P, QUERIES // 16], U16, name="rel_list")
 
         tails = [kept("tails%d" % k, [P, ENTITIES], F32) for k in range(BLOCKS)]
-        head_pairs = [kept("heads%d" % j, [P, 2, ENTITIES], F32) for j in range(BLOCKS // 2)]
-        rel_pairs = [kept("rels%d" % j, [P, 2, RELATIONS], F32) for j in range(BLOCKS // 2)]
+        heads = [kept("heads0", [P, ENTITIES], F32), placed("heads1", [P, ENTITIES], F32, 18)]
+        late_heads = kept("late_heads", [P, 2, ENTITIES], F32)
+        rels = [kept("rels%d" % k, [P, RELATIONS], F32) for k in range(2)]
+        late_rels = kept("late_rels", [P, 2, RELATIONS], F32)
         grads = kept("grads", [P, 4, SLOTS], F32)
         ident = kept("ident", [P, P], F32)
         zeros = kept("zeros", [P, P], F32)
@@ -57,14 +59,16 @@ def tile_attend_gdistm_hr_kernel(tc, hT, rT, G, tT, hoffs, roffs, offs, out_0, o
         nc.sync.dma_start(tails[0][:], dealt(tT)[:, 0, :])
         nc.sync.dma_start(tail_list[:], offs)
         nc.sync.dma_start(tails[1][:], dealt(tT)[:, 1, :])
-        nc.sync.dma_start(tails[2][:], dealt(tT)[:, 2, :])
-        nc.sync.dma_start(tails[3][:], dealt(tT)[:, 3, :])
         nc.sync.dma_start(rel_list[:], roffs)
         nc.sync.dma_start(head_list[:], hoffs)
-        nc.sync.dma_start(rel_pairs[0][:], dealt(rT)[:, 0:2, :])
-        nc.sync.dma_start(rel_pairs[1][:], dealt(rT)[:, 2:4, :])
-        nc.sync.dma_start(head_pairs[0][:], dealt(hT)[:, 0:2, :])
-        nc.sync.dma_start(head_pairs[1][:], dealt(hT)[:, 2:4, :])
+        nc.sync.dma_start(rels[1][:], dealt(rT)[:, 1, :])
+        nc.sync.dma_start(tails[2][:], dealt(tT)[:, 2, :])
+        nc.sync.dma_start(tails[3][:], dealt(tT)[:, 3, :])
+        nc.sync.dma_start(rels[0][:], dealt(rT)[:, 0, :])
+        nc.sync.dma_start(heads[0][:], dealt(hT)[:, 0, :])
+        nc.sync.dma_start(heads[1][:], dealt(hT)[:, 1, :])
+        nc.sync.dma_start(late_rels[:], dealt(rT)[:, 2:4, :])
+        nc.sync.dma_start(late_heads[:], dealt(hT)[:, 2:4, :])
 
         nc.gpsimd.memset(zeros[:], 0.0)
         nc.gpsimd.affine_select(out=ident[:], in_=zeros[:], compare_op=mybir.AluOpType.not_equal, fill=1.0, base=0,
@@ -92,14 +96,10 @@ def tile_attend_gdistm_hr_kernel(tc, hT, rT, G, tT, hoffs, roffs, offs, out_0, o
             copy(turned[:].bitcast(F32).rearrange("p (x u) -> p x u", u=2), bank[:].rearrange("p u x -> p x u"))
             return turned
 
-        def quantise_tails(k, turned, tag):
-            codes = over("t_codes%d" % k, [P, P], U32, tag)
+        def quantise_tails(k, turned, codes):
             scales = kept("t_scales%d" % k, [P, P], U8)
             nc.vector.quantize_mx(out=codes[:].bitcast(E4M3X4), scales=scales[:], in_=turned[:])
             return codes, scales
-
-        def tail_operand(k, picked, turned, copy):
-            return quantise_tails(k, leave_turned(turned, turn(k, picked), copy), "t_codes%d" % k)
 
         def product(k, operand):
             acc = banks.tile([P, QUERIES], F32, name="acc", tag="acc%d" % k)
@@ -114,24 +114,32 @@ def tile_attend_gdistm_hr_kernel(tc, hT, rT, G, tT, hoffs, roffs, offs, out_0, o
         def part(offsets, first, last):
             return offsets[:, first // 16:last // 16]
 
+        def pick_times(name, window, pick_list, b_even):
+            values = kept(name, [P, QUERIES], F32)
+            nc.vector.tensor_tensor(values[:], window.indirect(pick_list[:]), b_even[:], MULT)
+            return values
+
         def pick_pair(name, pair, pick_list, b_even):
-            values = kept(name + "_values", [P, QUERIES], F32)
-            whole = pair[:].rearrange("p e c -> p (e c)")
-            nc.vector.tensor_tensor(values[:], whole.indirect(pick_list[:]), b_even[:], MULT)
+            values = pick_times(name + "_values", pair[:].rearrange("p e c -> p (e c)"), pick_list, b_even)
             return values, pick_on_scalar(name + "_odd", pair[:, 1, :], pick_list, F32)
 
-        def put_pair(picked, put_list, windows, b_odd):
-            values, odd = picked
-            nc.vector.tensor_tensor(windows[1][:].indirect(put_list[:]), b_odd[:], odd[:], MULT)
+        def put_on_vector(window, put_list, b_odd, odd):
+            nc.vector.tensor_tensor(window[:].indirect(put_list[:]), b_odd[:], odd[:], MULT)
+
+        def put_on_scalar(window, put_list, values):
             for first, last in ((0, HALF), (HALF, QUERIES)):
-                nc.scalar.activation(windows[0][:].indirect(part(put_list, first, last)), values[:, first:last], COPY)
+                nc.scalar.activation(window[:].indirect(part(put_list, first, last)), values[:, first:last], COPY)
+
+        def put_pair(picked, put_list, windows, b_odd):
+            put_on_vector(windows[1], put_list, b_odd, picked[1])
+            put_on_scalar(windows[0], put_list, picked[0])
 
         dh = [kept("dh%d" % k, [P, ENTITIES], F32) for k in range(2)]
         for window in dh:
             nc.vector.memset(window[:].bitcast(I32), 0)
 
         g_rounded = [kept("g_rounded%d" % j, [P, 2, SLOTS], BF16) for j in range(2)]
-        g_turned = placed("g_turned", [P, 4 * QUERIES], BF16, 22)
+        g_turned = kept("g_turned", [P, 4 * QUERIES], BF16)
         g_codes = kept("g_codes", [P, QUERIES], U32)
         g_scales = kept("g_scales", [P, QUERIES], U8)
         for j in range(2):
@@ -143,36 +151,43 @@ def tile_attend_gdistm_hr_kernel(tc, hT, rT, G, tT, hoffs, roffs, offs, out_0, o
                 transpose_words(g_rounded[j][:, e, :], bank[:, e])
             copy(g_words[:, j], bank[:].rearrange("p e u x -> p x e u"))
         nc.vector.quantize_mx(out=g_codes[:].bitcast(E5M2X4), scales=g_scales[:], in_=g_turned[:])
-        dh.extend([placed("dh%d" % k, [P, ENTITIES], F32, 8 * k) for k in range(2, BLOCKS)])
-        for window in dh[2:]:
+        picked0 = pick_on_scalar("t_picked0", tails[0][:], tail_list, BF16, "g_rounded0")
+        picked1 = kept("t_picked1", [P, SLOTS], BF16)
+        nc.vector.tensor_copy(picked1[:, :HALF], tails[1][:].indirect(part(tail_list, 0, HALF)))
+        nc.scalar.activation(picked1[:, HALF:], tails[1][:].indirect(part(tail_list, HALF, SLOTS)), COPY)
+        turned = leave_turned(kept("t_turned0", [P, 4 * P], BF16), turn(0, picked0), nc.vector.tensor_copy)
+        acc = [product(0, quantise_tails(0, turned, kept("t_codes0", [P, P], U32)))]
+        turned = leave_turned(placed("t_turned1", [P, 4 * P], BF16, 3.5), turn(1, picked1), nc.vector.tensor_copy)
+        acc.append(product(1, quantise_tails(1, turned, placed("t_codes1", [P, P], U32, 8))))
+        b = [leave(over("b0", [P, QUERIES], F32, "t_picked1"), acc[0], nc.vector.tensor_copy)]
+        rels_odd = pick_on_scalar("r0_odd", rels[1][:], rel_list, F32)
+        b.append(leave(over("b1", [P, QUERIES], F32, "rels1"), acc[1], nc.scalar.copy))
+        put_on_vector(dh[1], head_list, b[1], rels_odd)
+        dr = [placed("dr%d" % k, [P, RELATIONS], F32, 4 * k) for k in range(2)]
+        dh.append(placed("dh2", [P, ENTITIES], F32, 8))
+        for window in dr + dh[2:]:
             nc.gpsimd.memset(window[:].bitcast(I32), 0)
 
-        picked = [pick_on_scalar("t_picked%d" % k, tails[k][:], tail_list, BF16, "g_rounded0" if k == 0 else None)
-                  for k in range(BLOCKS)]
-
-        def block_product(k, turned):
-            return product(k, tail_operand(k, picked[k], turned, nc.vector.tensor_copy))
-
-        b = []
-        for k in range(2):
-            acc = block_product(k, kept("t_turned%d" % k, [P, 4 * P], BF16))
-            b.append(leave(over("b%d" % k, [P, QUERIES], F32, "tails%d" % (k + 2)), acc, nc.scalar.copy))
-        acc = block_product(2, placed("t_turned2", [P, 4 * P], BF16, 3.5))
-        b.append(leave(kept("b2", [P, QUERIES], F32), acc, nc.vector.tensor_copy))
-        operand_bank = turn(3, picked[3])
-        turned = leave_turned(placed("t_turned3", [P, 4 * P], BF16, 11.5), operand_bank, nc.scalar.copy)
-        rels_picked = pick_pair("r0", rel_pairs[0], rel_list, b[0])
-        acc = product(3, quantise_tails(3, turned, "rels0"))
-        put_pair(rels_picked, head_list, dh, b[1])
-        b.append(leave(kept("b3", [P, QUERIES], F32), acc, nc.scalar.copy))
-        dr = [placed("dr%d" % k, [P, RELATIONS], F32, 4 * k) for k in range(BLOCKS)]
-        for window in dr:
+        picked = [pick_on_scalar("t_picked%d" % k, tails[k][:], tail_list, BF16) for k in (2, 3)]
+        turned2 = leave_turned(over("t_turned2", [P, 4 * P], BF16, "tails3"), turn(2, picked[0]), nc.scalar.copy)
+        turned3 = leave_turned(kept("t_turned3", [P, 4 * P], BF16), turn(3, picked[1]), nc.scalar.copy)
+        put_on_scalar(dh[0], head_list, pick_times("r0_values", rels[0][:], rel_list, b[0]))
+        acc.append(product(2, quantise_tails(2, turned2, over("t_codes2", [P, P], U32, "rels0"))))
+        acc.append(product(3, quantise_tails(3, turned3, kept("t_codes3", [P, P], U32))))
+        values = pick_times("h0_values", heads[0][:], head_list, b[0])
+        b.append(leave(over("b2", [P, QUERIES], F32, "heads0"), acc[2], nc.vector.tensor_copy))
+        b.append(leave(over("b3", [P, QUERIES], F32, "r0_values"), acc[3], nc.scalar.copy))
+        heads_odd = kept("h0_odd", [P, QUERIES], F32)
+        nc.vector.tensor_copy(heads_odd[:], heads[1][:].indirect(head_list[:]))
+        put_pair((values, heads_odd), rel_list, dr, b[1])
+        dh.append(placed("dh3", [P, ENTITIES], F32, 24))
+        dr.extend([placed("dr%d" % k, [P, RELATIONS], F32, 8 + 4 * k) for k in range(2, BLOCKS)])
+        for window in dh[3:] + dr[2:]:
             nc.gpsimd.memset(window[:].bitcast(I32), 0)
-        put_pair(pick_pair("r1", rel_pairs[1], rel_list, b[2]), head_list, dh[2:], b[3])
-        put_pair(pick_pair("h0", head_pairs[0], head_list, b[0]), rel_list, dr, b[1])
-        put_pair(pick_pair("h1", head_pairs[1], head_list, b[2]), rel_list, dr[2:], b[3])
+        put_pair(pick_pair("r1", late_rels, rel_list, b[2]), head_list, dh[2:], b[3])
+        put_pair(pick_pair("h1", late_heads, head_list, b[2]), rel_list, dr[2:], b[3])
 
-        for k in (1, 0, 3, 2):
-            nc.sync.dma_start(dealt(out_0)[:, k, :], dh[k][:])
-        for k in (1, 0, 3, 2):
-            nc.sync.dma_start(dealt(out_1)[:, k, :], dr[k][:])
+        for j in range(BLOCKS // 2):
+            for out, windows in ((out_0, dh), (out_1, dr)):
+                for k in (2 * j + 1, 2 * j):
+                    nc.sync.dma_start(dealt(out)[:, k, :], windows[k][:])

@@ -56,9 +56,9 @@ def tile_attend_gdistm_hr_kernel(tc, hT, rT, G, tT, hoffs, roffs, offs, out_0, o
         zeros = kept("zeros", [P, P], F32)
 
         nc.sync.dma_start(grads[:], G.rearrange("(p e) i -> p e i", e=4))
-        nc.sync.dma_start(tails[0][:], dealt(tT)[:, 0, :])
-        nc.sync.dma_start(tail_list[:], offs)
         nc.sync.dma_start(tails[1][:], dealt(tT)[:, 1, :])
+        nc.sync.dma_start(tail_list[:], offs)
+        nc.sync.dma_start(tails[0][:], dealt(tT)[:, 0, :])
         nc.sync.dma_start(rel_list[:], roffs)
         nc.sync.dma_start(head_list[:], hoffs)
         nc.sync.dma_start(rels[1][:], dealt(rT)[:, 1, :])
@@ -151,24 +151,23 @@ def tile_attend_gdistm_hr_kernel(tc, hT, rT, G, tT, hoffs, roffs, offs, out_0, o
                 transpose_words(g_rounded[j][:, e, :], bank[:, e])
             copy(g_words[:, j], bank[:].rearrange("p e u x -> p x e u"))
         nc.vector.quantize_mx(out=g_codes[:].bitcast(E5M2X4), scales=g_scales[:], in_=g_turned[:])
-        picked0 = pick_on_scalar("t_picked0", tails[0][:], tail_list, BF16, "g_rounded0")
-        picked1 = kept("t_picked1", [P, SLOTS], BF16)
-        nc.vector.tensor_copy(picked1[:, :HALF], tails[1][:].indirect(part(tail_list, 0, HALF)))
-        nc.scalar.activation(picked1[:, HALF:], tails[1][:].indirect(part(tail_list, HALF, SLOTS)), COPY)
-        turned = leave_turned(kept("t_turned0", [P, 4 * P], BF16), turn(0, picked0), nc.vector.tensor_copy)
-        acc = [product(0, quantise_tails(0, turned, kept("t_codes0", [P, P], U32)))]
-        turned = leave_turned(placed("t_turned1", [P, 4 * P], BF16, 3.5), turn(1, picked1), nc.vector.tensor_copy)
-        acc.append(product(1, quantise_tails(1, turned, placed("t_codes1", [P, P], U32, 8))))
-        b = [leave(over("b0", [P, QUERIES], F32, "t_picked1"), acc[0], nc.vector.tensor_copy)]
+        picked1 = pick_on_scalar("t_picked1", tails[1][:], tail_list, BF16, "g_rounded0")
+        picked0 = pick_on_scalar("t_picked0", tails[0][:], tail_list, BF16)
+        turned = leave_turned(kept("t_turned1", [P, 4 * P], BF16), turn(1, picked1), nc.vector.tensor_copy)
+        acc1 = product(1, quantise_tails(1, turned, kept("t_codes1", [P, P], U32)))
+        turned = leave_turned(placed("t_turned0", [P, 4 * P], BF16, 3.5), turn(0, picked0), nc.vector.tensor_copy)
+        acc = [product(0, quantise_tails(0, turned, placed("t_codes0", [P, P], U32, 8))), acc1]
         rels_odd = pick_on_scalar("r0_odd", rels[1][:], rel_list, F32)
-        b.append(leave(over("b1", [P, QUERIES], F32, "rels1"), acc[1], nc.scalar.copy))
-        put_on_vector(dh[1], head_list, b[1], rels_odd)
+        b1 = leave(over("b1", [P, QUERIES], F32, "rels1"), acc[1], nc.scalar.copy)
+        put_on_vector(dh[1], head_list, b1, rels_odd)
         dr = [placed("dr%d" % k, [P, RELATIONS], F32, 4 * k) for k in range(2)]
         dh.append(placed("dh2", [P, ENTITIES], F32, 8))
         for window in dr + dh[2:]:
             nc.gpsimd.memset(window[:].bitcast(I32), 0)
 
-        picked = [pick_on_scalar("t_picked%d" % k, tails[k][:], tail_list, BF16) for k in (2, 3)]
+        picked = [pick_on_scalar("t_picked2", tails[2][:], tail_list, BF16)]
+        b = [leave(over("b0", [P, QUERIES], F32, "tails2"), acc[0], nc.scalar.copy), b1]
+        picked.append(pick_on_scalar("t_picked3", tails[3][:], tail_list, BF16))
         turned2 = leave_turned(over("t_turned2", [P, 4 * P], BF16, "tails3"), turn(2, picked[0]), nc.scalar.copy)
         turned3 = leave_turned(kept("t_turned3", [P, 4 * P], BF16), turn(3, picked[1]), nc.scalar.copy)
         put_on_scalar(dh[0], head_list, pick_times("r0_values", rels[0][:], rel_list, b[0]))

@@ -47,10 +47,9 @@ def tile_attend_gdistm_hr_kernel(tc, hT, rT, G, tT, hoffs, roffs, offs, out_0, o
         rel_list = lists.tile([P, QUERIES // 16], U16, name="rel_list")
 
         tails = [kept("tails%d" % k, [P, ENTITIES], F32) for k in range(BLOCKS)]
-        heads = [kept("heads0", [P, ENTITIES], F32), placed("heads1", [P, ENTITIES], F32, 18)]
-        late_heads = kept("late_heads", [P, 2, ENTITIES], F32)
+        head_pairs = [kept("heads%d" % j, [P, 2, ENTITIES], F32) for j in range(BLOCKS // 2)]
         rels = [kept("rels%d" % k, [P, RELATIONS], F32) for k in range(2)]
-        late_rels = kept("late_rels", [P, 2, RELATIONS], F32)
+        late_rels = placed("late_rels", [P, 2, RELATIONS], F32, 18)
         grads = kept("grads", [P, 4, SLOTS], F32)
         ident = kept("ident", [P, P], F32)
         zeros = kept("zeros", [P, P], F32)
@@ -58,17 +57,16 @@ def tile_attend_gdistm_hr_kernel(tc, hT, rT, G, tT, hoffs, roffs, offs, out_0, o
         nc.sync.dma_start(grads[:], G.rearrange("(p e) i -> p e i", e=4))
         nc.sync.dma_start(tails[1][:], dealt(tT)[:, 1, :])
         nc.sync.dma_start(tail_list[:], offs)
-        nc.sync.dma_start(tails[0][:], dealt(tT)[:, 0, :])
         nc.sync.dma_start(rel_list[:], roffs)
         nc.sync.dma_start(head_list[:], hoffs)
+        nc.sync.dma_start(tails[0][:], dealt(tT)[:, 0, :])
         nc.sync.dma_start(rels[1][:], dealt(rT)[:, 1, :])
         nc.sync.dma_start(tails[2][:], dealt(tT)[:, 2, :])
         nc.sync.dma_start(tails[3][:], dealt(tT)[:, 3, :])
         nc.sync.dma_start(rels[0][:], dealt(rT)[:, 0, :])
-        nc.sync.dma_start(heads[0][:], dealt(hT)[:, 0, :])
-        nc.sync.dma_start(heads[1][:], dealt(hT)[:, 1, :])
         nc.sync.dma_start(late_rels[:], dealt(rT)[:, 2:4, :])
-        nc.sync.dma_start(late_heads[:], dealt(hT)[:, 2:4, :])
+        nc.sync.dma_start(head_pairs[0][:], dealt(hT)[:, 0:2, :])
+        nc.sync.dma_start(head_pairs[1][:], dealt(hT)[:, 2:4, :])
 
         nc.gpsimd.memset(zeros[:], 0.0)
         nc.gpsimd.affine_select(out=ident[:], in_=zeros[:], compare_op=mybir.AluOpType.not_equal, fill=1.0, base=0,
@@ -155,14 +153,13 @@ def tile_attend_gdistm_hr_kernel(tc, hT, rT, G, tT, hoffs, roffs, offs, out_0, o
         picked0 = pick_on_scalar("t_picked0", tails[0][:], tail_list, BF16)
         turned = leave_turned(kept("t_turned1", [P, 4 * P], BF16), turn(1, picked1), nc.vector.tensor_copy)
         acc1 = product(1, quantise_tails(1, turned, kept("t_codes1", [P, P], U32)))
-        turned = leave_turned(placed("t_turned0", [P, 4 * P], BF16, 3.5), turn(0, picked0), nc.vector.tensor_copy)
-        acc = [product(0, quantise_tails(0, turned, placed("t_codes0", [P, P], U32, 8))), acc1]
+        turned = leave_turned(placed("t_turned0", [P, 4 * P], BF16, 7.5), turn(0, picked0), nc.vector.tensor_copy)
+        acc = [product(0, quantise_tails(0, turned, kept("t_codes0", [P, P], U32))), acc1]
         rels_odd = pick_on_scalar("r0_odd", rels[1][:], rel_list, F32)
         b1 = leave(over("b1", [P, QUERIES], F32, "rels1"), acc[1], nc.scalar.copy)
         put_on_vector(dh[1], head_list, b1, rels_odd)
-        dr = [placed("dr%d" % k, [P, RELATIONS], F32, 4 * k) for k in range(2)]
-        dh.append(placed("dh2", [P, ENTITIES], F32, 8))
-        for window in dr + dh[2:]:
+        dh.extend([placed("dh%d" % k, [P, ENTITIES], F32, 8 * (k - 2)) for k in range(2, BLOCKS)])
+        for window in dh[2:]:
             nc.gpsimd.memset(window[:].bitcast(I32), 0)
 
         picked = [pick_on_scalar("t_picked2", tails[2][:], tail_list, BF16)]
@@ -173,20 +170,20 @@ def tile_attend_gdistm_hr_kernel(tc, hT, rT, G, tT, hoffs, roffs, offs, out_0, o
         put_on_scalar(dh[0], head_list, pick_times("r0_values", rels[0][:], rel_list, b[0]))
         acc.append(product(2, quantise_tails(2, turned2, over("t_codes2", [P, P], U32, "rels0"))))
         acc.append(product(3, quantise_tails(3, turned3, kept("t_codes3", [P, P], U32))))
-        values = pick_times("h0_values", heads[0][:], head_list, b[0])
-        b.append(leave(over("b2", [P, QUERIES], F32, "heads0"), acc[2], nc.vector.tensor_copy))
-        b.append(leave(over("b3", [P, QUERIES], F32, "r0_values"), acc[3], nc.scalar.copy))
-        heads_odd = kept("h0_odd", [P, QUERIES], F32)
-        nc.vector.tensor_copy(heads_odd[:], heads[1][:].indirect(head_list[:]))
-        put_pair((values, heads_odd), rel_list, dr, b[1])
-        dh.append(placed("dh3", [P, ENTITIES], F32, 24))
-        dr.extend([placed("dr%d" % k, [P, RELATIONS], F32, 8 + 4 * k) for k in range(2, BLOCKS)])
-        for window in dh[3:] + dr[2:]:
+        b.append(leave(over("b2", [P, QUERIES], F32, "t_turned3"), acc[2], nc.vector.tensor_copy))
+        b.append(leave(kept("b3", [P, QUERIES], F32), acc[3], nc.vector.tensor_copy))
+        values = pick_times("r1_values", late_rels[:].rearrange("p e c -> p (e c)"), rel_list, b[2])
+        rels_odd = kept("r1_odd", [P, QUERIES], F32)
+        nc.vector.tensor_copy(rels_odd[:, :HALF], late_rels[:, 1, :].indirect(part(rel_list, 0, HALF)))
+        nc.scalar.activation(rels_odd[:, HALF:], late_rels[:, 1, :].indirect(part(rel_list, HALF, QUERIES)), COPY)
+        put_pair((values, rels_odd), head_list, dh[2:], b[3])
+        dr = [placed("dr%d" % k, [P, RELATIONS], F32, 16 + 4 * k) for k in range(BLOCKS - 1)]
+        dr.append(over("dr3", [P, RELATIONS], F32, "r0_values"))
+        for window in dr:
             nc.gpsimd.memset(window[:].bitcast(I32), 0)
-        put_pair(pick_pair("r1", late_rels, rel_list, b[2]), head_list, dh[2:], b[3])
-        put_pair(pick_pair("h1", late_heads, head_list, b[2]), rel_list, dr[2:], b[3])
-
         for j in range(BLOCKS // 2):
-            for out, windows in ((out_0, dh), (out_1, dr)):
-                for k in (2 * j + 1, 2 * j):
-                    nc.sync.dma_start(dealt(out)[:, k, :], windows[k][:])
+            put_pair(pick_pair("h%d" % j, head_pairs[j], head_list, b[2 * j]), rel_list, dr[2 * j:], b[2 * j + 1])
+
+        for out, windows in ((out_0, dh), (out_1, dr)):
+            for k in (1, 0, 3, 2):
+                nc.sync.dma_start(dealt(out)[:, k, :], windows[k][:])

@@ -57,10 +57,10 @@ def tile_attend_gdistm_hr_kernel(tc, hT, rT, G, tT, hoffs, roffs, offs, out_0, o
         nc.sync.dma_start(grads[:], G.rearrange("(p e) i -> p e i", e=4))
         nc.sync.dma_start(tails[1][:], dealt(tT)[:, 1, :])
         nc.sync.dma_start(tail_list[:], offs)
-        nc.sync.dma_start(rel_list[:], roffs)
-        nc.sync.dma_start(head_list[:], hoffs)
         nc.sync.dma_start(tails[0][:], dealt(tT)[:, 0, :])
+        nc.sync.dma_start(rel_list[:], roffs)
         nc.sync.dma_start(rels[1][:], dealt(rT)[:, 1, :])
+        nc.sync.dma_start(head_list[:], hoffs)
         nc.sync.dma_start(tails[2][:], dealt(tT)[:, 2, :])
         nc.sync.dma_start(tails[3][:], dealt(tT)[:, 3, :])
         nc.sync.dma_start(rels[0][:], dealt(rT)[:, 0, :])

@@ -21,6 +21,7 @@ ENTITIES = 2048
 RELATIONS = 1024
 BLOCKS = FEATURES // P
 HALF = QUERIES // 2
+KIB = 1024
 
 FLOPS = 2 * FEATURES * QUERIES * SLOTS
 
@@ -36,35 +37,33 @@ def tile_attend_gdistm_hr_kernel(tc, hT, rT, G, tT, hoffs, roffs, offs, out_0, o
         def kept(name, shape, dtype):
             return held.tile(shape, dtype, name=name, align_bytes=64)
 
-        def placed(name, shape, dtype, kib):
-            return shared.tile(shape, dtype, name=name, align_bytes=64, offset=int(1024 * kib))
+        def placed(name, shape, dtype, offset):
+            return shared.tile(shape, dtype, name=name, align_bytes=64, offset=offset)
 
         def dealt(table):
             return table.rearrange("(p k) c -> p k c", k=BLOCKS)
+
+        def whole(tile):
+            return tile[:].rearrange("p k c -> p (k c)")
 
         tail_list = lists.tile([P, SLOTS // 16], U16, name="tail_list")
         head_list = lists.tile([P, QUERIES // 16], U16, name="head_list")
         rel_list = lists.tile([P, QUERIES // 16], U16, name="rel_list")
 
-        tails = [kept("tails%d" % k, [P, ENTITIES], F32) for k in range(BLOCKS)]
-        head_pairs = [kept("heads%d" % j, [P, 2, ENTITIES], F32) for j in range(BLOCKS // 2)]
-        rels = [kept("rels%d" % k, [P, RELATIONS], F32) for k in range(2)]
-        late_rels = placed("late_rels", [P, 2, RELATIONS], F32, 18)
         grads = kept("grads", [P, 4, SLOTS], F32)
+        tail_pairs = [kept("tails01", [P, 2, ENTITIES], F32), kept("tails23", [P, 2, ENTITIES], F32)]
+        rels = kept("rels", [P, BLOCKS, RELATIONS], F32)
+        head_pairs = [placed("heads01", [P, 2, ENTITIES], F32, 0), kept("heads23", [P, 2, ENTITIES], F32)]
         ident = kept("ident", [P, P], F32)
         zeros = kept("zeros", [P, P], F32)
 
         nc.sync.dma_start(grads[:], G.rearrange("(p e) i -> p e i", e=4))
-        nc.sync.dma_start(tails[1][:], dealt(tT)[:, 1, :])
         nc.sync.dma_start(tail_list[:], offs)
-        nc.sync.dma_start(tails[0][:], dealt(tT)[:, 0, :])
+        nc.sync.dma_start(tail_pairs[0][:], dealt(tT)[:, 0:2, :])
         nc.sync.dma_start(rel_list[:], roffs)
-        nc.sync.dma_start(rels[1][:], dealt(rT)[:, 1, :])
+        nc.sync.dma_start(rels[:], dealt(rT))
         nc.sync.dma_start(head_list[:], hoffs)
-        nc.sync.dma_start(tails[2][:], dealt(tT)[:, 2, :])
-        nc.sync.dma_start(tails[3][:], dealt(tT)[:, 3, :])
-        nc.sync.dma_start(rels[0][:], dealt(rT)[:, 0, :])
-        nc.sync.dma_start(late_rels[:], dealt(rT)[:, 2:4, :])
+        nc.sync.dma_start(tail_pairs[1][:], dealt(tT)[:, 2:4, :])
         nc.sync.dma_start(head_pairs[0][:], dealt(hT)[:, 0:2, :])
         nc.sync.dma_start(head_pairs[1][:], dealt(hT)[:, 2:4, :])
 
@@ -72,36 +71,53 @@ def tile_attend_gdistm_hr_kernel(tc, hT, rT, G, tT, hoffs, roffs, offs, out_0, o
         nc.gpsimd.affine_select(out=ident[:], in_=zeros[:], compare_op=mybir.AluOpType.not_equal, fill=1.0, base=0,
                                 pattern=[[-1, P]], channel_multiplier=1)
 
+        dh = [kept("dh%d" % k, [P, ENTITIES], F32) for k in range(BLOCKS)]
+        for k, window in enumerate(dh):
+            (nc.vector if k < 2 else nc.gpsimd).memset(window[:].bitcast(I32), 0)
+
         def transpose_words(src, bank):
             words = src.bitcast(F32)
             for u in range(2):
                 nc.tensor.transpose(bank[:, u, :], words[:, u::2], ident[:])
 
-        def over(name, shape, dtype, tag):
-            return held.tile(shape, dtype, name=name, tag=tag, align_bytes=64)
+        g_rounded = [kept("g_rounded%d" % j, [P, 2, SLOTS], BF16) for j in range(2)]
+        g_turned = placed("g_turned", [P, 4 * QUERIES], BF16, 36 * KIB)
+        g_codes = kept("g_codes", [P, QUERIES], U32)
+        g_scales = kept("g_scales", [P, QUERIES], U8)
+        g_words = g_turned[:].bitcast(F32).rearrange("p (x j e u) -> p j x e u", j=2, e=2, u=2)
+        for j in range(2):
+            nc.vector.tensor_copy(g_rounded[j][:], grads[:, 2 * j:2 * j + 2, :])
+        for j, copy in enumerate((nc.scalar.copy, nc.vector.tensor_copy)):
+            bank = banks.tile([P, 2, 2, P], F32, name="g_bank", tag="g%d" % j)
+            for e in range(2):
+                transpose_words(g_rounded[j][:, e, :], bank[:, e])
+            copy(g_words[:, j], bank[:].rearrange("p e u x -> p x e u"))
+        nc.vector.quantize_mx(out=g_codes[:].bitcast(E5M2X4), scales=g_scales[:], in_=g_turned[:])
 
-        def pick_on_scalar(name, window, offsets, dtype, tag=None):
-            picked = over(name, [P, QUERIES], dtype, tag or name)
-            nc.scalar.activation(picked[:], window.indirect(offsets[:]), COPY)
-            return picked
+        def pick_tails(j, kib):
+            even = placed("t_picked%d" % (2 * j), [P, SLOTS], BF16, kib * KIB)
+            odd = placed("t_picked%d" % (2 * j + 1), [P, 2, P, 2], BF16, (kib + 1) * KIB)
+            nc.scalar.activation(even[:], whole(tail_pairs[j]).indirect(tail_list[:]), COPY)
+            nc.vector.tensor_copy(odd[:].rearrange("p u x e -> p x u e"), tail_pairs[j][:, 1, :].indirect(tail_list[:]))
+            return even, odd
 
-        def turn(k, picked):
-            bank = banks.tile([P, 2, P], F32, name="t_bank", tag="turn%d" % (k % 2))
-            transpose_words(picked[:], bank[:])
-            return bank
+        def turn_tails(even, odd):
+            pair = [banks.tile([P, 2, P], F32, name="t_bank", tag="turn%d" % e) for e in range(2)]
+            odd_words = odd[:].rearrange("p u x e -> p u (x e)").bitcast(F32)
+            for u in range(2):
+                nc.tensor.transpose(pair[1][:, u, :], odd_words[:, u, :], ident[:])
+            transpose_words(even[:], pair[0][:])
+            return pair
 
-        def leave_turned(turned, bank, copy):
+        def leave_turned(k, offset, bank, copy):
+            turned = placed("t_turned%d" % k, [P, 4 * P], BF16, offset)
             copy(turned[:].bitcast(F32).rearrange("p (x u) -> p x u", u=2), bank[:].rearrange("p u x -> p x u"))
-            return turned
+            return turned[:]
 
-        def quantise_tails(k, turned, codes):
-            scales = kept("t_scales%d" % k, [P, P], U8)
-            nc.vector.quantize_mx(out=codes[:].bitcast(E4M3X4), scales=scales[:], in_=turned[:])
-            return codes, scales
-
-        def product(k, operand):
+        def product(k, turned, codes, scales):
+            nc.vector.quantize_mx(out=codes[:].bitcast(E4M3X4), scales=scales[:], in_=turned)
             acc = banks.tile([P, QUERIES], F32, name="acc", tag="acc%d" % k)
-            nc.tensor.matmul_mx(out=acc[:], lhsT=operand[0][:].bitcast(E4M3X4), lhsT_scale=operand[1][:],
+            nc.tensor.matmul_mx(out=acc[:], lhsT=codes[:].bitcast(E4M3X4), lhsT_scale=scales[:],
                                 rhs=g_codes[:].bitcast(E5M2X4), rhs_scale=g_scales[:], start=True, stop=True)
             return acc
 
@@ -109,81 +125,72 @@ def tile_attend_gdistm_hr_kernel(tc, hT, rT, G, tT, hoffs, roffs, offs, out_0, o
             copy(b[:], acc[:])
             return b
 
-        def part(offsets, first, last):
-            return offsets[:, first // 16:last // 16]
-
-        def pick_times(name, window, pick_list, b_even):
-            values = kept(name, [P, QUERIES], F32)
+        def pick_times(values, window, pick_list, b_even):
             nc.vector.tensor_tensor(values[:], window.indirect(pick_list[:]), b_even[:], MULT)
             return values
 
-        def pick_pair(name, pair, pick_list, b_even):
-            values = pick_times(name + "_values", pair[:].rearrange("p e c -> p (e c)"), pick_list, b_even)
-            return values, pick_on_scalar(name + "_odd", pair[:, 1, :], pick_list, F32)
+        def pick_on_scalar(picked, window, pick_list):
+            nc.scalar.activation(picked[:], window.indirect(pick_list[:]), COPY)
+            return picked
 
-        def put_on_vector(window, put_list, b_odd, odd):
-            nc.vector.tensor_tensor(window[:].indirect(put_list[:]), b_odd[:], odd[:], MULT)
+        def put_on_vector(window, put_list, b_block, picked):
+            nc.vector.tensor_tensor(window[:].indirect(put_list[:]), b_block[:], picked, MULT)
 
         def put_on_scalar(window, put_list, values):
             for first, last in ((0, HALF), (HALF, QUERIES)):
-                nc.scalar.activation(window[:].indirect(part(put_list, first, last)), values[:, first:last], COPY)
+                nc.scalar.activation(window[:].indirect(put_list[:, first // 16:last // 16]), values[:, first:last], COPY)
 
-        def put_pair(picked, put_list, windows, b_odd):
-            put_on_vector(windows[1], put_list, b_odd, picked[1])
-            put_on_scalar(windows[0], put_list, picked[0])
+        def column(name, kib=None):
+            return kept(name, [P, QUERIES], F32) if kib is None else placed(name, [P, QUERIES], F32, kib * KIB)
 
-        dh = [kept("dh%d" % k, [P, ENTITIES], F32) for k in range(2)]
-        for window in dh:
-            nc.vector.memset(window[:].bitcast(I32), 0)
+        turned = turn_tails(*pick_tails(0, 36))
+        turned1 = leave_turned(1, 52 * KIB, turned[1], nc.vector.tensor_copy)
+        turned0 = leave_turned(0, 40 * KIB, turned[0], nc.scalar.copy)
+        acc1 = product(1, turned1, kept("t_codes1", [P, P], U32), kept("t_scales1", [P, P], U8))
+        acc0 = product(0, turned0, placed("t_codes0", [P, P], U32, 46 * KIB), placed("t_scales0", [P, P], U8, 20 * KIB - 64))
+        b1 = leave(column("b1"), acc1, nc.vector.tensor_copy)
+        b0 = leave(column("b0", 35), acc0, nc.vector.tensor_copy)
+        rels012 = placed("r012_picked", [P, 3, QUERIES], F32, 40 * KIB)
+        rels3 = column("r3_picked", 46)
+        for k in (1, 0, 2):
+            nc.scalar.activation(rels012[:, k, :], rels[:, k, :].indirect(rel_list[:]), COPY)
+        nc.vector.tensor_copy(rels3[:, :HALF], rels[:, 3, :].indirect(rel_list[:, :HALF // 16]))
+        nc.scalar.activation(rels3[:, HALF:], rels[:, 3, :].indirect(rel_list[:, HALF // 16:]), COPY)
+        put_on_vector(dh[1], head_list, b1, rels012[:, 1, :])
+        put_on_vector(dh[0], head_list, b0, rels012[:, 0, :])
 
-        g_rounded = [kept("g_rounded%d" % j, [P, 2, SLOTS], BF16) for j in range(2)]
-        g_turned = kept("g_turned", [P, 4 * QUERIES], BF16)
-        g_codes = kept("g_codes", [P, QUERIES], U32)
-        g_scales = kept("g_scales", [P, QUERIES], U8)
-        for j in range(2):
-            nc.vector.tensor_copy(g_rounded[j][:], grads[:, 2 * j:2 * j + 2, :])
-        g_words = g_turned[:].bitcast(F32).rearrange("p (x j e u) -> p j x e u", j=2, e=2, u=2)
-        for j, copy in enumerate((nc.scalar.copy, nc.vector.tensor_copy)):
-            bank = banks.tile([P, 2, 2, P], F32, name="g_bank", tag="g%d" % j)
-            for e in range(2):
-                transpose_words(g_rounded[j][:, e, :], bank[:, e])
-            copy(g_words[:, j], bank[:].rearrange("p e u x -> p x e u"))
-        nc.vector.quantize_mx(out=g_codes[:].bitcast(E5M2X4), scales=g_scales[:], in_=g_turned[:])
-        picked1 = pick_on_scalar("t_picked1", tails[1][:], tail_list, BF16, "g_rounded0")
-        picked0 = pick_on_scalar("t_picked0", tails[0][:], tail_list, BF16)
-        turned = leave_turned(kept("t_turned1", [P, 4 * P], BF16), turn(1, picked1), nc.vector.tensor_copy)
-        acc1 = product(1, quantise_tails(1, turned, kept("t_codes1", [P, P], U32)))
-        turned = leave_turned(placed("t_turned0", [P, 4 * P], BF16, 7.5), turn(0, picked0), nc.vector.tensor_copy)
-        acc = [product(0, quantise_tails(0, turned, kept("t_codes0", [P, P], U32))), acc1]
-        rels_odd = pick_on_scalar("r0_odd", rels[1][:], rel_list, F32)
-        b1 = leave(over("b1", [P, QUERIES], F32, "rels1"), acc[1], nc.scalar.copy)
-        put_on_vector(dh[1], head_list, b1, rels_odd)
-        dh.extend([placed("dh%d" % k, [P, ENTITIES], F32, 8 * (k - 2)) for k in range(2, BLOCKS)])
-        for window in dh[2:]:
-            nc.gpsimd.memset(window[:].bitcast(I32), 0)
+        picked3 = pick_on_scalar(column("t_picked3"), tail_pairs[1][:, 1, :], tail_list)
+        picked2 = pick_on_scalar(kept("t_picked2", [P, SLOTS], BF16), whole(tail_pairs[1]), tail_list)
+        bank3 = banks.tile([P, 4, P], F32, name="t_bank", tag="g0")
+        for t in range(4):
+            nc.tensor.transpose(bank3[:, t, :], picked3[:, t::4], ident[:])
+        bank2 = banks.tile([P, 2, P], F32, name="t_bank", tag="turn0")
+        transpose_words(picked2[:], bank2[:])
+        turned3 = placed("t_turned3", [P, P, 4], BF16, 50 * KIB)
+        nc.scalar.copy(turned3[:], bank3[:].rearrange("p t x -> p x t"))
+        turned2 = leave_turned(2, 48 * KIB, bank2, nc.scalar.copy)
+        acc3 = product(3, turned3[:].rearrange("p x t -> p (x t)"), kept("t_codes3", [P, P], U32),
+                       kept("t_scales3", [P, P], U8))
+        acc2 = product(2, turned2, kept("t_codes2", [P, P], U32), kept("t_scales2", [P, P], U8))
+        heads0 = pick_times(column("h0_values"), whole(head_pairs[0]), head_list, b0)
+        heads1 = pick_on_scalar(column("h1_picked", 50), head_pairs[0][:, 1, :], head_list)
+        values3 = column("r3_values", 35)
+        nc.vector.tensor_tensor(values3[:], acc3[:], rels3[:], MULT)
+        b2 = leave(column("b2", 8), acc2, nc.scalar.copy)
+        b3 = leave(column("b3", 10), acc3, nc.vector.tensor_copy)
+        put_on_vector(dh[2], head_list, b2, rels012[:, 2, :])
+        put_on_scalar(dh[3], head_list, values3)
+        heads3 = pick_on_scalar(column("h3_picked", 46), head_pairs[1][:, 1, :], head_list)
+        heads2 = pick_times(column("h2_values"), whole(head_pairs[1]), head_list, b2)
+        dr = {}
+        for k, kib in ((2, 16), (3, 20), (0, 0), (1, 4)):
+            dr[k] = placed("dr%d" % k, [P, RELATIONS], F32, kib * KIB)
+            nc.gpsimd.memset(dr[k][:].bitcast(I32), 0)
+        put_on_vector(dr[1], rel_list, b1, heads1[:])
+        put_on_scalar(dr[0], rel_list, heads0)
+        put_on_vector(dr[3], rel_list, b3, heads3[:])
+        put_on_scalar(dr[2], rel_list, heads2)
 
-        picked = [pick_on_scalar("t_picked2", tails[2][:], tail_list, BF16)]
-        b = [leave(over("b0", [P, QUERIES], F32, "tails2"), acc[0], nc.scalar.copy), b1]
-        picked.append(pick_on_scalar("t_picked3", tails[3][:], tail_list, BF16))
-        turned2 = leave_turned(over("t_turned2", [P, 4 * P], BF16, "tails3"), turn(2, picked[0]), nc.scalar.copy)
-        turned3 = leave_turned(kept("t_turned3", [P, 4 * P], BF16), turn(3, picked[1]), nc.scalar.copy)
-        put_on_scalar(dh[0], head_list, pick_times("r0_values", rels[0][:], rel_list, b[0]))
-        acc.append(product(2, quantise_tails(2, turned2, over("t_codes2", [P, P], U32, "rels0"))))
-        acc.append(product(3, quantise_tails(3, turned3, kept("t_codes3", [P, P], U32))))
-        b.append(leave(over("b2", [P, QUERIES], F32, "t_turned3"), acc[2], nc.vector.tensor_copy))
-        b.append(leave(kept("b3", [P, QUERIES], F32), acc[3], nc.vector.tensor_copy))
-        values = pick_times("r1_values", late_rels[:].rearrange("p e c -> p (e c)"), rel_list, b[2])
-        rels_odd = kept("r1_odd", [P, QUERIES], F32)
-        nc.vector.tensor_copy(rels_odd[:, :HALF], late_rels[:, 1, :].indirect(part(rel_list, 0, HALF)))
-        nc.scalar.activation(rels_odd[:, HALF:], late_rels[:, 1, :].indirect(part(rel_list, HALF, QUERIES)), COPY)
-        put_pair((values, rels_odd), head_list, dh[2:], b[3])
-        dr = [placed("dr%d" % k, [P, RELATIONS], F32, 16 + 4 * k) for k in range(BLOCKS - 1)]
-        dr.append(over("dr3", [P, RELATIONS], F32, "r0_values"))
-        for window in dr:
-            nc.gpsimd.memset(window[:].bitcast(I32), 0)
-        for j in range(BLOCKS // 2):
-            put_pair(pick_pair("h%d" % j, head_pairs[j], head_list, b[2 * j]), rel_list, dr[2 * j:], b[2 * j + 1])
-
-        for out, windows in ((out_0, dh), (out_1, dr)):
-            for k in (1, 0, 3, 2):
+        for out, windows, order in ((out_0, dh, (1, 0, 2, 3)), (out_1, dr, (0, 1, 3, 2))):
+            for k in order:
                 nc.sync.dma_start(dealt(out)[:, k, :], windows[k][:])

@@ -35,10 +35,10 @@ def tile_attend_gdistm_hr_kernel(tc, hT, rT, G, tT, hoffs, roffs, offs, out_0, o
         banks = ctx.enter_context(tc.psum_pool(name="banks", bufs=1))
 
         def kept(name, shape, dtype):
-            return held.tile(shape, dtype, name=name, align_bytes=64)
+            return held.tile(shape, dtype, name=name, align_bytes=256)
 
         def placed(name, shape, dtype, offset):
-            return shared.tile(shape, dtype, name=name, align_bytes=64, offset=offset)
+            return shared.tile(shape, dtype, name=name, align_bytes=256, offset=offset)
 
         def dealt(table):
             return table.rearrange("(p k) c -> p k c", k=BLOCKS)
@@ -46,24 +46,27 @@ def tile_attend_gdistm_hr_kernel(tc, hT, rT, G, tT, hoffs, roffs, offs, out_0, o
         def whole(tile):
             return tile[:].rearrange("p k c -> p (k c)")
 
-        tail_list = lists.tile([P, SLOTS // 16], U16, name="tail_list")
-        head_list = lists.tile([P, QUERIES // 16], U16, name="head_list")
-        rel_list = lists.tile([P, QUERIES // 16], U16, name="rel_list")
+        tail_list = lists.tile([P, SLOTS // 16], U16, name="tail_list", align_bytes=256)
+        head_list = lists.tile([P, QUERIES // 16], U16, name="head_list", align_bytes=256)
+        rel_list = lists.tile([P, QUERIES // 16], U16, name="rel_list", align_bytes=256)
 
         grads = kept("grads", [P, 4, SLOTS], F32)
-        tail_pairs = [kept("tails01", [P, 2, ENTITIES], F32), kept("tails23", [P, 2, ENTITIES], F32)]
-        rels = kept("rels", [P, BLOCKS, RELATIONS], F32)
-        head_pairs = [placed("heads01", [P, 2, ENTITIES], F32, 0), kept("heads23", [P, 2, ENTITIES], F32)]
+        tails = [kept("tails%d" % k, [P, ENTITIES], F32) for k in range(2)]
+        late_tails = kept("tails23", [P, 2, ENTITIES], F32)
+        rel_pairs = [kept("rels%d" % j, [P, 2, RELATIONS], F32) for j in range(BLOCKS // 2)]
+        head_pairs = [kept("heads%d" % j, [P, 2, ENTITIES], F32) for j in range(BLOCKS // 2)]
         ident = kept("ident", [P, P], F32)
         zeros = kept("zeros", [P, P], F32)
 
         nc.sync.dma_start(grads[:], G.rearrange("(p e) i -> p e i", e=4))
+        nc.sync.dma_start(tails[1][:], dealt(tT)[:, 1, :])
         nc.sync.dma_start(tail_list[:], offs)
-        nc.sync.dma_start(tail_pairs[0][:], dealt(tT)[:, 0:2, :])
+        nc.sync.dma_start(tails[0][:], dealt(tT)[:, 0, :])
         nc.sync.dma_start(rel_list[:], roffs)
-        nc.sync.dma_start(rels[:], dealt(rT))
+        nc.sync.dma_start(rel_pairs[0][:], dealt(rT)[:, 0:2, :])
         nc.sync.dma_start(head_list[:], hoffs)
-        nc.sync.dma_start(tail_pairs[1][:], dealt(tT)[:, 2:4, :])
+        nc.sync.dma_start(late_tails[:], dealt(tT)[:, 2:4, :])
+        nc.sync.dma_start(rel_pairs[1][:], dealt(rT)[:, 2:4, :])
         nc.sync.dma_start(head_pairs[0][:], dealt(hT)[:, 0:2, :])
         nc.sync.dma_start(head_pairs[1][:], dealt(hT)[:, 2:4, :])
 
@@ -71,17 +74,17 @@ def tile_attend_gdistm_hr_kernel(tc, hT, rT, G, tT, hoffs, roffs, offs, out_0, o
         nc.gpsimd.affine_select(out=ident[:], in_=zeros[:], compare_op=mybir.AluOpType.not_equal, fill=1.0, base=0,
                                 pattern=[[-1, P]], channel_multiplier=1)
 
-        dh = [kept("dh%d" % k, [P, ENTITIES], F32) for k in range(BLOCKS)]
-        for k, window in enumerate(dh):
-            (nc.vector if k < 2 else nc.gpsimd).memset(window[:].bitcast(I32), 0)
+        dh = [kept("dh%d" % k, [P, ENTITIES], F32) for k in range(2)]
+        for window in dh:
+            nc.vector.memset(window[:].bitcast(I32), 0)
 
         def transpose_words(src, bank):
             words = src.bitcast(F32)
             for u in range(2):
                 nc.tensor.transpose(bank[:, u, :], words[:, u::2], ident[:])
 
-        g_rounded = [kept("g_rounded%d" % j, [P, 2, SLOTS], BF16) for j in range(2)]
-        g_turned = placed("g_turned", [P, 4 * QUERIES], BF16, 36 * KIB)
+        g_rounded = [placed("g_rounded%d" % j, [P, 2, SLOTS], BF16, (16 + 2 * j) * KIB) for j in range(2)]
+        g_turned = kept("g_turned", [P, 4 * QUERIES], BF16)
         g_codes = kept("g_codes", [P, QUERIES], U32)
         g_scales = kept("g_scales", [P, QUERIES], U8)
         g_words = g_turned[:].bitcast(F32).rearrange("p (x j e u) -> p j x e u", j=2, e=2, u=2)
@@ -94,20 +97,10 @@ def tile_attend_gdistm_hr_kernel(tc, hT, rT, G, tT, hoffs, roffs, offs, out_0, o
             copy(g_words[:, j], bank[:].rearrange("p e u x -> p x e u"))
         nc.vector.quantize_mx(out=g_codes[:].bitcast(E5M2X4), scales=g_scales[:], in_=g_turned[:])
 
-        def pick_tails(j, kib):
-            even = placed("t_picked%d" % (2 * j), [P, SLOTS], BF16, kib * KIB)
-            odd = placed("t_picked%d" % (2 * j + 1), [P, 2, P, 2], BF16, (kib + 1) * KIB)
-            nc.scalar.activation(even[:], whole(tail_pairs[j]).indirect(tail_list[:]), COPY)
-            nc.vector.tensor_copy(odd[:].rearrange("p u x e -> p x u e"), tail_pairs[j][:, 1, :].indirect(tail_list[:]))
-            return even, odd
-
-        def turn_tails(even, odd):
-            pair = [banks.tile([P, 2, P], F32, name="t_bank", tag="turn%d" % e) for e in range(2)]
-            odd_words = odd[:].rearrange("p u x e -> p u (x e)").bitcast(F32)
-            for u in range(2):
-                nc.tensor.transpose(pair[1][:, u, :], odd_words[:, u, :], ident[:])
-            transpose_words(even[:], pair[0][:])
-            return pair
+        def turn(k, picked):
+            bank = banks.tile([P, 2, P], F32, name="t_bank", tag="turn%d" % (k % 2))
+            transpose_words(picked[:], bank[:])
+            return bank
 
         def leave_turned(k, offset, bank, copy):
             turned = placed("t_turned%d" % k, [P, 4 * P], BF16, offset)
@@ -143,54 +136,53 @@ def tile_attend_gdistm_hr_kernel(tc, hT, rT, G, tT, hoffs, roffs, offs, out_0, o
         def column(name, kib=None):
             return kept(name, [P, QUERIES], F32) if kib is None else placed(name, [P, QUERIES], F32, kib * KIB)
 
-        turned = turn_tails(*pick_tails(0, 36))
-        turned1 = leave_turned(1, 52 * KIB, turned[1], nc.vector.tensor_copy)
-        turned0 = leave_turned(0, 40 * KIB, turned[0], nc.scalar.copy)
+        picked1 = pick_on_scalar(placed("t_picked1", [P, SLOTS], BF16, 16 * KIB), tails[1][:], tail_list)
+        picked0 = pick_on_scalar(placed("t_picked0", [P, SLOTS], BF16, 18 * KIB), tails[0][:], tail_list)
+        turned1 = leave_turned(1, 22 * KIB, turn(1, picked1), nc.vector.tensor_copy)
         acc1 = product(1, turned1, kept("t_codes1", [P, P], U32), kept("t_scales1", [P, P], U8))
-        acc0 = product(0, turned0, placed("t_codes0", [P, P], U32, 46 * KIB), placed("t_scales0", [P, P], U8, 20 * KIB - 64))
-        b1 = leave(column("b1"), acc1, nc.vector.tensor_copy)
-        b0 = leave(column("b0", 35), acc0, nc.vector.tensor_copy)
-        rels012 = placed("r012_picked", [P, 3, QUERIES], F32, 40 * KIB)
-        rels3 = column("r3_picked", 46)
-        for k in (1, 0, 2):
-            nc.scalar.activation(rels012[:, k, :], rels[:, k, :].indirect(rel_list[:]), COPY)
-        nc.vector.tensor_copy(rels3[:, :HALF], rels[:, 3, :].indirect(rel_list[:, :HALF // 16]))
-        nc.scalar.activation(rels3[:, HALF:], rels[:, 3, :].indirect(rel_list[:, HALF // 16:]), COPY)
-        put_on_vector(dh[1], head_list, b1, rels012[:, 1, :])
-        put_on_vector(dh[0], head_list, b0, rels012[:, 0, :])
+        turned0 = leave_turned(0, 40 * KIB - 512, turn(0, picked0), nc.vector.tensor_copy)
+        b1 = leave(column("b1", 18), acc1, nc.vector.tensor_copy)
+        acc0 = product(0, turned0, kept("t_codes0", [P, P], U32), kept("t_scales0", [P, P], U8))
+        rels1 = pick_on_scalar(column("r1_picked"), rel_pairs[0][:, 1, :], rel_list)
+        rels0 = pick_on_scalar(column("r0_picked"), rel_pairs[0][:, 0, :], rel_list)
+        b0 = leave(column("b0"), acc0, nc.scalar.copy)
+        put_on_vector(dh[1], head_list, b1, rels1[:])
+        put_on_vector(dh[0], head_list, b0, rels0[:])
+        dh.extend([placed("dh%d" % k, [P, ENTITIES], F32, (16 + 8 * k) * KIB) for k in range(2, BLOCKS)])
+        for window in dh[2:]:
+            nc.gpsimd.memset(window[:].bitcast(I32), 0)
 
-        picked3 = pick_on_scalar(column("t_picked3"), tail_pairs[1][:, 1, :], tail_list)
-        picked2 = pick_on_scalar(kept("t_picked2", [P, SLOTS], BF16), whole(tail_pairs[1]), tail_list)
+        picked3 = pick_on_scalar(column("t_picked3"), late_tails[:, 1, :], tail_list)
+        picked2 = pick_on_scalar(placed("t_picked2", [P, SLOTS], BF16, 24 * KIB), whole(late_tails), tail_list)
         bank3 = banks.tile([P, 4, P], F32, name="t_bank", tag="g0")
         for t in range(4):
             nc.tensor.transpose(bank3[:, t, :], picked3[:, t::4], ident[:])
-        bank2 = banks.tile([P, 2, P], F32, name="t_bank", tag="turn0")
-        transpose_words(picked2[:], bank2[:])
-        turned3 = placed("t_turned3", [P, P, 4], BF16, 50 * KIB)
+        bank2 = turn(2, picked2)
+        turned3 = placed("t_turned3", [P, P, 4], BF16, 26 * KIB)
         nc.scalar.copy(turned3[:], bank3[:].rearrange("p t x -> p x t"))
-        turned2 = leave_turned(2, 48 * KIB, bank2, nc.scalar.copy)
+        turned2 = leave_turned(2, 4 * KIB - 512, bank2, nc.scalar.copy)
         acc3 = product(3, turned3[:].rearrange("p x t -> p (x t)"), kept("t_codes3", [P, P], U32),
                        kept("t_scales3", [P, P], U8))
-        acc2 = product(2, turned2, kept("t_codes2", [P, P], U32), kept("t_scales2", [P, P], U8))
-        heads0 = pick_times(column("h0_values"), whole(head_pairs[0]), head_list, b0)
-        heads1 = pick_on_scalar(column("h1_picked", 50), head_pairs[0][:, 1, :], head_list)
-        values3 = column("r3_values", 35)
+        acc2 = product(2, turned2, placed("t_codes2", [P, P], U32, 12 * KIB - 256), kept("t_scales2", [P, P], U8))
+        rels3 = pick_on_scalar(column("r3_picked", 24), rel_pairs[1][:, 1, :], rel_list)
+        rels2 = column("r2_picked", 26)
+        nc.vector.tensor_copy(rels2[:, :HALF], rel_pairs[1][:, 0, :].indirect(rel_list[:, :HALF // 16]))
+        nc.scalar.activation(rels2[:, HALF:], rel_pairs[1][:, 0, :].indirect(rel_list[:, HALF // 16:]), COPY)
+        values3 = column("r3_values")
         nc.vector.tensor_tensor(values3[:], acc3[:], rels3[:], MULT)
-        b2 = leave(column("b2", 8), acc2, nc.scalar.copy)
-        b3 = leave(column("b3", 10), acc3, nc.vector.tensor_copy)
-        put_on_vector(dh[2], head_list, b2, rels012[:, 2, :])
+        b2 = leave(column("b2"), acc2, nc.scalar.copy)
+        b3 = leave(column("b3"), acc3, nc.vector.tensor_copy)
+        put_on_vector(dh[2], head_list, b2, rels2[:])
         put_on_scalar(dh[3], head_list, values3)
-        heads3 = pick_on_scalar(column("h3_picked", 46), head_pairs[1][:, 1, :], head_list)
-        heads2 = pick_times(column("h2_values"), whole(head_pairs[1]), head_list, b2)
-        dr = {}
-        for k, kib in ((2, 16), (3, 20), (0, 0), (1, 4)):
-            dr[k] = placed("dr%d" % k, [P, RELATIONS], F32, kib * KIB)
-            nc.gpsimd.memset(dr[k][:].bitcast(I32), 0)
-        put_on_vector(dr[1], rel_list, b1, heads1[:])
-        put_on_scalar(dr[0], rel_list, heads0)
-        put_on_vector(dr[3], rel_list, b3, heads3[:])
-        put_on_scalar(dr[2], rel_list, heads2)
+        dr = [placed("dr%d" % k, [P, RELATIONS], F32, 4 * k * KIB) for k in range(BLOCKS)]
+        for window in dr:
+            nc.gpsimd.memset(window[:].bitcast(I32), 0)
+        for j, (b_even, b_odd) in enumerate(((b0, b1), (b2, b3))):
+            values = pick_times(column("h%d_values" % (2 * j)), whole(head_pairs[j]), head_list, b_even)
+            odd = pick_on_scalar(column("h%d_picked" % (2 * j + 1)), head_pairs[j][:, 1, :], head_list)
+            put_on_vector(dr[2 * j + 1], rel_list, b_odd, odd[:])
+            put_on_scalar(dr[2 * j], rel_list, values)
 
-        for out, windows, order in ((out_0, dh, (1, 0, 2, 3)), (out_1, dr, (0, 1, 3, 2))):
+        for out, windows, order in ((out_0, dh, (1, 0, 2, 3)), (out_1, dr, (1, 0, 2, 3))):
             for k in order:
                 nc.sync.dma_start(dealt(out)[:, k, :], windows[k][:])

@@ -66,8 +66,8 @@ def tile_attend_gdistm_hr_kernel(tc, hT, rT, G, tT, hoffs, roffs, offs, out_0, o
         nc.sync.dma_start(rel_pairs[0][:], dealt(rT)[:, 0:2, :])
         nc.sync.dma_start(head_list[:], hoffs)
         nc.sync.dma_start(late_tails[:], dealt(tT)[:, 2:4, :])
-        nc.sync.dma_start(rel_pairs[1][:], dealt(rT)[:, 2:4, :])
         nc.sync.dma_start(head_pairs[0][:], dealt(hT)[:, 0:2, :])
+        nc.sync.dma_start(rel_pairs[1][:], dealt(rT)[:, 2:4, :])
         nc.sync.dma_start(head_pairs[1][:], dealt(hT)[:, 2:4, :])
 
         nc.gpsimd.memset(zeros[:], 0.0)
@@ -129,9 +129,13 @@ def tile_attend_gdistm_hr_kernel(tc, hT, rT, G, tT, hoffs, roffs, offs, out_0, o
         def put_on_vector(window, put_list, b_block, picked):
             nc.vector.tensor_tensor(window[:].indirect(put_list[:]), b_block[:], picked, MULT)
 
+        def put_half(window, put_list, values, first):
+            nc.scalar.activation(window[:].indirect(put_list[:, first // 16:(first + HALF) // 16]),
+                                 values[:, first:first + HALF], COPY)
+
         def put_on_scalar(window, put_list, values):
-            for first, last in ((0, HALF), (HALF, QUERIES)):
-                nc.scalar.activation(window[:].indirect(put_list[:, first // 16:last // 16]), values[:, first:last], COPY)
+            for first in (0, HALF):
+                put_half(window, put_list, values, first)
 
         def column(name, kib=None):
             return kept(name, [P, QUERIES], F32) if kib is None else placed(name, [P, QUERIES], F32, kib * KIB)
@@ -140,49 +144,52 @@ def tile_attend_gdistm_hr_kernel(tc, hT, rT, G, tT, hoffs, roffs, offs, out_0, o
         picked0 = pick_on_scalar(placed("t_picked0", [P, SLOTS], BF16, 18 * KIB), tails[0][:], tail_list)
         turned1 = leave_turned(1, 22 * KIB, turn(1, picked1), nc.vector.tensor_copy)
         acc1 = product(1, turned1, kept("t_codes1", [P, P], U32), kept("t_scales1", [P, P], U8))
-        turned0 = leave_turned(0, 40 * KIB - 512, turn(0, picked0), nc.vector.tensor_copy)
+        turned0 = leave_turned(0, 4 * KIB - 512, turn(0, picked0), nc.vector.tensor_copy)
         b1 = leave(column("b1", 18), acc1, nc.vector.tensor_copy)
         acc0 = product(0, turned0, kept("t_codes0", [P, P], U32), kept("t_scales0", [P, P], U8))
         rels1 = pick_on_scalar(column("r1_picked"), rel_pairs[0][:, 1, :], rel_list)
         rels0 = pick_on_scalar(column("r0_picked"), rel_pairs[0][:, 0, :], rel_list)
-        b0 = leave(column("b0"), acc0, nc.scalar.copy)
+        b0 = leave(column("b0", 25), acc0, nc.scalar.copy)
         put_on_vector(dh[1], head_list, b1, rels1[:])
         put_on_vector(dh[0], head_list, b0, rels0[:])
-        dh.extend([placed("dh%d" % k, [P, ENTITIES], F32, (16 + 8 * k) * KIB) for k in range(2, BLOCKS)])
-        for window in dh[2:]:
+        dr = [placed("dr%d" % k, [P, RELATIONS], F32, 4 * k * KIB) for k in range(2)]
+        for window in dr:
             nc.gpsimd.memset(window[:].bitcast(I32), 0)
 
         picked3 = pick_on_scalar(column("t_picked3"), late_tails[:, 1, :], tail_list)
-        picked2 = pick_on_scalar(placed("t_picked2", [P, SLOTS], BF16, 24 * KIB), whole(late_tails), tail_list)
+        picked2 = pick_on_scalar(kept("t_picked2", [P, SLOTS], BF16), whole(late_tails), tail_list)
         bank3 = banks.tile([P, 4, P], F32, name="t_bank", tag="g0")
         for t in range(4):
             nc.tensor.transpose(bank3[:, t, :], picked3[:, t::4], ident[:])
         bank2 = turn(2, picked2)
-        turned3 = placed("t_turned3", [P, P, 4], BF16, 26 * KIB)
+        turned3 = kept("t_turned3", [P, P, 4], BF16)
         nc.scalar.copy(turned3[:], bank3[:].rearrange("p t x -> p x t"))
-        turned2 = leave_turned(2, 4 * KIB - 512, bank2, nc.scalar.copy)
+        turned2 = leave_turned(2, 40 * KIB - 512, bank2, nc.scalar.copy)
         acc3 = product(3, turned3[:].rearrange("p x t -> p (x t)"), kept("t_codes3", [P, P], U32),
                        kept("t_scales3", [P, P], U8))
         acc2 = product(2, turned2, placed("t_codes2", [P, P], U32, 12 * KIB - 256), kept("t_scales2", [P, P], U8))
-        rels3 = pick_on_scalar(column("r3_picked", 24), rel_pairs[1][:, 1, :], rel_list)
-        rels2 = column("r2_picked", 26)
-        nc.vector.tensor_copy(rels2[:, :HALF], rel_pairs[1][:, 0, :].indirect(rel_list[:, :HALF // 16]))
-        nc.scalar.activation(rels2[:, HALF:], rel_pairs[1][:, 0, :].indirect(rel_list[:, HALF // 16:]), COPY)
-        values3 = column("r3_values")
-        nc.vector.tensor_tensor(values3[:], acc3[:], rels3[:], MULT)
-        b2 = leave(column("b2"), acc2, nc.scalar.copy)
-        b3 = leave(column("b3"), acc3, nc.vector.tensor_copy)
-        put_on_vector(dh[2], head_list, b2, rels2[:])
-        put_on_scalar(dh[3], head_list, values3)
-        dr = [placed("dr%d" % k, [P, RELATIONS], F32, 4 * k * KIB) for k in range(BLOCKS)]
-        for window in dr:
+        dh.extend([placed("dh%d" % k, [P, ENTITIES], F32, (16 + 8 * k) * KIB) for k in range(2, BLOCKS)])
+        dr.extend([placed("dr%d" % k, [P, RELATIONS], F32, 4 * k * KIB) for k in range(2, BLOCKS)])
+        for window in dh[2:] + dr[2:]:
             nc.gpsimd.memset(window[:].bitcast(I32), 0)
-        for j, (b_even, b_odd) in enumerate(((b0, b1), (b2, b3))):
-            values = pick_times(column("h%d_values" % (2 * j)), whole(head_pairs[j]), head_list, b_even)
-            odd = pick_on_scalar(column("h%d_picked" % (2 * j + 1)), head_pairs[j][:, 1, :], head_list)
-            put_on_vector(dr[2 * j + 1], rel_list, b_odd, odd[:])
-            put_on_scalar(dr[2 * j], rel_list, values)
 
-        for out, windows, order in ((out_0, dh, (1, 0, 2, 3)), (out_1, dr, (1, 0, 2, 3))):
-            for k in order:
-                nc.sync.dma_start(dealt(out)[:, k, :], windows[k][:])
+        def pick_pair(name, pair, pick_list, b_even):
+            values = pick_times(column(name + "_values"), whole(pair), pick_list, b_even)
+            return values, pick_on_scalar(column(name + "_odd"), pair[:, 1, :], pick_list)
+
+        def put_pair(picked, put_list, windows, b_odd):
+            put_on_vector(windows[1], put_list, b_odd, picked[1][:])
+            put_on_scalar(windows[0], put_list, picked[0])
+
+        heads01 = pick_pair("h01", head_pairs[0], head_list, b0)
+        b3 = leave(column("b3", 24), acc3, nc.vector.tensor_copy)
+        put_on_vector(dr[1], rel_list, b1, heads01[1][:])
+        put_half(dr[0], rel_list, heads01[0], 0)
+        b2 = leave(column("b2", 26), acc2, nc.scalar.copy)
+        put_half(dr[0], rel_list, heads01[0], HALF)
+        put_pair(pick_pair("r23", rel_pairs[1], rel_list, b2), head_list, dh[2:4], b3)
+        put_pair(pick_pair("h23", head_pairs[1], head_list, b2), rel_list, dr[2:4], b3)
+
+        for out, windows, k in ((out_0, dh, 1), (out_0, dh, 0), (out_1, dr, 1), (out_1, dr, 0),
+                                (out_0, dh, 3), (out_0, dh, 2), (out_1, dr, 3), (out_1, dr, 2)):
+            nc.sync.dma_start(dealt(out)[:, k, :], windows[k][:])

@@ -190,6 +190,8 @@ def tile_attend_gdistm_hr_kernel(tc, hT, rT, G, tT, hoffs, roffs, offs, out_0, o
         put_pair(pick_pair("r23", rel_pairs[1], rel_list, b2), head_list, dh[2:4], b3)
         put_pair(pick_pair("h23", head_pairs[1], head_list, b2), rel_list, dr[2:4], b3)
 
-        for out, windows, k in ((out_0, dh, 1), (out_0, dh, 0), (out_1, dr, 1), (out_1, dr, 0),
-                                (out_0, dh, 3), (out_0, dh, 2), (out_1, dr, 3), (out_1, dr, 2)):
+        for out, windows, k in ((out_0, dh, 1), (out_0, dh, 0), (out_1, dr, 1), (out_1, dr, 0), (out_0, dh, 3)):
+            for first in range(2):
+                nc.sync.dma_start(dealt(out)[first::2, k, :], windows[k][first::2, :])
+        for out, windows, k in ((out_0, dh, 2), (out_1, dr, 3), (out_1, dr, 2)):
             nc.sync.dma_start(dealt(out)[:, k, :], windows[k][:])

@@ -58,10 +58,14 @@ def tile_attend_gdistm_hr_kernel(tc, hT, rT, G, tT, hoffs, roffs, offs, out_0, o
         ident = kept("ident", [P, P], F32)
         zeros = kept("zeros", [P, P], F32)
 
-        nc.sync.dma_start(grads[:], G.rearrange("(p e) i -> p e i", e=4))
-        nc.sync.dma_start(tails[1][:], dealt(tT)[:, 1, :])
+        def load_on_two_queues(tile, rows):
+            nc.sync.dma_start(tile[0::2], rows[0::2])
+            nc.scalar.dma_start(tile[1::2], rows[1::2])
+
+        load_on_two_queues(grads[:], dealt(G))
+        load_on_two_queues(tails[1][:], dealt(tT)[:, 1, :])
         nc.sync.dma_start(tail_list[:], offs)
-        nc.sync.dma_start(tails[0][:], dealt(tT)[:, 0, :])
+        load_on_two_queues(tails[0][:], dealt(tT)[:, 0, :])
         nc.sync.dma_start(rel_list[:], roffs)
         nc.sync.dma_start(rel_pairs[0][:], dealt(rT)[:, 0:2, :])
         nc.sync.dma_start(head_list[:], hoffs)
@@ -190,8 +194,9 @@ def tile_attend_gdistm_hr_kernel(tc, hT, rT, G, tT, hoffs, roffs, offs, out_0, o
         put_pair(pick_pair("r23", rel_pairs[1], rel_list, b2), head_list, dh[2:4], b3)
         put_pair(pick_pair("h23", head_pairs[1], head_list, b2), rel_list, dr[2:4], b3)
 
-        for out, windows, k in ((out_0, dh, 1), (out_0, dh, 0), (out_1, dr, 1), (out_1, dr, 0), (out_0, dh, 3)):
+        for out, windows, k in ((out_0, dh, 1), (out_0, dh, 0)):
             for first in range(2):
                 nc.sync.dma_start(dealt(out)[first::2, k, :], windows[k][first::2, :])
-        for out, windows, k in ((out_0, dh, 2), (out_1, dr, 3), (out_1, dr, 2)):
+        for out, windows, k in ((out_1, dr, 1), (out_1, dr, 0), (out_0, dh, 3), (out_0, dh, 2), (out_1, dr, 3),
+                                (out_1, dr, 2)):
             nc.sync.dma_start(dealt(out)[:, k, :], windows[k][:])

@@ -57,6 +57,7 @@ def tile_attend_gdistm_hr_kernel(tc, hT, rT, G, tT, hoffs, roffs, offs, out_0, o
         head_pairs = [kept("heads%d" % j, [P, 2, ENTITIES], F32) for j in range(BLOCKS // 2)]
         ident = kept("ident", [P, P], F32)
         zeros = kept("zeros", [P, P], F32)
+        one = kept("one", [P, 1], F32)
 
         def load_on_two_queues(tile, rows):
             nc.sync.dma_start(tile[0::2], rows[0::2])
@@ -77,6 +78,7 @@ def tile_attend_gdistm_hr_kernel(tc, hT, rT, G, tT, hoffs, roffs, offs, out_0, o
         nc.gpsimd.memset(zeros[:], 0.0)
         nc.gpsimd.affine_select(out=ident[:], in_=zeros[:], compare_op=mybir.AluOpType.not_equal, fill=1.0, base=0,
                                 pattern=[[-1, P]], channel_multiplier=1)
+        nc.gpsimd.memset(one[:], 1.0)
 
         dh = [kept("dh%d" % k, [P, ENTITIES], F32) for k in range(2)]
         for window in dh:
@@ -133,13 +135,8 @@ def tile_attend_gdistm_hr_kernel(tc, hT, rT, G, tT, hoffs, roffs, offs, out_0, o
         def put_on_vector(window, put_list, b_block, picked):
             nc.vector.tensor_tensor(window[:].indirect(put_list[:]), b_block[:], picked, MULT)
 
-        def put_half(window, put_list, values, first):
-            nc.scalar.activation(window[:].indirect(put_list[:, first // 16:(first + HALF) // 16]),
-                                 values[:, first:first + HALF], COPY)
-
         def put_on_scalar(window, put_list, values):
-            for first in (0, HALF):
-                put_half(window, put_list, values, first)
+            nc.scalar.activation(window[:].indirect(put_list[:]), values[:], COPY, scale=one[:])
 
         def column(name, kib=None):
             return kept(name, [P, QUERIES], F32) if kib is None else placed(name, [P, QUERIES], F32, kib * KIB)
@@ -177,26 +174,34 @@ def tile_attend_gdistm_hr_kernel(tc, hT, rT, G, tT, hoffs, roffs, offs, out_0, o
         for window in dh[2:] + dr[2:]:
             nc.gpsimd.memset(window[:].bitcast(I32), 0)
 
-        def pick_pair(name, pair, pick_list, b_even):
-            values = pick_times(column(name + "_values"), whole(pair), pick_list, b_even)
-            return values, pick_on_scalar(column(name + "_odd"), pair[:, 1, :], pick_list)
+        def pick_times_b2(name, pair, pick_list):
+            values = column(name)
+            for j in range(2):
+                nc.vector.tensor_tensor(values[:, j * HALF:(j + 1) * HALF],
+                                        whole(pair).indirect(pick_list[:, j * HALF // 16:(j + 1) * HALF // 16]),
+                                        b2[j][:], MULT)
+            return values
 
-        def put_pair(picked, put_list, windows, b_odd):
-            put_on_vector(windows[1], put_list, b_odd, picked[1][:])
-            put_on_scalar(windows[0], put_list, picked[0])
-
-        heads01 = pick_pair("h01", head_pairs[0], head_list, b0)
+        dr0_values = pick_times(column("dr0_values"), whole(head_pairs[0]), head_list, b0)
+        heads1 = pick_on_scalar(column("h1_picked"), head_pairs[0][:, 1, :], head_list)
+        b2 = [placed("b2_%d" % j, [P, HALF], F32, (25 + j) * KIB) for j in range(2)]
+        for j in range(2):
+            nc.scalar.copy(b2[j][:], acc2[:, j * HALF:(j + 1) * HALF])
+        put_on_vector(dr[1], rel_list, b1, heads1[:])
+        put_on_scalar(dr[0], rel_list, dr0_values)
+        dh2_values = pick_times_b2("dh2_values", rel_pairs[1], rel_list)
+        rels3 = pick_on_scalar(column("r3_picked"), rel_pairs[1][:, 1, :], rel_list)
+        put_on_scalar(dh[2], head_list, dh2_values)
+        dr2_values = pick_times_b2("dr2_values", head_pairs[1], head_list)
         b3 = leave(column("b3", 24), acc3, nc.vector.tensor_copy)
-        put_on_vector(dr[1], rel_list, b1, heads01[1][:])
-        put_half(dr[0], rel_list, heads01[0], 0)
-        b2 = leave(column("b2", 26), acc2, nc.scalar.copy)
-        put_half(dr[0], rel_list, heads01[0], HALF)
-        put_pair(pick_pair("r23", rel_pairs[1], rel_list, b2), head_list, dh[2:4], b3)
-        put_pair(pick_pair("h23", head_pairs[1], head_list, b2), rel_list, dr[2:4], b3)
+        heads3 = pick_on_scalar(column("h3_picked"), head_pairs[1][:, 1, :], head_list)
+        put_on_vector(dh[3], head_list, b3, rels3[:])
+        put_on_scalar(dr[2], rel_list, dr2_values)
+        put_on_vector(dr[3], rel_list, b3, heads3[:])
 
         for out, windows, k in ((out_0, dh, 1), (out_0, dh, 0)):
             for first in range(2):
                 nc.sync.dma_start(dealt(out)[first::2, k, :], windows[k][first::2, :])
-        for out, windows, k in ((out_1, dr, 1), (out_1, dr, 0), (out_0, dh, 3), (out_0, dh, 2), (out_1, dr, 3),
-                                (out_1, dr, 2)):
+        for out, windows, k in ((out_1, dr, 1), (out_1, dr, 0), (out_0, dh, 2), (out_0, dh, 3), (out_1, dr, 2),
+                                (out_1, dr, 3)):
             nc.sync.dma_start(dealt(out)[:, k, :], windows[k][:])

from contextlib import ExitStack

import concourse.mybir as mybir

F32 = mybir.dt.float32
BF16 = mybir.dt.bfloat16
I32 = mybir.dt.int32
U32 = mybir.dt.uint32
U16 = mybir.dt.uint16
U8 = mybir.dt.uint8
E4M3X4 = mybir.dt.float8_e4m3fn_x4
E5M2X4 = mybir.dt.float8_e5m2_x4
COPY = mybir.ActivationFunctionType.Copy
MULT = mybir.AluOpType.mult

P = 128
FEATURES = 512
QUERIES = 512
SLOTS = 512
ENTITIES = 2048
RELATIONS = 1024
BLOCKS = FEATURES // P
HALF = QUERIES // 2
KIB = 1024

FLOPS = 2 * FEATURES * QUERIES * SLOTS


def tile_attend_gdistm_hr_kernel(tc, hT, rT, G, tT, hoffs, roffs, offs, out_0, out_1):
    nc = tc.nc
    with ExitStack() as ctx:
        lists = ctx.enter_context(tc.tile_pool(name="lists", bufs=1))
        held = ctx.enter_context(tc.tile_pool(name="held", bufs=1))
        shared = ctx.enter_context(tc.tile_pool(name="shared", bufs=1))
        banks = ctx.enter_context(tc.psum_pool(name="banks", bufs=1))

        def kept(name, shape, dtype):
            return held.tile(shape, dtype, name=name, align_bytes=256)

        def placed(name, shape, dtype, offset):
            return shared.tile(shape, dtype, name=name, align_bytes=256, offset=offset)

        def dealt(table):
            return table.rearrange("(p k) c -> p k c", k=BLOCKS)

        def whole(tile):
            return tile[:].rearrange("p k c -> p (k c)")

        tail_list = lists.tile([P, SLOTS // 16], U16, name="tail_list", align_bytes=256)
        head_list = lists.tile([P, QUERIES // 16], U16, name="head_list", align_bytes=256)
        rel_list = lists.tile([P, QUERIES // 16], U16, name="rel_list", align_bytes=256)

        grads = kept("grads", [P, 4, SLOTS], F32)
        tails = [kept("tails%d" % k, [P, ENTITIES], F32) for k in range(2)]
        late_tails = kept("tails23", [P, 2, ENTITIES], F32)
        rel_pairs = [kept("rels%d" % j, [P, 2, RELATIONS], F32) for j in range(BLOCKS // 2)]
        head_pairs = [kept("heads%d" % j, [P, 2, ENTITIES], F32) for j in range(BLOCKS // 2)]
        ident = kept("ident", [P, P], F32)
        zeros = kept("zeros", [P, P], F32)
        one = kept("one", [P, 1], F32)

        def load_on_two_queues(tile, rows):
            nc.sync.dma_start(tile[0::2], rows[0::2])
            nc.scalar.dma_start(tile[1::2], rows[1::2])

        load_on_two_queues(grads[:], dealt(G))
        load_on_two_queues(tails[1][:], dealt(tT)[:, 1, :])
        nc.sync.dma_start(tail_list[:], offs)
        load_on_two_queues(tails[0][:], dealt(tT)[:, 0, :])
        nc.sync.dma_start(rel_list[:], roffs)
        nc.sync.dma_start(rel_pairs[0][:], dealt(rT)[:, 0:2, :])
        nc.sync.dma_start(head_list[:], hoffs)
        nc.sync.dma_start(late_tails[:], dealt(tT)[:, 2:4, :])
        nc.sync.dma_start(head_pairs[0][:], dealt(hT)[:, 0:2, :])
        nc.sync.dma_start(rel_pairs[1][:], dealt(rT)[:, 2:4, :])
        nc.sync.dma_start(head_pairs[1][:], dealt(hT)[:, 2:4, :])

        nc.gpsimd.memset(zeros[:], 0.0)
        nc.gpsimd.affine_select(out=ident[:], in_=zeros[:], compare_op=mybir.AluOpType.not_equal, fill=1.0, base=0,
                                pattern=[[-1, P]], channel_multiplier=1)
        nc.gpsimd.memset(one[:], 1.0)

        dh = [kept("dh%d" % k, [P, ENTITIES], F32) for k in range(2)]
        for window in dh:
            nc.vector.memset(window[:].bitcast(I32), 0)

        def transpose_words(src, bank):
            words = src.bitcast(F32)
            for u in range(2):
                nc.tensor.transpose(bank[:, u, :], words[:, u::2], ident[:])

        g_rounded = [placed("g_rounded%d" % j, [P, 2, SLOTS], BF16, (16 + 2 * j) * KIB) for j in range(2)]
        g_turned = kept("g_turned", [P, 4 * QUERIES], BF16)
        g_codes = kept("g_codes", [P, QUERIES], U32)
        g_scales = kept("g_scales", [P, QUERIES], U8)
        g_words = g_turned[:].bitcast(F32).rearrange("p (x j e u) -> p j x e u", j=2, e=2, u=2)
        for j in range(2):
            nc.vector.tensor_copy(g_rounded[j][:], grads[:, 2 * j:2 * j + 2, :])
        for j, copy in enumerate((nc.scalar.copy, nc.vector.tensor_copy)):
            bank = banks.tile([P, 2, 2, P], F32, name="g_bank", tag="g%d" % j)
            for e in range(2):
                transpose_words(g_rounded[j][:, e, :], bank[:, e])
            copy(g_words[:, j], bank[:].rearrange("p e u x -> p x e u"))
        nc.vector.quantize_mx(out=g_codes[:].bitcast(E5M2X4), scales=g_scales[:], in_=g_turned[:])

        def turn(k, picked):
            bank = banks.tile([P, 2, P], F32, name="t_bank", tag="turn%d" % (k % 2))
            transpose_words(picked[:], bank[:])
            return bank

        def leave_turned(k, offset, bank, copy):
            turned = placed("t_turned%d" % k, [P, 4 * P], BF16, offset)
            copy(turned[:].bitcast(F32).rearrange("p (x u) -> p x u", u=2), bank[:].rearrange("p u x -> p x u"))
            return turned[:]

        def product(k, turned, codes, scales):
            nc.vector.quantize_mx(out=codes[:].bitcast(E4M3X4), scales=scales[:], in_=turned)
            acc = banks.tile([P, QUERIES], F32, name="acc", tag="acc%d" % k)
            nc.tensor.matmul_mx(out=acc[:], lhsT=codes[:].bitcast(E4M3X4), lhsT_scale=scales[:],
                                rhs=g_codes[:].bitcast(E5M2X4), rhs_scale=g_scales[:], start=True, stop=True)
            return acc

        def leave(b, acc, copy):
            copy(b[:], acc[:])
            return b

        def pick_times(values, window, pick_list, b_even):
            nc.vector.tensor_tensor(values[:], window.indirect(pick_list[:]), b_even[:], MULT)
            return values

        def pick_on_scalar(picked, window, pick_list):
            nc.scalar.activation(picked[:], window.indirect(pick_list[:]), COPY)
            return picked

        def put_on_vector(window, put_list, b_block, picked):
            nc.vector.tensor_tensor(window[:].indirect(put_list[:]), b_block[:], picked, MULT)

        def put_on_scalar(window, put_list, values):
            nc.scalar.activation(window[:].indirect(put_list[:]), values[:], COPY, scale=one[:])

        def column(name, kib=None):
            return kept(name, [P, QUERIES], F32) if kib is None else placed(name, [P, QUERIES], F32, kib * KIB)

        picked1 = pick_on_scalar(placed("t_picked1", [P, SLOTS], BF16, 16 * KIB), tails[1][:], tail_list)
        picked0 = pick_on_scalar(placed("t_picked0", [P, SLOTS], BF16, 18 * KIB), tails[0][:], tail_list)
        turned1 = leave_turned(1, 22 * KIB, turn(1, picked1), nc.vector.tensor_copy)
        acc1 = product(1, turned1, kept("t_codes1", [P, P], U32), kept("t_scales1", [P, P], U8))
        turned0 = leave_turned(0, 4 * KIB - 512, turn(0, picked0), nc.vector.tensor_copy)
        b1 = leave(column("b1", 18), acc1, nc.vector.tensor_copy)
        acc0 = product(0, turned0, kept("t_codes0", [P, P], U32), kept("t_scales0", [P, P], U8))
        rels1 = pick_on_scalar(column("r1_picked"), rel_pairs[0][:, 1, :], rel_list)
        rels0 = pick_on_scalar(column("r0_picked"), rel_pairs[0][:, 0, :], rel_list)
        b0 = leave(column("b0", 25), acc0, nc.scalar.copy)
        put_on_vector(dh[1], head_list, b1, rels1[:])
        put_on_vector(dh[0], head_list, b0, rels0[:])
        dr = [placed("dr%d" % k, [P, RELATIONS], F32, 4 * k * KIB) for k in range(2)]
        for window in dr:
            nc.gpsimd.memset(window[:].bitcast(I32), 0)

        picked3 = pick_on_scalar(column("t_picked3"), late_tails[:, 1, :], tail_list)
        picked2 = pick_on_scalar(kept("t_picked2", [P, SLOTS], BF16), whole(late_tails), tail_list)
        bank3 = banks.tile([P, 4, P], F32, name="t_bank", tag="g0")
        for t in range(4):
            nc.tensor.transpose(bank3[:, t, :], picked3[:, t::4], ident[:])
        bank2 = turn(2, picked2)
        turned3 = kept("t_turned3", [P, P, 4], BF16)
        nc.scalar.copy(turned3[:], bank3[:].rearrange("p t x -> p x t"))
        turned2 = leave_turned(2, 40 * KIB - 512, bank2, nc.scalar.copy)
        acc3 = product(3, turned3[:].rearrange("p x t -> p (x t)"), kept("t_codes3", [P, P], U32),
                       kept("t_scales3", [P, P], U8))
        acc2 = product(2, turned2, placed("t_codes2", [P, P], U32, 12 * KIB - 256), kept("t_scales2", [P, P], U8))
        dh.extend([placed("dh%d" % k, [P, ENTITIES], F32, (16 + 8 * k) * KIB) for k in range(2, BLOCKS)])
        dr.extend([placed("dr%d" % k, [P, RELATIONS], F32, 4 * k * KIB) for k in range(2, BLOCKS)])
        for window in dh[2:] + dr[2:]:
            nc.gpsimd.memset(window[:].bitcast(I32), 0)

        def pick_times_b2(name, pair, pick_list):
            values = column(name)
            for j in range(2):
                nc.vector.tensor_tensor(values[:, j * HALF:(j + 1) * HALF],
                                        whole(pair).indirect(pick_list[:, j * HALF // 16:(j + 1) * HALF // 16]),
                                        b2[j][:], MULT)
            return values

        dr0_values = pick_times(column("dr0_values"), whole(head_pairs[0]), head_list, b0)
        heads1 = pick_on_scalar(column("h1_picked"), head_pairs[0][:, 1, :], head_list)
        b2 = [placed("b2_%d" % j, [P, HALF], F32, (25 + j) * KIB) for j in range(2)]
        for j in range(2):
            nc.scalar.copy(b2[j][:], acc2[:, j * HALF:(j + 1) * HALF])
        put_on_vector(dr[1], rel_list, b1, heads1[:])
        put_on_scalar(dr[0], rel_list, dr0_values)
        dh2_values = pick_times_b2("dh2_values", rel_pairs[1], rel_list)
        rels3 = pick_on_scalar(column("r3_picked"), rel_pairs[1][:, 1, :], rel_list)
        put_on_scalar(dh[2], head_list, dh2_values)
        dr2_values = pick_times_b2("dr2_values", head_pairs[1], head_list)
        b3 = leave(column("b3", 24), acc3, nc.vector.tensor_copy)
        heads3 = pick_on_scalar(column("h3_picked"), head_pairs[1][:, 1, :], head_list)
        put_on_vector(dh[3], head_list, b3, rels3[:])
        put_on_scalar(dr[2], rel_list, dr2_values)
        put_on_vector(dr[3], rel_list, b3, heads3[:])

        for out, windows, k in ((out_0, dh, 1), (out_0, dh, 0)):
            for first in range(2):
                nc.sync.dma_start(dealt(out)[first::2, k, :], windows[k][first::2, :])
        for out, windows, k in ((out_1, dr, 1), (out_1, dr, 0), (out_0, dh, 2), (out_0, dh, 3), (out_1, dr, 2),
                                (out_1, dr, 3)):
            nc.sync.dma_start(dealt(out)[:, k, :], windows[k][:])
